import numpy as np
import ml_dtypes


def mxq(x, axis, fmt="e4m3"):
    dtype, down = {"e4m3": (ml_dtypes.float8_e4m3fn, 7), "e5m2": (ml_dtypes.float8_e5m2, 14)}[fmt]
    v = np.moveaxis(np.asarray(x, np.float32).astype(ml_dtypes.bfloat16).astype(np.float64), axis, -1)
    blocks = v.reshape(v.shape[:-1] + (-1, 32))
    amax = np.abs(blocks).max(-1, keepdims=True)
    byte = np.maximum(np.where(amax > 0, np.frexp(amax)[1] - 1 + 127, 0) - down, 1)
    scale = np.exp2(byte - 127.0)
    codes = (blocks / scale).astype(np.float32).astype(dtype).astype(np.float64)
    return np.moveaxis((codes * scale).reshape(v.shape), -1, axis)


WIDE = False


def mx_kscale(k):
    if not WIDE:
        return np.ones(k)
    levels = np.array([10, -10, 5, -5, 0])
    if k % 512:
        return np.exp2(np.random.permutation(np.resize(levels, k // 32))).repeat(32)
    a = np.empty((k // 512, 16))
    for p in range(k // 512):
        a[p, :8] = np.random.permutation(np.resize(levels, 8))
        for g in range(8):
            far = levels[np.abs(levels - a[p, g]) >= 10]
            a[p, g + 8] = far[np.random.randint(len(far))]
    return np.exp2(a.ravel()).repeat(32)


def f64(x):
    return np.asarray(x).astype(np.float64)


def striped(idx):
    return np.tile(idx.reshape(-1, 16).T, (8, 1)).astype(np.uint16)


def unstriped(offs):
    return offs[:16].T.reshape(-1).astype(np.int64)


K, T, E, C, N = 1536, 1024, 12, 256, 128
TOP = 3


def by_expert(wq, xq):
    return np.concatenate([wq[e].T @ xq[:, e * C:(e + 1) * C] for e in range(E)], axis=1)


def setup_inputs():
    n = np.random.standard_normal
    s = mx_kscale(K)[:, None]
    deal = np.repeat(np.arange(E), C).reshape(TOP, T)[:, np.random.permutation(T)]
    deal = np.take_along_axis(deal, np.argsort(np.random.rand(TOP, T), axis=0), axis=0)
    for _ in range(8):
        s_, t_ = np.random.permutation(T).reshape(2, -1); r = np.random.randint(TOP, size=T // 2); x, y = deal[r, s_].copy(), deal[r, t_].copy()
        ok = ~((deal[:, s_] == y).any(0) | (deal[:, t_] == x).any(0)); deal[r[ok], s_[ok]] = y[ok]; deal[r[ok], t_[ok]] = x[ok]
    order = np.lexsort((np.random.rand(TOP * T), deal.reshape(-1)))
    slot_token = order % T; pos = np.empty(TOP * T, np.int64); pos[order] = np.arange(TOP * T); pos = pos.reshape(TOP, T)
    g = np.random.uniform(0.5, 1.5, (TOP, T)); g = g / g.sum(0)
    w_slot = np.empty(E * C)
    for r in range(TOP): w_slot[pos[r]] = g[r]
    return {
        "xT": (n((K, T)) * s).astype(np.float32),
        "w": (n((E, K, N)) / np.sqrt(K) / s[None]).astype(np.float32),
        "gate": np.tile(w_slot, (K, 1)).astype(np.float32),
        "offs": striped(slot_token),
        "pos1": striped(pos[0]),
        "pos2": striped(pos[1]),
        "pos3": striped(pos[2]),
    }


def reference(xT, w, gate, offs, pos1, pos2, pos3):
    idx = unstriped(offs)
    xq = mxq(f64(gate) * f64(xT)[:, idx], 0, "e4m3")
    y = by_expert(mxq(f64(w), 1, "e4m3"), xq)
    return y[:, unstriped(pos1)] + y[:, unstriped(pos2)] + y[:, unstriped(pos3)]

@@ -1,0 +1,174 @@
+from contextlib import ExitStack
+
+import concourse.mybir as mybir
+
+K, T, E, C, N = 1536, 1024, 12, 256, 128
+S = E * C
+
+F32 = mybir.dt.float32
+BF16 = mybir.dt.bfloat16
+U32 = mybir.dt.uint32
+U16 = mybir.dt.uint16
+U8 = mybir.dt.uint8
+FP8X4 = mybir.dt.float8_e4m3fn_x4
+MULT = mybir.AluOpType.mult
+ADD = mybir.AluOpType.add
+
+P = 128
+PACK = 4
+K_PASS = P * PACK
+PASSES = K // K_PASS
+W_GROUP = 4
+
+FLOPS = 2 * K * S * N
+BYTES = 4 * (K * T + E * K * N + S + N * T) + 2 * (S + 3 * T)
+
+CUTS = [[768, 768, 768, 768], [768, 768, 768, 768], [768, 768, 768, 384, 256, 128]]
+GATE_CUT = 768
+TOKEN_CUTS = [640, 384]
+
+
+def powers_of_two(width):
+    parts = []
+    start = 0
+    for size in (1024, 512, 256, 128):
+        if width - start >= size:
+            parts.append((start, size))
+            start += size
+    return parts
+
+
+def tile_moe_pre_lin_none_kernel(tc, xT, w, gate, offs, pos1, pos2, pos3, out):
+    nc = tc.nc
+    with ExitStack() as ctx:
+        keep = ctx.enter_context(tc.tile_pool(name="keep", bufs=1))
+        rows = ctx.enter_context(tc.tile_pool(name="rows", bufs=2))
+        ring = ctx.enter_context(tc.tile_pool(name="ring", bufs=3))
+        psum = ctx.enter_context(tc.psum_pool(name="psum", bufs=8))
+
+        offsets = keep.tile([P, S // 16], U16, name="offsets")
+        nc.sync.dma_start(offsets[:], offs)
+        gates = keep.tile([P, S], F32, name="gates")
+        y = keep.tile([P, S], F32, name="y")
+        x_codes = [keep.tile([P, S], U32, name=f"x_codes{g}", align_bytes=64) for g in range(PASSES)]
+        x_scales = [keep.tile([P, S], U8, name=f"x_scales{g}", align_bytes=64) for g in range(PASSES)]
+        w_codes = [keep.tile([P, E * N], U32, name=f"w_codes{g}", align_bytes=64) for g in range(PASSES)]
+        w_scales = [keep.tile([P, E * N], U8, name=f"w_scales{g}", align_bytes=64) for g in range(PASSES)]
+
+        def load_rows(g, j):
+            window = rows.tile([P, T], F32, name=f"window{j}")
+            src = xT[g * K_PASS:(g + 1) * K_PASS, :].rearrange("(p j) t -> p j t", j=PACK)
+            nc.sync.dma_start(window[:], src[:, j, :])
+            return window
+
+        def load_gate(c):
+            cols = slice(c * GATE_CUT, (c + 1) * GATE_CUT)
+            nc.sync.dma_start(gates[:, cols], gate[0:P, cols])
+
+        def gather(windows, s0, n):
+            picked = ring.tile([P, PACK, n], F32, name="picked")
+            for j in range(PACK):
+                nc.vector.tensor_tensor(
+                    picked[:, j, :],
+                    windows[j][:].indirect(offsets[:, s0 // 16:(s0 + n) // 16]),
+                    gates[:, s0:s0 + n],
+                    MULT,
+                )
+            grouped = ring.tile([P, n, PACK], BF16, name="x_grouped", align_bytes=64)
+            nc.scalar.copy(
+                grouped[:].rearrange("p (c i) j -> p c j i", i=4),
+                picked[:].rearrange("p j (c i) -> p c j i", i=4),
+            )
+            return grouped
+
+        def quantize(grouped, codes, scales, start, n):
+            flat = grouped[:].rearrange("p n j -> p (n j)")
+            for a, size in powers_of_two(n):
+                cols = slice(start + a, start + a + size)
+                nc.vector.quantize_mx(
+                    out=codes[:, cols].bitcast(FP8X4),
+                    scales=scales[:, cols],
+                    in_=flat[:, a * PACK:(a + size) * PACK],
+                )
+
+        def stage_weights(g, e0):
+            raw = ring.tile([P, W_GROUP, PACK, N], F32, name="w_raw")
+            src = w[e0:e0 + W_GROUP, g * K_PASS:(g + 1) * K_PASS, :]
+            nc.sync.dma_start(
+                raw[:].rearrange("p e j n -> p e (j n)"),
+                src.rearrange("e (p j) n -> p e (j n)", j=PACK),
+            )
+            grouped = ring.tile([P, W_GROUP * N, PACK], BF16, name="w_grouped", align_bytes=64)
+            for e in range(W_GROUP):
+                nc.scalar.copy(
+                    grouped[:, e * N:(e + 1) * N, :].rearrange("p (c i) j -> p c j i", i=4),
+                    raw[:, e, :, :].rearrange("p j (c i) -> p c j i", i=4),
+                )
+            return grouped
+
+        def multiply(s0, n):
+            start = s0
+            while start < s0 + n:
+                e = start // C
+                stop = min((e + 1) * C, s0 + n)
+                acc = psum.tile([P, stop - start], F32, name="acc")
+                for g in range(PASSES):
+                    nc.tensor.matmul_mx(
+                        out=acc[:],
+                        lhsT=w_codes[g][:, e * N:(e + 1) * N].bitcast(FP8X4),
+                        lhsT_scale=w_scales[g][:, e * N:(e + 1) * N],
+                        rhs=x_codes[g][:, start:stop].bitcast(FP8X4),
+                        rhs_scale=x_scales[g][:, start:stop],
+                        start=(g == 0),
+                        stop=(g == PASSES - 1),
+                    )
+                nc.scalar.copy(y[:, start:stop], acc[:])
+                start = stop
+
+        def finish(pending):
+            for grouped, codes, scales, start, n, last in pending:
+                quantize(grouped, codes, scales, start, n)
+            for grouped, codes, scales, start, n, last in pending:
+                if last:
+                    multiply(start, n)
+
+        weight_jobs = [(g, e0) for g in range(PASSES) for e0 in range(0, E, W_GROUP)]
+        pending = []
+        step = 0
+        for g in range(PASSES):
+            windows = []
+            for j in range(PACK):
+                windows.append(load_rows(g, j))
+                if g == 0 and j == 0:
+                    load_gate(0)
+            s0 = 0
+            for c, n in enumerate(CUTS[g]):
+                if g == 0 and c > 0:
+                    load_gate(c)
+                grouped = gather(windows, s0, n)
+                finish(pending)
+                pending = []
+                if step < len(weight_jobs):
+                    wg, e0 = weight_jobs[step]
+                    w_grouped = stage_weights(wg, e0)
+                    pending.append((w_grouped, w_codes[wg], w_scales[wg], e0 * N, W_GROUP * N, False))
+                pending.append((grouped, x_codes[g], x_scales[g], s0, n, g == PASSES - 1))
+                s0 += n
+                step += 1
+        finish(pending)
+
+        lists = []
+        for r, pos in enumerate((pos1, pos2, pos3)):
+            tile = keep.tile([P, T // 16], U16, name=f"pos{r}")
+            nc.sync.dma_start(tile[:], pos)
+            lists.append(tile)
+        t0 = 0
+        for n in TOKEN_CUTS:
+            parts = ring.tile([P, 3, n], F32, name="picked")
+            total = ring.tile([P, n], F32, name="total")
+            for r in range(3):
+                nc.vector.tensor_copy(parts[:, r, :], y[:].indirect(lists[r][:, t0 // 16:(t0 + n) // 16]))
+            nc.vector.tensor_tensor(total[:], parts[:, 0, :], parts[:, 1, :], ADD)
+            nc.vector.tensor_tensor(total[:], total[:], parts[:, 2, :], ADD)
+            nc.sync.dma_start(out[:, t0:t0 + n], total[:])
+            t0 += n

@@ -18,23 +18,31 @@ P = 128
 PACK = 4
 K_PASS = P * PACK
 PASSES = K // K_PASS
-W_GROUP = 4
+W_JOB = 4
+W_BLOCKS = E * PASSES
 
 FLOPS = 2 * K * S * N
 BYTES = 4 * (K * T + E * K * N + S + N * T) + 2 * (S + 3 * T)
 
-CUTS = [[768, 768, 768, 768], [768, 768, 768, 768], [768, 768, 768, 384, 256, 128]]
-GATE_CUT = 768
+WIDE = 1536
+WINDOW = WIDE + 8
+CUTS = [[WIDE, WIDE], [WIDE, WIDE], [WIDE, 768, 384, 256, 128]]
+FIRST_CUTS = [(0, 256), (256, 768), (768, WIDE)]
+PIECE = 512
+JOBS_PER_STEP = 2
 TOKEN_CUTS = [640, 384]
 
 
-def powers_of_two(width):
+def pieces(width):
     parts = []
     start = 0
-    for size in (1024, 512, 256, 128):
+    size = PIECE
+    while start < width:
         if width - start >= size:
             parts.append((start, size))
             start += size
+        else:
+            size //= 2
     return parts
 
 
@@ -42,69 +50,69 @@ def tile_moe_pre_lin_none_kernel(tc, xT, w, gate, offs, pos1, pos2, pos3, out):
     nc = tc.nc
     with ExitStack() as ctx:
         keep = ctx.enter_context(tc.tile_pool(name="keep", bufs=1))
-        rows = ctx.enter_context(tc.tile_pool(name="rows", bufs=2))
-        ring = ctx.enter_context(tc.tile_pool(name="ring", bufs=3))
+        two = ctx.enter_context(tc.tile_pool(name="two", bufs=2))
+        three = ctx.enter_context(tc.tile_pool(name="three", bufs=3))
+        four = ctx.enter_context(tc.tile_pool(name="four", bufs=4))
         psum = ctx.enter_context(tc.psum_pool(name="psum", bufs=8))
 
         offsets = keep.tile([P, S // 16], U16, name="offsets")
         nc.sync.dma_start(offsets[:], offs)
         gates = keep.tile([P, S], F32, name="gates")
         y = keep.tile([P, S], F32, name="y")
+        picked = keep.tile([P, 2 * PACK * WIDE], F32, name="picked")
         x_codes = [keep.tile([P, S], U32, name=f"x_codes{g}", align_bytes=64) for g in range(PASSES)]
         x_scales = [keep.tile([P, S], U8, name=f"x_scales{g}", align_bytes=64) for g in range(PASSES)]
-        w_codes = [keep.tile([P, E * N], U32, name=f"w_codes{g}", align_bytes=64) for g in range(PASSES)]
-        w_scales = [keep.tile([P, E * N], U8, name=f"w_scales{g}", align_bytes=64) for g in range(PASSES)]
+        w_codes = keep.tile([P, W_BLOCKS * N], U32, name="w_codes", align_bytes=64)
+        w_scales = keep.tile([P, W_BLOCKS * N], U8, name="w_scales", align_bytes=64)
+        w_blocks = w.rearrange("e (g p j) n -> p (e g) (j n)", p=P, j=PACK)
 
         def load_rows(g, j):
-            window = rows.tile([P, T], F32, name=f"window{j}")
+            window = two.tile([P, WINDOW], F32, name=f"window{j}")
             src = xT[g * K_PASS:(g + 1) * K_PASS, :].rearrange("(p j) t -> p j t", j=PACK)
-            nc.sync.dma_start(window[:], src[:, j, :])
+            nc.sync.dma_start(window[:, 0:T], src[:, j, :])
             return window
 
-        def load_gate(c):
-            cols = slice(c * GATE_CUT, (c + 1) * GATE_CUT)
-            nc.sync.dma_start(gates[:, cols], gate[0:P, cols])
+        def load_gate(start, stop):
+            nc.sync.dma_start(gates[:, start:stop], gate[0:P, start:stop])
 
-        def gather(windows, s0, n):
-            picked = ring.tile([P, PACK, n], F32, name="picked")
+        def gather(windows, s0, n, base, split_first):
+            planes = picked[:, base:base + PACK * n].rearrange("p (j s) -> p j s", j=PACK)
             for j in range(PACK):
-                nc.vector.tensor_tensor(
-                    picked[:, j, :],
-                    windows[j][:].indirect(offsets[:, s0 // 16:(s0 + n) // 16]),
-                    gates[:, s0:s0 + n],
-                    MULT,
-                )
-            grouped = ring.tile([P, n, PACK], BF16, name="x_grouped", align_bytes=64)
-            nc.scalar.copy(
-                grouped[:].rearrange("p (c i) j -> p c j i", i=4),
-                picked[:].rearrange("p j (c i) -> p c j i", i=4),
-            )
-            return grouped
-
-        def quantize(grouped, codes, scales, start, n):
-            flat = grouped[:].rearrange("p n j -> p (n j)")
-            for a, size in powers_of_two(n):
-                cols = slice(start + a, start + a + size)
-                nc.vector.quantize_mx(
-                    out=codes[:, cols].bitcast(FP8X4),
-                    scales=scales[:, cols],
-                    in_=flat[:, a * PACK:(a + size) * PACK],
-                )
-
-        def stage_weights(g, e0):
-            raw = ring.tile([P, W_GROUP, PACK, N], F32, name="w_raw")
-            src = w[e0:e0 + W_GROUP, g * K_PASS:(g + 1) * K_PASS, :]
-            nc.sync.dma_start(
-                raw[:].rearrange("p e j n -> p e (j n)"),
-                src.rearrange("e (p j) n -> p e (j n)", j=PACK),
-            )
-            grouped = ring.tile([P, W_GROUP * N, PACK], BF16, name="w_grouped", align_bytes=64)
-            for e in range(W_GROUP):
+                cuts = FIRST_CUTS if split_first and j == 0 else [(0, n)]
+                for a, b in cuts:
+                    nc.vector.tensor_tensor(
+                        planes[:, j, a:b],
+                        windows[j][:].indirect(offsets[:, (s0 + a) // 16:(s0 + b) // 16]),
+                        gates[:, s0 + a:s0 + b],
+                        MULT,
+                    )
+            staged = []
+            for a, size in pieces(n):
+                grouped = four.tile([P, size, PACK], BF16, name="x_grouped", align_bytes=64)
                 nc.scalar.copy(
-                    grouped[:, e * N:(e + 1) * N, :].rearrange("p (c i) j -> p c j i", i=4),
-                    raw[:, e, :, :].rearrange("p j (c i) -> p c j i", i=4),
+                    grouped[:].rearrange("p (c i) j -> p c j i", i=4),
+                    planes[:, :, a:a + size].rearrange("p j (c i) -> p c j i", i=4),
                 )
-            return grouped
+                staged.append((grouped, s0 + a, size))
+            return staged
+
+        def quantize(grouped, codes, scales, start, size):
+            nc.vector.quantize_mx(
+                out=codes[:, start:start + size].bitcast(FP8X4),
+                scales=scales[:, start:start + size],
+                in_=grouped[:].rearrange("p n j -> p (n j)"),
+            )
+
+        def stage_weights(b0):
+            raw = two.tile([P, W_JOB, PACK * N], F32, name="w_raw")
+            nc.sync.dma_start(raw[:], w_blocks[:, b0:b0 + W_JOB, :])
+            grouped = three.tile([P, W_JOB * N, PACK], BF16, name="w_grouped", align_bytes=64)
+            for b in range(W_JOB):
+                nc.scalar.copy(
+                    grouped[:, b * N:(b + 1) * N, :].rearrange("p (c i) j -> p c j i", i=4),
+                    raw[:, b, :].rearrange("p (j c i) -> p c j i", j=PACK, i=4),
+                )
+            return grouped, b0 * N, W_JOB * N
 
         def multiply(s0, n):
             start = s0
@@ -113,10 +121,11 @@ def tile_moe_pre_lin_none_kernel(tc, xT, w, gate, offs, pos1, pos2, pos3, out):
                 stop = min((e + 1) * C, s0 + n)
                 acc = psum.tile([P, stop - start], F32, name="acc")
                 for g in range(PASSES):
+                    cols = slice((e * PASSES + g) * N, (e * PASSES + g + 1) * N)
                     nc.tensor.matmul_mx(
                         out=acc[:],
-                        lhsT=w_codes[g][:, e * N:(e + 1) * N].bitcast(FP8X4),
-                        lhsT_scale=w_scales[g][:, e * N:(e + 1) * N],
+                        lhsT=w_codes[:, cols].bitcast(FP8X4),
+                        lhsT_scale=w_scales[:, cols],
                         rhs=x_codes[g][:, start:stop].bitcast(FP8X4),
                         rhs_scale=x_scales[g][:, start:stop],
                         start=(g == 0),
@@ -125,37 +134,36 @@ def tile_moe_pre_lin_none_kernel(tc, xT, w, gate, offs, pos1, pos2, pos3, out):
                 nc.scalar.copy(y[:, start:stop], acc[:])
                 start = stop
 
-        def finish(pending):
-            for grouped, codes, scales, start, n, last in pending:
-                quantize(grouped, codes, scales, start, n)
-            for grouped, codes, scales, start, n, last in pending:
-                if last:
-                    multiply(start, n)
+        def finish(g, staged_x, staged_w):
+            for grouped, start, size in staged_w:
+                quantize(grouped, w_codes, w_scales, start, size)
+            for grouped, start, size in staged_x:
+                quantize(grouped, x_codes[g], x_scales[g], start, size)
+                if g == PASSES - 1:
+                    multiply(start, size)
 
-        weight_jobs = [(g, e0) for g in range(PASSES) for e0 in range(0, E, W_GROUP)]
-        pending = []
-        step = 0
+        weight_jobs = list(range(0, W_BLOCKS, W_JOB))
+        pending = (0, [], [])
+        base = 0
         for g in range(PASSES):
             windows = []
             for j in range(PACK):
                 windows.append(load_rows(g, j))
                 if g == 0 and j == 0:
-                    load_gate(0)
+                    for a, b in FIRST_CUTS:
+                        load_gate(a, b)
+            if g == 0:
+                load_gate(WIDE, S)
             s0 = 0
-            for c, n in enumerate(CUTS[g]):
-                if g == 0 and c > 0:
-                    load_gate(c)
-                grouped = gather(windows, s0, n)
-                finish(pending)
-                pending = []
-                if step < len(weight_jobs):
-                    wg, e0 = weight_jobs[step]
-                    w_grouped = stage_weights(wg, e0)
-                    pending.append((w_grouped, w_codes[wg], w_scales[wg], e0 * N, W_GROUP * N, False))
-                pending.append((grouped, x_codes[g], x_scales[g], s0, n, g == PASSES - 1))
+            for n in CUTS[g]:
+                staged_x = gather(windows, s0, n, base, g == 0 and s0 == 0)
+                base = PACK * WIDE - base
+                finish(*pending)
+                staged_w = [stage_weights(b0) for b0 in weight_jobs[:JOBS_PER_STEP]]
+                weight_jobs = weight_jobs[JOBS_PER_STEP:]
+                pending = (g, staged_x, staged_w)
                 s0 += n
-                step += 1
-        finish(pending)
+        finish(*pending)
 
         lists = []
         for r, pos in enumerate((pos1, pos2, pos3)):
@@ -164,11 +172,11 @@ def tile_moe_pre_lin_none_kernel(tc, xT, w, gate, offs, pos1, pos2, pos3, out):
             lists.append(tile)
         t0 = 0
         for n in TOKEN_CUTS:
-            parts = ring.tile([P, 3, n], F32, name="picked")
-            total = ring.tile([P, n], F32, name="total")
+            parts = picked[:, PACK * t0:PACK * (t0 + n)].rearrange("p (r t) -> p r t", r=PACK)
             for r in range(3):
                 nc.vector.tensor_copy(parts[:, r, :], y[:].indirect(lists[r][:, t0 // 16:(t0 + n) // 16]))
-            nc.vector.tensor_tensor(total[:], parts[:, 0, :], parts[:, 1, :], ADD)
-            nc.vector.tensor_tensor(total[:], total[:], parts[:, 2, :], ADD)
-            nc.sync.dma_start(out[:, t0:t0 + n], total[:])
+            last_adder = nc.vector if t0 + n == T else nc.gpsimd
+            nc.gpsimd.tensor_tensor(parts[:, 3, :], parts[:, 0, :], parts[:, 1, :], ADD)
+            last_adder.tensor_tensor(parts[:, 3, :], parts[:, 3, :], parts[:, 2, :], ADD)
+            nc.sync.dma_start(out[:, t0:t0 + n], parts[:, 3, :])
             t0 += n

@@ -26,7 +26,7 @@ BYTES = 4 * (K * T + E * K * N + S + N * T) + 2 * (S + 3 * T)
 
 WIDE = 1536
 WINDOW = WIDE + 8
-CUTS = [[WIDE, WIDE], [WIDE, WIDE], [WIDE, 768, 384, 256, 128]]
+CUTS = [[WIDE, WIDE], [WIDE, WIDE], [1024, 768, 512, 384, 256, 128]]
 FIRST_CUTS = [(0, 256), (256, 768), (768, WIDE)]
 PIECE = 512
 JOBS_PER_STEP = 2
@@ -170,13 +170,16 @@ def tile_moe_pre_lin_none_kernel(tc, xT, w, gate, offs, pos1, pos2, pos3, out):
             tile = keep.tile([P, T // 16], U16, name=f"pos{r}")
             nc.sync.dma_start(tile[:], pos)
             lists.append(tile)
-        t0 = 0
-        for n in TOKEN_CUTS:
-            parts = picked[:, PACK * t0:PACK * (t0 + n)].rearrange("p (r t) -> p r t", r=PACK)
+        early, late = TOKEN_CUTS
+        first = picked[:, 0:PACK * early].rearrange("p (r t) -> p r t", r=PACK)
+        second = picked[:, PACK * early:PACK * early + 3 * late].rearrange("p (r t) -> p r t", r=3)
+        for parts, t0, n in ((first, 0, early), (second, early, late)):
             for r in range(3):
                 nc.vector.tensor_copy(parts[:, r, :], y[:].indirect(lists[r][:, t0 // 16:(t0 + n) // 16]))
-            last_adder = nc.vector if t0 + n == T else nc.gpsimd
-            nc.gpsimd.tensor_tensor(parts[:, 3, :], parts[:, 0, :], parts[:, 1, :], ADD)
-            last_adder.tensor_tensor(parts[:, 3, :], parts[:, 3, :], parts[:, 2, :], ADD)
-            nc.sync.dma_start(out[:, t0:t0 + n], parts[:, 3, :])
-            t0 += n
+        nc.gpsimd.tensor_tensor(first[:, 3, :], first[:, 0, :], first[:, 1, :], ADD)
+        nc.gpsimd.tensor_tensor(first[:, 3, :], first[:, 3, :], first[:, 2, :], ADD)
+        nc.sync.dma_start(out[:, 0:early], first[:, 3, :])
+        total = first[:, 2, 0:late]
+        nc.gpsimd.tensor_tensor(total, second[:, 0, :], second[:, 1, :], ADD)
+        nc.vector.tensor_tensor(total, total, second[:, 2, :], ADD)
+        nc.sync.dma_start(out[:, early:T], total)

@@ -18,7 +18,7 @@ P = 128
 PACK = 4
 K_PASS = P * PACK
 PASSES = K // K_PASS
-W_JOB = 4
+W_LOAD = 2
 W_BLOCKS = E * PASSES
 
 FLOPS = 2 * K * S * N
@@ -28,8 +28,10 @@ WIDE = 1536
 WINDOW = WIDE + 8
 CUTS = [[WIDE, WIDE], [WIDE, WIDE], [1024, 768, 512, 384, 256, 128]]
 FIRST_CUTS = [(0, 256), (256, 768), (768, WIDE)]
-PIECE = 512
-JOBS_PER_STEP = 2
+PIECE = 1024
+WEIGHT_JOBS = [[8], [8, 4], [8, 4], [4]]
+VECTOR_EMPTIES = 256
+HELD = 256
 TOKEN_CUTS = [640, 384]
 
 
@@ -52,7 +54,8 @@ def tile_moe_pre_lin_none_kernel(tc, xT, w, gate, offs, pos1, pos2, pos3, out):
         keep = ctx.enter_context(tc.tile_pool(name="keep", bufs=1))
         two = ctx.enter_context(tc.tile_pool(name="two", bufs=2))
         three = ctx.enter_context(tc.tile_pool(name="three", bufs=3))
-        four = ctx.enter_context(tc.tile_pool(name="four", bufs=4))
+        five = ctx.enter_context(tc.tile_pool(name="five", bufs=5))
+        six = ctx.enter_context(tc.tile_pool(name="six", bufs=6))
         psum = ctx.enter_context(tc.psum_pool(name="psum", bufs=8))
 
         offsets = keep.tile([P, S // 16], U16, name="offsets")
@@ -67,7 +70,7 @@ def tile_moe_pre_lin_none_kernel(tc, xT, w, gate, offs, pos1, pos2, pos3, out):
         w_blocks = w.rearrange("e (g p j) n -> p (e g) (j n)", p=P, j=PACK)
 
         def load_rows(g, j):
-            window = two.tile([P, WINDOW], F32, name=f"window{j}")
+            window = six.tile([P, WINDOW], F32, name="window")
             src = xT[g * K_PASS:(g + 1) * K_PASS, :].rearrange("(p j) t -> p j t", j=PACK)
             nc.sync.dma_start(window[:, 0:T], src[:, j, :])
             return window
@@ -87,8 +90,9 @@ def tile_moe_pre_lin_none_kernel(tc, xT, w, gate, offs, pos1, pos2, pos3, out):
                         MULT,
                     )
             staged = []
-            for a, size in pieces(n):
-                grouped = four.tile([P, size, PACK], BF16, name="x_grouped", align_bytes=64)
+            for a in range(0, n, PIECE):
+                size = min(PIECE, n - a)
+                grouped = three.tile([P, size, PACK], BF16, name="x_grouped", align_bytes=64)
                 nc.scalar.copy(
                     grouped[:].rearrange("p (c i) j -> p c j i", i=4),
                     planes[:, :, a:a + size].rearrange("p j (c i) -> p c j i", i=4),
@@ -97,22 +101,26 @@ def tile_moe_pre_lin_none_kernel(tc, xT, w, gate, offs, pos1, pos2, pos3, out):
             return staged
 
         def quantize(grouped, codes, scales, start, size):
-            nc.vector.quantize_mx(
-                out=codes[:, start:start + size].bitcast(FP8X4),
-                scales=scales[:, start:start + size],
-                in_=grouped[:].rearrange("p n j -> p (n j)"),
-            )
-
-        def stage_weights(b0):
-            raw = two.tile([P, W_JOB, PACK * N], F32, name="w_raw")
-            nc.sync.dma_start(raw[:], w_blocks[:, b0:b0 + W_JOB, :])
-            grouped = three.tile([P, W_JOB * N, PACK], BF16, name="w_grouped", align_bytes=64)
-            for b in range(W_JOB):
-                nc.scalar.copy(
-                    grouped[:, b * N:(b + 1) * N, :].rearrange("p (c i) j -> p c j i", i=4),
-                    raw[:, b, :].rearrange("p (j c i) -> p c j i", j=PACK, i=4),
+            flat = grouped[:].rearrange("p n j -> p (n j)")
+            for a, width in pieces(size):
+                nc.vector.quantize_mx(
+                    out=codes[:, start + a:start + a + width].bitcast(FP8X4),
+                    scales=scales[:, start + a:start + a + width],
+                    in_=flat[:, PACK * a:PACK * (a + width)],
                 )
-            return grouped, b0 * N, W_JOB * N
+
+        def stage_weights(b0, count):
+            grouped = two.tile([P, count * N, PACK], BF16, name="w_grouped", align_bytes=64)
+            for first in range(0, count, W_LOAD):
+                raw = five.tile([P, W_LOAD, PACK * N], F32, name="w_raw")
+                nc.sync.dma_start(raw[:], w_blocks[:, b0 + first:b0 + first + W_LOAD, :])
+                for b in range(W_LOAD):
+                    cols = slice((first + b) * N, (first + b + 1) * N)
+                    nc.scalar.copy(
+                        grouped[:, cols, :].rearrange("p (c i) j -> p c j i", i=4),
+                        raw[:, b, :].rearrange("p (j c i) -> p c j i", j=PACK, i=4),
+                    )
+            return grouped, b0 * N, count * N
 
         def multiply(s0, n):
             start = s0
@@ -131,7 +139,10 @@ def tile_moe_pre_lin_none_kernel(tc, xT, w, gate, offs, pos1, pos2, pos3, out):
                         start=(g == 0),
                         stop=(g == PASSES - 1),
                     )
-                nc.scalar.copy(y[:, start:stop], acc[:])
+                if start >= S - VECTOR_EMPTIES:
+                    nc.vector.tensor_copy(y[:, start:stop], acc[:])
+                else:
+                    nc.scalar.copy(y[:, start:stop], acc[:])
                 start = stop
 
         def finish(g, staged_x, staged_w):
@@ -139,10 +150,12 @@ def tile_moe_pre_lin_none_kernel(tc, xT, w, gate, offs, pos1, pos2, pos3, out):
                 quantize(grouped, w_codes, w_scales, start, size)
             for grouped, start, size in staged_x:
                 quantize(grouped, x_codes[g], x_scales[g], start, size)
-                if g == PASSES - 1:
+            if g == PASSES - 1:
+                for grouped, start, size in staged_x:
                     multiply(start, size)
 
-        weight_jobs = list(range(0, W_BLOCKS, W_JOB))
+        step = 0
+        next_block = 0
         pending = (0, [], [])
         base = 0
         for g in range(PASSES):
@@ -158,9 +171,15 @@ def tile_moe_pre_lin_none_kernel(tc, xT, w, gate, offs, pos1, pos2, pos3, out):
             for n in CUTS[g]:
                 staged_x = gather(windows, s0, n, base, g == 0 and s0 == 0)
                 base = PACK * WIDE - base
-                finish(*pending)
-                staged_w = [stage_weights(b0) for b0 in weight_jobs[:JOBS_PER_STEP]]
-                weight_jobs = weight_jobs[JOBS_PER_STEP:]
+                if g == PASSES - 1 and s0 + n > S - HELD:
+                    staged_x = pending[1] + staged_x
+                else:
+                    finish(*pending)
+                staged_w = []
+                for count in WEIGHT_JOBS[step] if step < len(WEIGHT_JOBS) else []:
+                    staged_w.append(stage_weights(next_block, count))
+                    next_block += count
+                step += 1
                 pending = (g, staged_x, staged_w)
                 s0 += n
         finish(*pending)

@@ -20,19 +20,20 @@ K_PASS = P * PACK
 PASSES = K // K_PASS
 W_LOAD = 2
 W_BLOCKS = E * PASSES
+RAW_PLACES = 3
 
 FLOPS = 2 * K * S * N
 BYTES = 4 * (K * T + E * K * N + S + N * T) + 2 * (S + 3 * T)
 
-WIDE = 1536
-WINDOW = WIDE + 8
-CUTS = [[WIDE, WIDE], [WIDE, WIDE], [1024, 768, 512, 384, 256, 128]]
-FIRST_CUTS = [(0, 256), (256, 768), (768, WIDE)]
-PIECE = 1024
-WEIGHT_JOBS = [[8], [8, 4], [8, 4], [4]]
-VECTOR_EMPTIES = 256
+WINDOW = S + 8
+FIRST_CUTS = [(0, 256), (256, 768), (768, 1792), (1792, S)]
+LAST_UNITS = [1536, 768, 384, 256, 128]
 HELD = 256
+PIECE = 1024
+BLOCK_WORDS = N * PACK // 2
+VECTOR_EMPTIES = 256
 TOKEN_CUTS = [640, 384]
+LAST = 128
 
 
 def pieces(width):
@@ -52,77 +53,67 @@ def tile_moe_pre_lin_none_kernel(tc, xT, w, gate, offs, pos1, pos2, pos3, out):
     nc = tc.nc
     with ExitStack() as ctx:
         keep = ctx.enter_context(tc.tile_pool(name="keep", bufs=1))
-        two = ctx.enter_context(tc.tile_pool(name="two", bufs=2))
         three = ctx.enter_context(tc.tile_pool(name="three", bufs=3))
-        five = ctx.enter_context(tc.tile_pool(name="five", bufs=5))
-        six = ctx.enter_context(tc.tile_pool(name="six", bufs=6))
+        four = ctx.enter_context(tc.tile_pool(name="four", bufs=4))
         psum = ctx.enter_context(tc.psum_pool(name="psum", bufs=8))
 
         offsets = keep.tile([P, S // 16], U16, name="offsets")
         nc.sync.dma_start(offsets[:], offs)
         gates = keep.tile([P, S], F32, name="gates")
-        y = keep.tile([P, S], F32, name="y")
-        picked = keep.tile([P, 2 * PACK * WIDE], F32, name="picked")
+        picked = keep.tile([P, 6 * S], F32, name="picked", align_bytes=64)
         x_codes = [keep.tile([P, S], U32, name=f"x_codes{g}", align_bytes=64) for g in range(PASSES)]
         x_scales = [keep.tile([P, S], U8, name=f"x_scales{g}", align_bytes=64) for g in range(PASSES)]
         w_codes = keep.tile([P, W_BLOCKS * N], U32, name="w_codes", align_bytes=64)
         w_scales = keep.tile([P, W_BLOCKS * N], U8, name="w_scales", align_bytes=64)
+        w_raw = keep.tile([P, RAW_PLACES * W_LOAD * PACK * N], F32, name="w_raw", tag="w_raw_then_y")
         w_blocks = w.rearrange("e (g p j) n -> p (e g) (j n)", p=P, j=PACK)
 
         def load_rows(g, j):
-            window = six.tile([P, WINDOW], F32, name="window")
+            window = four.tile([P, WINDOW], F32, name="window")
             src = xT[g * K_PASS:(g + 1) * K_PASS, :].rearrange("(p j) t -> p j t", j=PACK)
             nc.sync.dma_start(window[:, 0:T], src[:, j, :])
             return window
 
-        def load_gate(start, stop):
-            nc.sync.dma_start(gates[:, start:stop], gate[0:P, start:stop])
+        def gather(window, plane, s0, n):
+            nc.vector.tensor_tensor(
+                plane, window[:].indirect(offsets[:, s0 // 16:(s0 + n) // 16]), gates[:, s0:s0 + n], MULT
+            )
 
-        def gather(windows, s0, n, base, split_first):
-            planes = picked[:, base:base + PACK * n].rearrange("p (j s) -> p j s", j=PACK)
-            for j in range(PACK):
-                cuts = FIRST_CUTS if split_first and j == 0 else [(0, n)]
-                for a, b in cuts:
-                    nc.vector.tensor_tensor(
-                        planes[:, j, a:b],
-                        windows[j][:].indirect(offsets[:, (s0 + a) // 16:(s0 + b) // 16]),
-                        gates[:, s0 + a:s0 + b],
-                        MULT,
-                    )
+        def interleave(planes, s0, n):
             staged = []
             for a in range(0, n, PIECE):
                 size = min(PIECE, n - a)
-                grouped = three.tile([P, size, PACK], BF16, name="x_grouped", align_bytes=64)
+                grouped = three.tile([P, size * PACK], BF16, name="x_grouped", align_bytes=64)
                 nc.scalar.copy(
-                    grouped[:].rearrange("p (c i) j -> p c j i", i=4),
+                    grouped[:].rearrange("p (c i j) -> p c j i", i=4, j=PACK),
                     planes[:, :, a:a + size].rearrange("p j (c i) -> p c j i", i=4),
                 )
-                staged.append((grouped, s0 + a, size))
+                staged.append((grouped[:], s0 + a, size))
             return staged
 
         def quantize(grouped, codes, scales, start, size):
-            flat = grouped[:].rearrange("p n j -> p (n j)")
             for a, width in pieces(size):
                 nc.vector.quantize_mx(
                     out=codes[:, start + a:start + a + width].bitcast(FP8X4),
                     scales=scales[:, start + a:start + a + width],
-                    in_=flat[:, PACK * a:PACK * (a + width)],
+                    in_=grouped[:, PACK * a:PACK * (a + width)],
                 )
 
-        def stage_weights(b0, count):
-            grouped = two.tile([P, count * N, PACK], BF16, name="w_grouped", align_bytes=64)
+        def quantize_weights(b0, count, column):
+            grouped = picked[:, column:column + count * BLOCK_WORDS].bitcast(BF16)
             for first in range(0, count, W_LOAD):
-                raw = five.tile([P, W_LOAD, PACK * N], F32, name="w_raw")
-                nc.sync.dma_start(raw[:], w_blocks[:, b0 + first:b0 + first + W_LOAD, :])
+                at = (b0 + first) // W_LOAD % RAW_PLACES * W_LOAD * PACK * N
+                raw = w_raw[:, at:at + W_LOAD * PACK * N].rearrange("p (b c) -> p b c", b=W_LOAD)
+                nc.sync.dma_start(raw, w_blocks[:, b0 + first:b0 + first + W_LOAD, :])
                 for b in range(W_LOAD):
-                    cols = slice((first + b) * N, (first + b + 1) * N)
+                    cols = slice((first + b) * N * PACK, (first + b + 1) * N * PACK)
                     nc.scalar.copy(
-                        grouped[:, cols, :].rearrange("p (c i) j -> p c j i", i=4),
+                        grouped[:, cols].rearrange("p (c i j) -> p c j i", i=4, j=PACK),
                         raw[:, b, :].rearrange("p (j c i) -> p c j i", j=PACK, i=4),
                     )
-            return grouped, b0 * N, count * N
+            quantize(grouped, w_codes, w_scales, b0 * N, count * N)
 
-        def multiply(s0, n):
+        def multiply(y, s0, n):
             start = s0
             while start < s0 + n:
                 e = start // C
@@ -145,60 +136,75 @@ def tile_moe_pre_lin_none_kernel(tc, xT, w, gate, offs, pos1, pos2, pos3, out):
                     nc.scalar.copy(y[:, start:stop], acc[:])
                 start = stop
 
-        def finish(g, staged_x, staged_w):
-            for grouped, start, size in staged_w:
-                quantize(grouped, w_codes, w_scales, start, size)
-            for grouped, start, size in staged_x:
-                quantize(grouped, x_codes[g], x_scales[g], start, size)
-            if g == PASSES - 1:
-                for grouped, start, size in staged_x:
-                    multiply(start, size)
-
-        step = 0
-        next_block = 0
-        pending = (0, [], [])
-        base = 0
-        for g in range(PASSES):
-            windows = []
-            for j in range(PACK):
-                windows.append(load_rows(g, j))
-                if g == 0 and j == 0:
-                    for a, b in FIRST_CUTS:
-                        load_gate(a, b)
-            if g == 0:
-                load_gate(WIDE, S)
-            s0 = 0
-            for n in CUTS[g]:
-                staged_x = gather(windows, s0, n, base, g == 0 and s0 == 0)
-                base = PACK * WIDE - base
-                if g == PASSES - 1 and s0 + n > S - HELD:
-                    staged_x = pending[1] + staged_x
-                else:
-                    finish(*pending)
-                staged_w = []
-                for count in WEIGHT_JOBS[step] if step < len(WEIGHT_JOBS) else []:
-                    staged_w.append(stage_weights(next_block, count))
-                    next_block += count
-                step += 1
-                pending = (g, staged_x, staged_w)
-                s0 += n
-        finish(*pending)
-
+        planes = picked[:, 0:PACK * S].rearrange("p (j s) -> p j s", j=PACK)
+        window = load_rows(0, 0)
+        for a, b in FIRST_CUTS:
+            nc.sync.dma_start(gates[:, a:b], gate[0:P, a:b])
+            gather(window, planes[:, 0, a:b], a, b - a)
+        quantize_weights(0, 4, S)
+        gather(load_rows(0, 1), planes[:, 1, :], 0, S)
+        quantize_weights(4, 8, 2 * S)
+        gather(load_rows(0, 2), planes[:, 2, :], 0, S)
+        window = load_rows(0, 3)
+        quantize_weights(12, 8, 4 * S - 4 * BLOCK_WORDS)
+        quantize_weights(20, 4, 5 * S)
+        gather(window, planes[:, 3, :], 0, S)
         lists = []
         for r, pos in enumerate((pos1, pos2, pos3)):
             tile = keep.tile([P, T // 16], U16, name=f"pos{r}")
             nc.sync.dma_start(tile[:], pos)
             lists.append(tile)
+        staged = interleave(planes, 0, S)
+
+        planes = picked[:, 2 * S:6 * S].rearrange("p (j s) -> p j s", j=PACK)
+        for j in (2, 3, 0, 1):
+            if j == 0:
+                for piece in staged:
+                    quantize(piece[0], x_codes[0], x_scales[0], piece[1], piece[2])
+            gather(load_rows(1, j), planes[:, j, :], 0, S)
+        quantize_weights(24, 12, 0)
+        staged = interleave(planes, 0, S)
+
+        y = keep.tile([P, S], F32, name="y", tag="w_raw_then_y")
+        windows = [load_rows(2, j) for j in range(PACK)]
+        staged_pass = 1
+        s0 = 0
+        base = 0
+        for n in LAST_UNITS:
+            planes = picked[:, base:base + PACK * n].rearrange("p (j s) -> p j s", j=PACK)
+            for j in range(PACK):
+                gather(windows[j], planes[:, j, :], s0, n)
+            if staged_pass == 1:
+                for piece in staged:
+                    quantize(piece[0], x_codes[1], x_scales[1], piece[1], piece[2])
+                staged = interleave(planes, s0, n)
+            elif s0 + n > S - HELD:
+                staged = staged + interleave(planes, s0, n)
+            else:
+                fresh = interleave(planes, s0, n)
+                for piece in staged:
+                    quantize(piece[0], x_codes[2], x_scales[2], piece[1], piece[2])
+                for piece in staged:
+                    multiply(y, piece[1], piece[2])
+                staged = fresh
+            staged_pass = 2
+            s0 += n
+            base = 2 * S - base
+        for piece in staged:
+            quantize(piece[0], x_codes[2], x_scales[2], piece[1], piece[2])
+        for piece in staged:
+            multiply(y, piece[1], piece[2])
+
         early, late = TOKEN_CUTS
-        first = picked[:, 0:PACK * early].rearrange("p (r t) -> p r t", r=PACK)
-        second = picked[:, PACK * early:PACK * early + 3 * late].rearrange("p (r t) -> p r t", r=3)
-        for parts, t0, n in ((first, 0, early), (second, early, late)):
-            for r in range(3):
-                nc.vector.tensor_copy(parts[:, r, :], y[:].indirect(lists[r][:, t0 // 16:(t0 + n) // 16]))
-        nc.gpsimd.tensor_tensor(first[:, 3, :], first[:, 0, :], first[:, 1, :], ADD)
-        nc.gpsimd.tensor_tensor(first[:, 3, :], first[:, 3, :], first[:, 2, :], ADD)
-        nc.sync.dma_start(out[:, 0:early], first[:, 3, :])
-        total = first[:, 2, 0:late]
-        nc.gpsimd.tensor_tensor(total, second[:, 0, :], second[:, 1, :], ADD)
-        nc.vector.tensor_tensor(total, total, second[:, 2, :], ADD)
-        nc.sync.dma_start(out[:, early:T], total)
+        sums = picked[:, 0:3 * T].rearrange("p (r t) -> p r t", r=3)
+        for t0, n in ((0, early), (early, late)):
+            nc.vector.tensor_copy(sums[:, 0, t0:t0 + n], y[:].indirect(lists[0][:, t0 // 16:(t0 + n) // 16]))
+        for t0, n in ((0, early), (early, late)):
+            nc.vector.tensor_tensor(
+                sums[:, 1, t0:t0 + n], y[:].indirect(lists[1][:, t0 // 16:(t0 + n) // 16]), sums[:, 0, t0:t0 + n], ADD
+            )
+        for t0, n in ((0, early), (early, late - LAST), (T - LAST, LAST)):
+            nc.vector.tensor_tensor(
+                sums[:, 2, t0:t0 + n], y[:].indirect(lists[2][:, t0 // 16:(t0 + n) // 16]), sums[:, 1, t0:t0 + n], ADD
+            )
+            nc.sync.dma_start(out[:, t0:t0 + n], sums[:, 2, t0:t0 + n])

@@ -20,17 +20,16 @@ K_PASS = P * PACK
 PASSES = K // K_PASS
 W_LOAD = 2
 W_BLOCKS = E * PASSES
-RAW_PLACES = 3
 
 FLOPS = 2 * K * S * N
 BYTES = 4 * (K * T + E * K * N + S + N * T) + 2 * (S + 3 * T)
 
 WINDOW = S + 8
-FIRST_CUTS = [(0, 256), (256, 768), (768, 1792), (1792, S)]
+FIRST_CUTS = [(0, 128), (128, 384), (384, 896), (896, 1920), (1920, S)]
 LAST_UNITS = [1536, 768, 384, 256, 128]
 HELD = 256
 PIECE = 1024
-BLOCK_WORDS = N * PACK // 2
+BLOCK = N * PACK
 VECTOR_EMPTIES = 256
 TOKEN_CUTS = [640, 384]
 LAST = 128
@@ -65,7 +64,7 @@ def tile_moe_pre_lin_none_kernel(tc, xT, w, gate, offs, pos1, pos2, pos3, out):
         x_scales = [keep.tile([P, S], U8, name=f"x_scales{g}", align_bytes=64) for g in range(PASSES)]
         w_codes = keep.tile([P, W_BLOCKS * N], U32, name="w_codes", align_bytes=64)
         w_scales = keep.tile([P, W_BLOCKS * N], U8, name="w_scales", align_bytes=64)
-        w_raw = keep.tile([P, RAW_PLACES * W_LOAD * PACK * N], F32, name="w_raw", tag="w_raw_then_y")
+        y = keep.tile([P, S], F32, name="y")
         w_blocks = w.rearrange("e (g p j) n -> p (e g) (j n)", p=P, j=PACK)
 
         def load_rows(g, j):
@@ -99,19 +98,24 @@ def tile_moe_pre_lin_none_kernel(tc, xT, w, gate, offs, pos1, pos2, pos3, out):
                     in_=grouped[:, PACK * a:PACK * (a + width)],
                 )
 
-        def quantize_weights(b0, count, column):
-            grouped = picked[:, column:column + count * BLOCK_WORDS].bitcast(BF16)
-            for first in range(0, count, W_LOAD):
-                at = (b0 + first) // W_LOAD % RAW_PLACES * W_LOAD * PACK * N
-                raw = w_raw[:, at:at + W_LOAD * PACK * N].rearrange("p (b c) -> p b c", b=W_LOAD)
-                nc.sync.dma_start(raw, w_blocks[:, b0 + first:b0 + first + W_LOAD, :])
-                for b in range(W_LOAD):
-                    cols = slice((first + b) * N * PACK, (first + b + 1) * N * PACK)
+        def quantize_weights(b0, landings):
+            count = sum(blocks for column, blocks in landings)
+            grouped = three.tile([P, count * BLOCK], BF16, name="x_grouped", align_bytes=64)
+            first = 0
+            for column, blocks in landings:
+                raw = picked[:, column:column + blocks * BLOCK].rearrange("p (b c) -> p b c", b=blocks)
+                nc.sync.dma_start(raw, w_blocks[:, b0 + first:b0 + first + blocks, :])
+                for b in range(blocks):
+                    cols = slice((first + b) * BLOCK, (first + b + 1) * BLOCK)
                     nc.scalar.copy(
                         grouped[:, cols].rearrange("p (c i j) -> p c j i", i=4, j=PACK),
                         raw[:, b, :].rearrange("p (j c i) -> p c j i", j=PACK, i=4),
                     )
-            quantize(grouped, w_codes, w_scales, b0 * N, count * N)
+                first += blocks
+            quantize(grouped[:], w_codes, w_scales, b0 * N, count * N)
+
+        def side_by_side(column, loads):
+            return [(column + i * W_LOAD * BLOCK, W_LOAD) for i in range(loads)]
 
         def multiply(y, s0, n):
             start = s0
@@ -141,13 +145,13 @@ def tile_moe_pre_lin_none_kernel(tc, xT, w, gate, offs, pos1, pos2, pos3, out):
         for a, b in FIRST_CUTS:
             nc.sync.dma_start(gates[:, a:b], gate[0:P, a:b])
             gather(window, planes[:, 0, a:b], a, b - a)
-        quantize_weights(0, 4, S)
+        quantize_weights(0, side_by_side(S, 2))
         gather(load_rows(0, 1), planes[:, 1, :], 0, S)
-        quantize_weights(4, 8, 2 * S)
+        quantize_weights(4, side_by_side(5 * S, 1) + side_by_side(2 * S, 3))
         gather(load_rows(0, 2), planes[:, 2, :], 0, S)
         window = load_rows(0, 3)
-        quantize_weights(12, 8, 4 * S - 4 * BLOCK_WORDS)
-        quantize_weights(20, 4, 5 * S)
+        quantize_weights(12, side_by_side(3 * S, 2) + side_by_side(4 * S + BLOCK, 2))
+        quantize_weights(20, side_by_side(5 * S + 2 * BLOCK, 1) + [(4 * S - BLOCK // 2, 1), (5 * S + 4 * BLOCK, 1)])
         gather(window, planes[:, 3, :], 0, S)
         lists = []
         for r, pos in enumerate((pos1, pos2, pos3)):
@@ -157,15 +161,19 @@ def tile_moe_pre_lin_none_kernel(tc, xT, w, gate, offs, pos1, pos2, pos3, out):
         staged = interleave(planes, 0, S)
 
         planes = picked[:, 2 * S:6 * S].rearrange("p (j s) -> p j s", j=PACK)
-        for j in (2, 3, 0, 1):
-            if j == 0:
-                for piece in staged:
-                    quantize(piece[0], x_codes[0], x_scales[0], piece[1], piece[2])
+        for j in (2, 3):
             gather(load_rows(1, j), planes[:, j, :], 0, S)
-        quantize_weights(24, 12, 0)
+        for piece in staged[:-1]:
+            quantize(piece[0], x_codes[0], x_scales[0], piece[1], piece[2])
+        window = load_rows(1, 0)
+        gather(window, planes[:, 0, 0:S - PIECE], 0, S - PIECE)
+        quantize(staged[-1][0], x_codes[0], x_scales[0], staged[-1][1], staged[-1][2])
+        gather(window, planes[:, 0, S - PIECE:S], S - PIECE, PIECE)
+        gather(load_rows(1, 1), planes[:, 1, :], 0, S)
+        quantize_weights(24, side_by_side(0, 4))
+        quantize_weights(32, side_by_side(8 * BLOCK, 2))
         staged = interleave(planes, 0, S)
 
-        y = keep.tile([P, S], F32, name="y", tag="w_raw_then_y")
         windows = [load_rows(2, j) for j in range(PACK)]
         staged_pass = 1
         s0 = 0

@@ -18,24 +18,27 @@ P = 128
 PACK = 4
 K_PASS = P * PACK
 PASSES = K // K_PASS
-W_LOAD = 2
-W_BLOCKS = E * PASSES
+LIST = 16
 
 FLOPS = 2 * K * S * N
 BYTES = 4 * (K * T + E * K * N + S + N * T) + 2 * (S + 3 * T)
 
 WINDOW = S + 8
-FIRST_CUTS = [(0, 128), (128, 384), (384, 896), (896, 1920), (1920, S)]
-LAST_UNITS = [1536, 768, 384, 256, 128]
-HELD = 256
+PLACES = 6
+W_BLOCKS = E * PASSES
+BLOCK = PACK * N
+W_LOAD = 2
+LOAD = W_LOAD * BLOCK
 PIECE = 1024
-BLOCK = N * PACK
+FIRST_CUTS = [(0, 128), (128, 352), (352, 768), (768, 1536), (1536, S)]
+LAST_UNITS = [1536, 768, 384, 256, 128]
+HELD_UNITS = 3
 VECTOR_EMPTIES = 256
-TOKEN_CUTS = [640, 384]
-LAST = 128
+EARLY_TOKENS = 640
+LAST_TOKENS = 128
 
 
-def pieces(width):
+def quantize_widths(width):
     parts = []
     start = 0
     size = PIECE
@@ -48,18 +51,22 @@ def pieces(width):
     return parts
 
 
+def side_by_side(column, loads):
+    return [column + i * LOAD for i in range(loads)]
+
+
 def tile_moe_pre_lin_none_kernel(tc, xT, w, gate, offs, pos1, pos2, pos3, out):
     nc = tc.nc
     with ExitStack() as ctx:
         keep = ctx.enter_context(tc.tile_pool(name="keep", bufs=1))
-        three = ctx.enter_context(tc.tile_pool(name="three", bufs=3))
-        four = ctx.enter_context(tc.tile_pool(name="four", bufs=4))
+        grouped_pool = ctx.enter_context(tc.tile_pool(name="grouped", bufs=S // PIECE))
+        window_pool = ctx.enter_context(tc.tile_pool(name="windows", bufs=PACK))
         psum = ctx.enter_context(tc.psum_pool(name="psum", bufs=8))
 
-        offsets = keep.tile([P, S // 16], U16, name="offsets")
+        offsets = keep.tile([P, S // LIST], U16, name="offsets")
         nc.sync.dma_start(offsets[:], offs)
         gates = keep.tile([P, S], F32, name="gates")
-        picked = keep.tile([P, 6 * S], F32, name="picked", align_bytes=64)
+        picked = keep.tile([P, PLACES * S], F32, name="picked", align_bytes=64)
         x_codes = [keep.tile([P, S], U32, name=f"x_codes{g}", align_bytes=64) for g in range(PASSES)]
         x_scales = [keep.tile([P, S], U8, name=f"x_scales{g}", align_bytes=64) for g in range(PASSES)]
         w_codes = keep.tile([P, W_BLOCKS * N], U32, name="w_codes", align_bytes=64)
@@ -67,152 +74,148 @@ def tile_moe_pre_lin_none_kernel(tc, xT, w, gate, offs, pos1, pos2, pos3, out):
         y = keep.tile([P, S], F32, name="y")
         w_blocks = w.rearrange("e (g p j) n -> p (e g) (j n)", p=P, j=PACK)
 
-        def load_rows(g, j):
-            window = four.tile([P, WINDOW], F32, name="window")
-            src = xT[g * K_PASS:(g + 1) * K_PASS, :].rearrange("(p j) t -> p j t", j=PACK)
-            nc.sync.dma_start(window[:, 0:T], src[:, j, :])
+        def load_window(g, j):
+            window = window_pool.tile([P, WINDOW], F32, name="window")
+            rows = xT[g * K_PASS:(g + 1) * K_PASS, :].rearrange("(p j) t -> p j t", j=PACK)
+            nc.sync.dma_start(window[:, 0:T], rows[:, j, :])
             return window
 
         def gather(window, plane, s0, n):
             nc.vector.tensor_tensor(
-                plane, window[:].indirect(offsets[:, s0 // 16:(s0 + n) // 16]), gates[:, s0:s0 + n], MULT
+                plane, window[:].indirect(offsets[:, s0 // LIST:(s0 + n) // LIST]), gates[:, s0:s0 + n], MULT
             )
 
-        def interleave(planes, s0, n):
+        def round_and_interleave(grouped, planes):
+            nc.scalar.copy(
+                grouped.rearrange("p (c i j) -> p c j i", i=4, j=PACK),
+                planes.rearrange("p j (c i) -> p c j i", i=4),
+            )
+
+        def interleave_slots(planes, s0, n):
             staged = []
             for a in range(0, n, PIECE):
                 size = min(PIECE, n - a)
-                grouped = three.tile([P, size * PACK], BF16, name="x_grouped", align_bytes=64)
-                nc.scalar.copy(
-                    grouped[:].rearrange("p (c i j) -> p c j i", i=4, j=PACK),
-                    planes[:, :, a:a + size].rearrange("p j (c i) -> p c j i", i=4),
-                )
-                staged.append((grouped[:], s0 + a, size))
+                grouped = grouped_pool.tile([P, size * PACK], BF16, name="grouped", align_bytes=64)
+                round_and_interleave(grouped[:], planes[:, :, a:a + size])
+                staged.append((grouped, s0 + a, size))
             return staged
 
         def quantize(grouped, codes, scales, start, size):
-            for a, width in pieces(size):
+            for a, width in quantize_widths(size):
                 nc.vector.quantize_mx(
                     out=codes[:, start + a:start + a + width].bitcast(FP8X4),
                     scales=scales[:, start + a:start + a + width],
                     in_=grouped[:, PACK * a:PACK * (a + width)],
                 )
 
-        def quantize_weights(b0, landings):
-            count = sum(blocks for column, blocks in landings)
-            grouped = three.tile([P, count * BLOCK], BF16, name="x_grouped", align_bytes=64)
-            first = 0
-            for column, blocks in landings:
-                raw = picked[:, column:column + blocks * BLOCK].rearrange("p (b c) -> p b c", b=blocks)
-                nc.sync.dma_start(raw, w_blocks[:, b0 + first:b0 + first + blocks, :])
-                for b in range(blocks):
+        def quantize_slots(g, staged):
+            for grouped, start, size in staged:
+                quantize(grouped, x_codes[g], x_scales[g], start, size)
+
+        def stage_weights(grouped, b0, first_load, columns):
+            for load, column in enumerate(columns, first_load):
+                first = load * W_LOAD
+                raw = picked[:, column:column + LOAD].rearrange("p (b c) -> p b c", b=W_LOAD)
+                nc.sync.dma_start(raw, w_blocks[:, b0 + first:b0 + first + W_LOAD, :])
+                for b in range(W_LOAD):
                     cols = slice((first + b) * BLOCK, (first + b + 1) * BLOCK)
-                    nc.scalar.copy(
-                        grouped[:, cols].rearrange("p (c i j) -> p c j i", i=4, j=PACK),
-                        raw[:, b, :].rearrange("p (j c i) -> p c j i", j=PACK, i=4),
-                    )
-                first += blocks
-            quantize(grouped[:], w_codes, w_scales, b0 * N, count * N)
+                    round_and_interleave(grouped[:, cols], raw[:, b, :].rearrange("p (j n) -> p j n", j=PACK))
 
-        def side_by_side(column, loads):
-            return [(column + i * W_LOAD * BLOCK, W_LOAD) for i in range(loads)]
+        def quantize_weights(b0, columns, plane=None):
+            half = len(columns) // 2
+            grouped = grouped_pool.tile([P, len(columns) * LOAD], BF16, name="grouped", align_bytes=64)
+            stage_weights(grouped, b0, 0, columns[:half])
+            window = load_window(0, plane) if plane is not None else None
+            stage_weights(grouped, b0, half, columns[half:])
+            quantize(grouped, w_codes, w_scales, b0 * N, len(columns) * W_LOAD * N)
+            return window
 
-        def multiply(y, s0, n):
-            start = s0
-            while start < s0 + n:
-                e = start // C
-                stop = min((e + 1) * C, s0 + n)
-                acc = psum.tile([P, stop - start], F32, name="acc")
-                for g in range(PASSES):
-                    cols = slice((e * PASSES + g) * N, (e * PASSES + g + 1) * N)
-                    nc.tensor.matmul_mx(
-                        out=acc[:],
-                        lhsT=w_codes[:, cols].bitcast(FP8X4),
-                        lhsT_scale=w_scales[:, cols],
-                        rhs=x_codes[g][:, start:stop].bitcast(FP8X4),
-                        rhs_scale=x_scales[g][:, start:stop],
-                        start=(g == 0),
-                        stop=(g == PASSES - 1),
-                    )
-                if start >= S - VECTOR_EMPTIES:
-                    nc.vector.tensor_copy(y[:, start:stop], acc[:])
-                else:
-                    nc.scalar.copy(y[:, start:stop], acc[:])
-                start = stop
+        def multiply(staged):
+            for grouped, s0, n in staged:
+                start = s0
+                while start < s0 + n:
+                    e = start // C
+                    stop = min((e + 1) * C, s0 + n)
+                    acc = psum.tile([P, stop - start], F32, name="acc")
+                    for g in range(PASSES):
+                        cols = slice((e * PASSES + g) * N, (e * PASSES + g + 1) * N)
+                        nc.tensor.matmul_mx(
+                            out=acc[:],
+                            lhsT=w_codes[:, cols].bitcast(FP8X4),
+                            lhsT_scale=w_scales[:, cols],
+                            rhs=x_codes[g][:, start:stop].bitcast(FP8X4),
+                            rhs_scale=x_scales[g][:, start:stop],
+                            start=(g == 0),
+                            stop=(g == PASSES - 1),
+                        )
+                    if start >= S - VECTOR_EMPTIES:
+                        nc.vector.tensor_copy(y[:, start:stop], acc[:])
+                    else:
+                        nc.scalar.copy(y[:, start:stop], acc[:])
+                    start = stop
 
         planes = picked[:, 0:PACK * S].rearrange("p (j s) -> p j s", j=PACK)
-        window = load_rows(0, 0)
+        window = load_window(0, 0)
         for a, b in FIRST_CUTS:
             nc.sync.dma_start(gates[:, a:b], gate[0:P, a:b])
             gather(window, planes[:, 0, a:b], a, b - a)
-        quantize_weights(0, side_by_side(S, 2))
-        gather(load_rows(0, 1), planes[:, 1, :], 0, S)
-        quantize_weights(4, side_by_side(5 * S, 1) + side_by_side(2 * S, 3))
-        gather(load_rows(0, 2), planes[:, 2, :], 0, S)
-        window = load_rows(0, 3)
-        quantize_weights(12, side_by_side(3 * S, 2) + side_by_side(4 * S + BLOCK, 2))
-        quantize_weights(20, side_by_side(5 * S + 2 * BLOCK, 1) + [(4 * S - BLOCK // 2, 1), (5 * S + 4 * BLOCK, 1)])
-        gather(window, planes[:, 3, :], 0, S)
+        gather(load_window(0, 1), planes[:, 1, :], 0, S)
+        landings = [side_by_side((i + 2) * S, 3) + side_by_side((PLACES - 1) * S + i * LOAD, 1) for i in range(3)]
+        batch = len(landings[0]) * W_LOAD
+        quantize_weights(0, landings[0])
+        gather(quantize_weights(batch, landings[1], plane=2), planes[:, 2, :], 0, S)
+        gather(quantize_weights(2 * batch, landings[2], plane=3), planes[:, 3, :], 0, S)
         lists = []
         for r, pos in enumerate((pos1, pos2, pos3)):
-            tile = keep.tile([P, T // 16], U16, name=f"pos{r}")
+            tile = keep.tile([P, T // LIST], U16, name=f"pos{r}")
             nc.sync.dma_start(tile[:], pos)
             lists.append(tile)
-        staged = interleave(planes, 0, S)
+        staged = interleave_slots(planes, 0, S)
 
-        planes = picked[:, 2 * S:6 * S].rearrange("p (j s) -> p j s", j=PACK)
+        planes = picked[:, 2 * S:PLACES * S].rearrange("p (j s) -> p j s", j=PACK)
         for j in (2, 3):
-            gather(load_rows(1, j), planes[:, j, :], 0, S)
-        for piece in staged[:-1]:
-            quantize(piece[0], x_codes[0], x_scales[0], piece[1], piece[2])
-        window = load_rows(1, 0)
+            gather(load_window(1, j), planes[:, j, :], 0, S)
+        quantize_slots(0, staged[:-1])
+        window = load_window(1, 0)
         gather(window, planes[:, 0, 0:S - PIECE], 0, S - PIECE)
-        quantize(staged[-1][0], x_codes[0], x_scales[0], staged[-1][1], staged[-1][2])
+        quantize_slots(0, staged[-1:])
         gather(window, planes[:, 0, S - PIECE:S], S - PIECE, PIECE)
-        gather(load_rows(1, 1), planes[:, 1, :], 0, S)
-        quantize_weights(24, side_by_side(0, 4))
-        quantize_weights(32, side_by_side(8 * BLOCK, 2))
-        staged = interleave(planes, 0, S)
+        gather(load_window(1, 1), planes[:, 1, :], 0, S)
+        quantize_weights(3 * batch, side_by_side(0, 4))
+        quantize_weights(4 * batch, side_by_side(4 * LOAD, 2))
+        staged = interleave_slots(planes, 0, S)
 
-        windows = [load_rows(2, j) for j in range(PACK)]
-        staged_pass = 1
+        windows = [load_window(2, j) for j in range(PACK)]
         s0 = 0
-        base = 0
-        for n in LAST_UNITS:
+        for u, n in enumerate(LAST_UNITS):
+            base = u % 2 * 2 * S
             planes = picked[:, base:base + PACK * n].rearrange("p (j s) -> p j s", j=PACK)
             for j in range(PACK):
                 gather(windows[j], planes[:, j, :], s0, n)
-            if staged_pass == 1:
-                for piece in staged:
-                    quantize(piece[0], x_codes[1], x_scales[1], piece[1], piece[2])
-                staged = interleave(planes, s0, n)
-            elif s0 + n > S - HELD:
-                staged = staged + interleave(planes, s0, n)
+            if u == 0:
+                quantize_slots(1, staged)
+                staged = interleave_slots(planes, s0, n)
+            elif u > len(LAST_UNITS) - HELD_UNITS:
+                staged = staged + interleave_slots(planes, s0, n)
             else:
-                fresh = interleave(planes, s0, n)
-                for piece in staged:
-                    quantize(piece[0], x_codes[2], x_scales[2], piece[1], piece[2])
-                for piece in staged:
-                    multiply(y, piece[1], piece[2])
+                fresh = interleave_slots(planes, s0, n)
+                quantize_slots(2, staged)
+                multiply(staged)
                 staged = fresh
-            staged_pass = 2
             s0 += n
-            base = 2 * S - base
-        for piece in staged:
-            quantize(piece[0], x_codes[2], x_scales[2], piece[1], piece[2])
-        for piece in staged:
-            multiply(y, piece[1], piece[2])
+        quantize_slots(2, staged)
+        multiply(staged)
 
-        early, late = TOKEN_CUTS
         sums = picked[:, 0:3 * T].rearrange("p (r t) -> p r t", r=3)
-        for t0, n in ((0, early), (early, late)):
-            nc.vector.tensor_copy(sums[:, 0, t0:t0 + n], y[:].indirect(lists[0][:, t0 // 16:(t0 + n) // 16]))
-        for t0, n in ((0, early), (early, late)):
-            nc.vector.tensor_tensor(
-                sums[:, 1, t0:t0 + n], y[:].indirect(lists[1][:, t0 // 16:(t0 + n) // 16]), sums[:, 0, t0:t0 + n], ADD
-            )
-        for t0, n in ((0, early), (early, late - LAST), (T - LAST, LAST)):
-            nc.vector.tensor_tensor(
-                sums[:, 2, t0:t0 + n], y[:].indirect(lists[2][:, t0 // 16:(t0 + n) // 16]), sums[:, 1, t0:t0 + n], ADD
-            )
-            nc.sync.dma_start(out[:, t0:t0 + n], sums[:, 2, t0:t0 + n])
+
+        def fetch(r, start, stop):
+            return y[:].indirect(lists[r][:, start // LIST:stop // LIST])
+
+        runs = [(0, EARLY_TOKENS), (EARLY_TOKENS, T)]
+        for a, b in runs:
+            nc.vector.tensor_copy(sums[:, 0, a:b], fetch(0, a, b))
+        for a, b in runs:
+            nc.vector.tensor_tensor(sums[:, 1, a:b], fetch(1, a, b), sums[:, 0, a:b], ADD)
+        for a, b in [runs[0], (EARLY_TOKENS, T - LAST_TOKENS), (T - LAST_TOKENS, T)]:
+            nc.vector.tensor_tensor(sums[:, 2, a:b], fetch(2, a, b), sums[:, 1, a:b], ADD)
+            nc.sync.dma_start(out[:, a:b], sums[:, 2, a:b])

@@ -31,9 +31,11 @@ W_LOAD = 2
 LOAD = W_LOAD * BLOCK
 PIECE = 1024
 FIRST_CUTS = [(0, 128), (128, 352), (352, 768), (768, 1536), (1536, S)]
-LAST_UNITS = [1536, 768, 384, 256, 128]
+LAST_UNITS = [1536, 768, 512, 256]
+LATE = S - 256
+LATE_EXPERT = LATE // C
 HELD_UNITS = 3
-VECTOR_EMPTIES = 256
+VECTOR_EMPTIES = 128
 EARLY_TOKENS = 640
 LAST_TOKENS = 128
 
@@ -60,22 +62,27 @@ def tile_moe_pre_lin_none_kernel(tc, xT, w, gate, offs, pos1, pos2, pos3, out):
     with ExitStack() as ctx:
         keep = ctx.enter_context(tc.tile_pool(name="keep", bufs=1))
         grouped_pool = ctx.enter_context(tc.tile_pool(name="grouped", bufs=S // PIECE))
-        window_pool = ctx.enter_context(tc.tile_pool(name="windows", bufs=PACK))
+        window_pool = ctx.enter_context(tc.tile_pool(name="windows", bufs=3))
         psum = ctx.enter_context(tc.psum_pool(name="psum", bufs=8))
 
         offsets = keep.tile([P, S // LIST], U16, name="offsets")
         nc.sync.dma_start(offsets[:], offs)
         gates = keep.tile([P, S], F32, name="gates")
         picked = keep.tile([P, PLACES * S], F32, name="picked", align_bytes=64)
-        x_codes = [keep.tile([P, S], U32, name=f"x_codes{g}", align_bytes=64) for g in range(PASSES)]
+        x_codes = [keep.tile([P, LATE if g < 2 else S], U32, name=f"x_codes{g}", align_bytes=64) for g in range(PASSES)]
+        late_codes = []
+        late_x0 = keep.tile([P, PACK * (S - LATE)], BF16, name="late_x0", align_bytes=64)
+        late_w = keep.tile([P, (E - LATE_EXPERT) * PASSES * BLOCK], BF16, name="late_w", align_bytes=64)
         x_scales = [keep.tile([P, S], U8, name=f"x_scales{g}", align_bytes=64) for g in range(PASSES)]
-        w_codes = keep.tile([P, W_BLOCKS * N], U32, name="w_codes", align_bytes=64)
+        w_codes = keep.tile([P, LATE_EXPERT * PASSES * N], U32, name="w_codes", align_bytes=64)
         w_scales = keep.tile([P, W_BLOCKS * N], U8, name="w_scales", align_bytes=64)
-        y = keep.tile([P, S], F32, name="y")
         w_blocks = w.rearrange("e (g p j) n -> p (e g) (j n)", p=P, j=PACK)
 
-        def load_window(g, j):
-            window = window_pool.tile([P, WINDOW], F32, name="window")
+        def load_window(g, j, narrow=False):
+            if narrow:
+                window = keep.tile([P, LAST_UNITS[0] + 8], F32, name=f"narrow{j}")
+            else:
+                window = window_pool.tile([P, WINDOW], F32, name="window")
             rows = xT[g * K_PASS:(g + 1) * K_PASS, :].rearrange("(p j) t -> p j t", j=PACK)
             nc.sync.dma_start(window[:, 0:T], rows[:, j, :])
             return window
@@ -100,17 +107,29 @@ def tile_moe_pre_lin_none_kernel(tc, xT, w, gate, offs, pos1, pos2, pos3, out):
                 staged.append((grouped, s0 + a, size))
             return staged
 
+        def x_words(g, start, stop):
+            if g < 2 and start >= LATE:
+                first = g * (S - LATE) - LATE
+                return late_codes[0][:, first + start:first + stop]
+            return x_codes[g][:, start:stop]
+
+        def w_words(start, stop):
+            first = LATE_EXPERT * PASSES * N
+            if start >= first:
+                return late_codes[0][:, 2 * (S - LATE) + start - first:2 * (S - LATE) + stop - first]
+            return w_codes[:, start:stop]
+
         def quantize(grouped, codes, scales, start, size):
             for a, width in quantize_widths(size):
                 nc.vector.quantize_mx(
-                    out=codes[:, start + a:start + a + width].bitcast(FP8X4),
+                    out=codes(start + a, start + a + width).bitcast(FP8X4),
                     scales=scales[:, start + a:start + a + width],
                     in_=grouped[:, PACK * a:PACK * (a + width)],
                 )
 
         def quantize_slots(g, staged):
             for grouped, start, size in staged:
-                quantize(grouped, x_codes[g], x_scales[g], start, size)
+                quantize(grouped, lambda a, b: x_words(g, a, b), x_scales[g], start, size)
 
         def stage_weights(grouped, b0, first_load, columns):
             for load, column in enumerate(columns, first_load):
@@ -127,7 +146,7 @@ def tile_moe_pre_lin_none_kernel(tc, xT, w, gate, offs, pos1, pos2, pos3, out):
             stage_weights(grouped, b0, 0, columns[:half])
             window = load_window(0, plane) if plane is not None else None
             stage_weights(grouped, b0, half, columns[half:])
-            quantize(grouped, w_codes, w_scales, b0 * N, len(columns) * W_LOAD * N)
+            quantize(grouped, w_words, w_scales, b0 * N, len(columns) * W_LOAD * N)
             return window
 
         def multiply(staged):
@@ -135,20 +154,20 @@ def tile_moe_pre_lin_none_kernel(tc, xT, w, gate, offs, pos1, pos2, pos3, out):
                 start = s0
                 while start < s0 + n:
                     e = start // C
-                    stop = min((e + 1) * C, s0 + n)
+                    stop = start + (C // 2 if e == E - 1 else C)
                     acc = psum.tile([P, stop - start], F32, name="acc")
                     for g in range(PASSES):
                         cols = slice((e * PASSES + g) * N, (e * PASSES + g + 1) * N)
                         nc.tensor.matmul_mx(
                             out=acc[:],
-                            lhsT=w_codes[:, cols].bitcast(FP8X4),
+                            lhsT=w_words(cols.start, cols.stop).bitcast(FP8X4),
                             lhsT_scale=w_scales[:, cols],
-                            rhs=x_codes[g][:, start:stop].bitcast(FP8X4),
+                            rhs=x_words(g, start, stop).bitcast(FP8X4),
                             rhs_scale=x_scales[g][:, start:stop],
                             start=(g == 0),
                             stop=(g == PASSES - 1),
                         )
-                    if start >= S - VECTOR_EMPTIES:
+                    if start == LATE:
                         nc.vector.tensor_copy(y[:, start:stop], acc[:])
                     else:
                         nc.scalar.copy(y[:, start:stop], acc[:])
@@ -170,41 +189,74 @@ def tile_moe_pre_lin_none_kernel(tc, xT, w, gate, offs, pos1, pos2, pos3, out):
             tile = keep.tile([P, T // LIST], U16, name=f"pos{r}")
             nc.sync.dma_start(tile[:], pos)
             lists.append(tile)
-        staged = interleave_slots(planes, 0, S)
+        staged = interleave_slots(planes, 0, LATE)
+        round_and_interleave(late_x0[:], planes[:, :, LATE:S])
 
         planes = picked[:, 2 * S:PLACES * S].rearrange("p (j s) -> p j s", j=PACK)
         for j in (2, 3):
             gather(load_window(1, j), planes[:, j, :], 0, S)
-        quantize_slots(0, staged[:-1])
-        window = load_window(1, 0)
-        gather(window, planes[:, 0, 0:S - PIECE], 0, S - PIECE)
-        quantize_slots(0, staged[-1:])
-        gather(window, planes[:, 0, S - PIECE:S], S - PIECE, PIECE)
-        gather(load_window(1, 1), planes[:, 1, :], 0, S)
+        quantize_slots(0, staged)
+        for j in (0, 1):
+            gather(load_window(1, j), planes[:, j, :], 0, S)
         quantize_weights(3 * batch, side_by_side(0, 4))
-        quantize_weights(4 * batch, side_by_side(4 * LOAD, 2))
-        staged = interleave_slots(planes, 0, S)
+        raw = picked[:, 4 * LOAD:6 * LOAD].rearrange("p (b c) -> p b c", b=4)
+        nc.sync.dma_start(raw, w_blocks[:, 4 * batch:W_BLOCKS, :])
+        single = grouped_pool.tile([P, BLOCK], BF16, name="grouped", align_bytes=64)
+        for b in range(4):
+            target = single[:] if b == 0 else late_w[:, (b - 1) * BLOCK:b * BLOCK]
+            round_and_interleave(target, raw[:, b, :].rearrange("p (j n) -> p j n", j=PACK))
+        quantize(single, w_words, w_scales, 4 * batch * N, N)
+        staged1 = interleave_slots(planes, 0, S)
+        last, start, size = staged1[-1]
+        late_x1 = last[:, PACK * (LATE - start):PACK * size]
+        staged1[-1] = (last, start, LATE - start)
 
-        windows = [load_window(2, j) for j in range(PACK)]
-        s0 = 0
-        for u, n in enumerate(LAST_UNITS):
-            base = u % 2 * 2 * S
+        windows = [load_window(2, j, narrow=j >= 2) for j in range(PACK)]
+        y = window_pool.tile([P, S], F32, name="window")
+
+        def gather_unit(base, s0, n):
             planes = picked[:, base:base + PACK * n].rearrange("p (j s) -> p j s", j=PACK)
             for j in range(PACK):
                 gather(windows[j], planes[:, j, :], s0, n)
-            if u == 0:
-                quantize_slots(1, staged)
-                staged = interleave_slots(planes, s0, n)
-            elif u > len(LAST_UNITS) - HELD_UNITS:
-                staged = staged + interleave_slots(planes, s0, n)
-            else:
-                fresh = interleave_slots(planes, s0, n)
-                quantize_slots(2, staged)
-                multiply(staged)
-                staged = fresh
-            s0 += n
-        quantize_slots(2, staged)
-        multiply(staged)
+            return planes
+
+        def inside(column, n):
+            return picked[:, column:column + 2 * n].bitcast(BF16)
+
+        def interleave_parts(planes, s0, parts):
+            staged = []
+            a = 0
+            for grouped, n in parts:
+                round_and_interleave(grouped, planes[:, :, a:a + n])
+                staged.append((grouped, s0 + a, n))
+                a += n
+            return staged
+
+        held = keep.tile([P, PACK * 768], BF16, name="held", tag="held", align_bytes=64)
+        planes = gather_unit(0, 0, 1536)
+        quantize_slots(1, staged1)
+        staged_a = interleave_parts(planes, 0, [(inside(4 * S, 1024), 1024), (inside(4 * S + 2048, 512), 512)])
+        planes = gather_unit(2 * S, 1536, 768)
+        staged_b = interleave_parts(planes, 1536, [(held[:], 768)])
+        quantize_slots(2, staged_a)
+        multiply(staged_a)
+        planes = gather_unit(0, 2304, 512)
+        staged_c = interleave_parts(planes, 2304, [(inside(5 * S, 512), 512)])
+        quantize_slots(2, staged_b)
+        multiply(staged_b)
+        planes = gather_unit(2 * S, LATE, 256)
+        staged_d = interleave_parts(planes, LATE, [(inside(5 * S + 1024, 256), 256)])
+        grouped = staged_c[0][0]
+        quantize_slots(2, [(grouped[:, 0:PACK * C], 2304, C), (grouped[:, PACK * C:PACK * 2 * C], 2304 + C, C)])
+        multiply(staged_c)
+        blocks = (E - LATE_EXPERT) * PASSES
+        late_codes.append(keep.tile([P, 2 * (S - LATE) + blocks * N], U32, name="late", tag="held", align_bytes=64))
+        quantize_slots(0, [(late_x0, LATE, S - LATE)])
+        quantize_slots(1, [(late_x1, LATE, S - LATE)])
+        quantize(late_w, w_words, w_scales, LATE_EXPERT * PASSES * N, blocks * N)
+        grouped = staged_d[0][0]
+        quantize_slots(2, [(grouped[:, 0:PACK * 128], LATE, 128), (grouped[:, PACK * 128:PACK * 256], LATE + 128, 128)])
+        multiply(staged_d)
 
         sums = picked[:, 0:3 * T].rearrange("p (r t) -> p r t", r=3)
 

@@ -94,8 +94,8 @@ def tile_moe_pre_lin_none_kernel(tc, xT, w, gate, offs, pos1, pos2, pos3, out):
 
         def round_and_interleave(grouped, planes):
             nc.scalar.copy(
-                grouped.rearrange("p (c i j) -> p c j i", i=4, j=PACK),
-                planes.rearrange("p j (c i) -> p c j i", i=4),
+                grouped.rearrange("p (c i j) -> p c j i", i=2, j=PACK),
+                planes.rearrange("p j (c i) -> p c j i", i=2),
             )
 
         def interleave_slots(planes, s0, n):

@@ -33,7 +33,7 @@ PIECE = 1024
 FIRST_CUTS = [(0, 128), (128, 352), (352, 768), (768, 1536), (1536, S)]
 LAST_UNITS = [1536, 768, 512, 256]
 LATE = S - 256
-LATE_EXPERT = LATE // C
+LATE_EXPERT = 9
 HELD_UNITS = 3
 VECTOR_EMPTIES = 128
 EARLY_TOKENS = 640
@@ -198,14 +198,16 @@ def tile_moe_pre_lin_none_kernel(tc, xT, w, gate, offs, pos1, pos2, pos3, out):
         quantize_slots(0, staged)
         for j in (0, 1):
             gather(load_window(1, j), planes[:, j, :], 0, S)
-        quantize_weights(3 * batch, side_by_side(0, 4))
-        raw = picked[:, 4 * LOAD:6 * LOAD].rearrange("p (b c) -> p b c", b=4)
-        nc.sync.dma_start(raw, w_blocks[:, 4 * batch:W_BLOCKS, :])
-        single = grouped_pool.tile([P, BLOCK], BF16, name="grouped", align_bytes=64)
-        for b in range(4):
-            target = single[:] if b == 0 else late_w[:, (b - 1) * BLOCK:b * BLOCK]
-            round_and_interleave(target, raw[:, b, :].rearrange("p (j n) -> p j n", j=PACK))
-        quantize(single, w_words, w_scales, 4 * batch * N, N)
+        early_w = grouped_pool.tile([P, PASSES * BLOCK], BF16, name="grouped", align_bytes=64)
+        for e in range(LATE_EXPERT - 1, E):
+            column = (e - LATE_EXPERT + 1) * PASSES * BLOCK
+            raw = picked[:, column:column + PASSES * BLOCK].rearrange("p (b c) -> p b c", b=PASSES)
+            nc.sync.dma_start(raw, w_blocks[:, e * PASSES:(e + 1) * PASSES, :])
+            for g in range(PASSES):
+                first = ((e - LATE_EXPERT) * PASSES + g) * BLOCK
+                target = early_w[:, g * BLOCK:(g + 1) * BLOCK] if e < LATE_EXPERT else late_w[:, first:first + BLOCK]
+                round_and_interleave(target, raw[:, g, :].rearrange("p (j n) -> p j n", j=PACK))
+        quantize(early_w, w_words, w_scales, 3 * batch * N, PASSES * N)
         staged1 = interleave_slots(planes, 0, S)
         last, start, size = staged1[-1]
         late_x1 = last[:, PACK * (LATE - start):PACK * size]
@@ -246,14 +248,16 @@ def tile_moe_pre_lin_none_kernel(tc, xT, w, gate, offs, pos1, pos2, pos3, out):
         multiply(staged_b)
         planes = gather_unit(2 * S, LATE, 256)
         staged_d = interleave_parts(planes, LATE, [(inside(5 * S + 1024, 256), 256)])
+        blocks = (E - LATE_EXPERT) * PASSES
+        late_codes.append(keep.tile([P, 2 * (S - LATE) + blocks * N], U32, name="late", tag="held", align_bytes=64))
+        for first, count in ((0, 2), (2, 4)):
+            quantize(late_w[:, first * BLOCK:(first + count) * BLOCK], w_words, w_scales, (LATE_EXPERT * PASSES + first) * N, count * N)
+        quantize_slots(0, [(late_x0, LATE, S - LATE)])
+        quantize_slots(1, [(late_x1, LATE, S - LATE)])
+        quantize(late_w[:, 6 * BLOCK:9 * BLOCK], w_words, w_scales, (LATE_EXPERT * PASSES + 6) * N, 3 * N)
         grouped = staged_c[0][0]
         quantize_slots(2, [(grouped[:, 0:PACK * C], 2304, C), (grouped[:, PACK * C:PACK * 2 * C], 2304 + C, C)])
         multiply(staged_c)
-        blocks = (E - LATE_EXPERT) * PASSES
-        late_codes.append(keep.tile([P, 2 * (S - LATE) + blocks * N], U32, name="late", tag="held", align_bytes=64))
-        quantize_slots(0, [(late_x0, LATE, S - LATE)])
-        quantize_slots(1, [(late_x1, LATE, S - LATE)])
-        quantize(late_w, w_words, w_scales, LATE_EXPERT * PASSES * N, blocks * N)
         grouped = staged_d[0][0]
         quantize_slots(2, [(grouped[:, 0:PACK * 128], LATE, 128), (grouped[:, PACK * 128:PACK * 256], LATE + 128, 128)])
         multiply(staged_d)

@@ -23,19 +23,18 @@ LIST = 16
 FLOPS = 2 * K * S * N
 BYTES = 4 * (K * T + E * K * N + S + N * T) + 2 * (S + 3 * T)
 
-WINDOW = S + 8
+SPARE = 8
 PLACES = 6
 W_BLOCKS = E * PASSES
 BLOCK = PACK * N
 W_LOAD = 2
 LOAD = W_LOAD * BLOCK
 PIECE = 1024
-FIRST_CUTS = [(0, 128), (128, 352), (352, 768), (768, 1536), (1536, S)]
-LAST_UNITS = [1536, 768, 512, 256]
-LATE = S - 256
-LATE_EXPERT = 9
-HELD_UNITS = 3
-VECTOR_EMPTIES = 128
+FIRST_CUTS = [(0, 160), (160, 416), (416, 864), (864, 1664), (1664, S)]
+UNIT_EXPERTS = [6, 3, 2, 1]
+LATE_SLOT = S - C
+LATE_EXPERT = E - 3
+HALF = C // 2
 EARLY_TOKENS = 640
 LAST_TOKENS = 128
 
@@ -57,6 +56,11 @@ def side_by_side(column, loads):
     return [column + i * LOAD for i in range(loads)]
 
 
+def cut(staged, width):
+    grouped, s0, n = staged
+    return [(grouped[:, PACK * a:PACK * (a + width)], s0 + a, width) for a in range(0, n, width)]
+
+
 def tile_moe_pre_lin_none_kernel(tc, xT, w, gate, offs, pos1, pos2, pos3, out):
     nc = tc.nc
     with ExitStack() as ctx:
@@ -69,23 +73,24 @@ def tile_moe_pre_lin_none_kernel(tc, xT, w, gate, offs, pos1, pos2, pos3, out):
         nc.sync.dma_start(offsets[:], offs)
         gates = keep.tile([P, S], F32, name="gates")
         picked = keep.tile([P, PLACES * S], F32, name="picked", align_bytes=64)
-        x_codes = [keep.tile([P, LATE if g < 2 else S], U32, name=f"x_codes{g}", align_bytes=64) for g in range(PASSES)]
-        late_codes = []
-        late_x0 = keep.tile([P, PACK * (S - LATE)], BF16, name="late_x0", align_bytes=64)
+        x_codes = [
+            keep.tile([P, S if g == PASSES - 1 else LATE_SLOT], U32, name=f"x_codes{g}", align_bytes=64)
+            for g in range(PASSES)
+        ]
+        late_x0 = keep.tile([P, PACK * C], BF16, name="late_x0", align_bytes=64)
         late_w = keep.tile([P, (E - LATE_EXPERT) * PASSES * BLOCK], BF16, name="late_w", align_bytes=64)
         x_scales = [keep.tile([P, S], U8, name=f"x_scales{g}", align_bytes=64) for g in range(PASSES)]
         w_codes = keep.tile([P, LATE_EXPERT * PASSES * N], U32, name="w_codes", align_bytes=64)
         w_scales = keep.tile([P, W_BLOCKS * N], U8, name="w_scales", align_bytes=64)
         w_blocks = w.rearrange("e (g p j) n -> p (e g) (j n)", p=P, j=PACK)
 
-        def load_window(g, j, narrow=False):
-            if narrow:
-                window = keep.tile([P, LAST_UNITS[0] + 8], F32, name=f"narrow{j}")
-            else:
-                window = window_pool.tile([P, WINDOW], F32, name="window")
+        def load_plane(window, g, j):
             rows = xT[g * K_PASS:(g + 1) * K_PASS, :].rearrange("(p j) t -> p j t", j=PACK)
             nc.sync.dma_start(window[:, 0:T], rows[:, j, :])
             return window
+
+        def load_window(g, j):
+            return load_plane(window_pool.tile([P, S + SPARE], F32, name="window"), g, j)
 
         def gather(window, plane, s0, n):
             nc.vector.tensor_tensor(
@@ -98,31 +103,30 @@ def tile_moe_pre_lin_none_kernel(tc, xT, w, gate, offs, pos1, pos2, pos3, out):
                 planes.rearrange("p j (c i) -> p c j i", i=2),
             )
 
-        def interleave_slots(planes, s0, n):
+        def interleave_slots(planes, slots):
             staged = []
-            for a in range(0, n, PIECE):
-                size = min(PIECE, n - a)
+            for a in range(0, slots, PIECE):
+                size = min(PIECE, slots - a)
                 grouped = grouped_pool.tile([P, size * PACK], BF16, name="grouped", align_bytes=64)
                 round_and_interleave(grouped[:], planes[:, :, a:a + size])
-                staged.append((grouped, s0 + a, size))
+                staged.append((grouped, a, size))
             return staged
 
         def x_words(g, start, stop):
-            if g < 2 and start >= LATE:
-                first = g * (S - LATE) - LATE
-                return late_codes[0][:, first + start:first + stop]
+            if g < PASSES - 1 and start >= LATE_SLOT:
+                return late_codes[:, g * C + start - LATE_SLOT:g * C + stop - LATE_SLOT]
             return x_codes[g][:, start:stop]
 
         def w_words(start, stop):
-            first = LATE_EXPERT * PASSES * N
-            if start >= first:
-                return late_codes[0][:, 2 * (S - LATE) + start - first:2 * (S - LATE) + stop - first]
+            first_late = LATE_EXPERT * PASSES * N
+            if start >= first_late:
+                return late_codes[:, 2 * C + start - first_late:2 * C + stop - first_late]
             return w_codes[:, start:stop]
 
-        def quantize(grouped, codes, scales, start, size):
+        def quantize(grouped, words, scales, start, size):
             for a, width in quantize_widths(size):
                 nc.vector.quantize_mx(
-                    out=codes(start + a, start + a + width).bitcast(FP8X4),
+                    out=words(start + a, start + a + width).bitcast(FP8X4),
                     scales=scales[:, start + a:start + a + width],
                     in_=grouped[:, PACK * a:PACK * (a + width)],
                 )
@@ -131,47 +135,46 @@ def tile_moe_pre_lin_none_kernel(tc, xT, w, gate, offs, pos1, pos2, pos3, out):
             for grouped, start, size in staged:
                 quantize(grouped, lambda a, b: x_words(g, a, b), x_scales[g], start, size)
 
-        def stage_weights(grouped, b0, first_load, columns):
-            for load, column in enumerate(columns, first_load):
-                first = load * W_LOAD
-                raw = picked[:, column:column + LOAD].rearrange("p (b c) -> p b c", b=W_LOAD)
-                nc.sync.dma_start(raw, w_blocks[:, b0 + first:b0 + first + W_LOAD, :])
-                for b in range(W_LOAD):
-                    cols = slice((first + b) * BLOCK, (first + b + 1) * BLOCK)
-                    round_and_interleave(grouped[:, cols], raw[:, b, :].rearrange("p (j n) -> p j n", j=PACK))
+        def quantize_blocks(grouped, b0, blocks):
+            quantize(grouped, w_words, w_scales, b0 * N, blocks * N)
 
-        def quantize_weights(b0, columns, plane=None):
-            half = len(columns) // 2
+        def stage_blocks(grouped, column, b0, blocks):
+            raw = picked[:, column:column + blocks * BLOCK].rearrange("p (b c) -> p b c", b=blocks)
+            nc.sync.dma_start(raw, w_blocks[:, b0:b0 + blocks, :])
+            for b in range(blocks):
+                block = raw[:, b, :].rearrange("p (j n) -> p j n", j=PACK)
+                round_and_interleave(grouped[:, b * BLOCK:(b + 1) * BLOCK], block)
+
+        def quantize_batch(b0, columns, plane=None):
             grouped = grouped_pool.tile([P, len(columns) * LOAD], BF16, name="grouped", align_bytes=64)
-            stage_weights(grouped, b0, 0, columns[:half])
-            window = load_window(0, plane) if plane is not None else None
-            stage_weights(grouped, b0, half, columns[half:])
-            quantize(grouped, w_words, w_scales, b0 * N, len(columns) * W_LOAD * N)
+            window = None
+            for i, column in enumerate(columns):
+                if plane is not None and i == len(columns) // 2:
+                    window = load_window(0, plane)
+                stage_blocks(grouped[:, i * LOAD:(i + 1) * LOAD], column, b0 + i * W_LOAD, W_LOAD)
+            quantize_blocks(grouped, b0, len(columns) * W_LOAD)
             return window
 
-        def multiply(staged):
-            for grouped, s0, n in staged:
-                start = s0
-                while start < s0 + n:
-                    e = start // C
-                    stop = start + (C // 2 if e == E - 1 else C)
-                    acc = psum.tile([P, stop - start], F32, name="acc")
-                    for g in range(PASSES):
-                        cols = slice((e * PASSES + g) * N, (e * PASSES + g + 1) * N)
-                        nc.tensor.matmul_mx(
-                            out=acc[:],
-                            lhsT=w_words(cols.start, cols.stop).bitcast(FP8X4),
-                            lhsT_scale=w_scales[:, cols],
-                            rhs=x_words(g, start, stop).bitcast(FP8X4),
-                            rhs_scale=x_scales[g][:, start:stop],
-                            start=(g == 0),
-                            stop=(g == PASSES - 1),
-                        )
-                    if start == LATE:
-                        nc.vector.tensor_copy(y[:, start:stop], acc[:])
-                    else:
-                        nc.scalar.copy(y[:, start:stop], acc[:])
-                    start = stop
+        def multiply(s0, n):
+            width = HALF if s0 == LATE_SLOT else C
+            for start in range(s0, s0 + n, width):
+                stop = start + width
+                acc = psum.tile([P, width], F32, name="acc")
+                for g in range(PASSES):
+                    first = (start // C * PASSES + g) * N
+                    nc.tensor.matmul_mx(
+                        out=acc[:],
+                        lhsT=w_words(first, first + N).bitcast(FP8X4),
+                        lhsT_scale=w_scales[:, first:first + N],
+                        rhs=x_words(g, start, stop).bitcast(FP8X4),
+                        rhs_scale=x_scales[g][:, start:stop],
+                        start=(g == 0),
+                        stop=(g == PASSES - 1),
+                    )
+                if start == LATE_SLOT:
+                    nc.vector.tensor_copy(y[:, start:stop], acc[:])
+                else:
+                    nc.scalar.copy(y[:, start:stop], acc[:])
 
         planes = picked[:, 0:PACK * S].rearrange("p (j s) -> p j s", j=PACK)
         window = load_window(0, 0)
@@ -181,16 +184,16 @@ def tile_moe_pre_lin_none_kernel(tc, xT, w, gate, offs, pos1, pos2, pos3, out):
         gather(load_window(0, 1), planes[:, 1, :], 0, S)
         landings = [side_by_side((i + 2) * S, 3) + side_by_side((PLACES - 1) * S + i * LOAD, 1) for i in range(3)]
         batch = len(landings[0]) * W_LOAD
-        quantize_weights(0, landings[0])
-        gather(quantize_weights(batch, landings[1], plane=2), planes[:, 2, :], 0, S)
-        gather(quantize_weights(2 * batch, landings[2], plane=3), planes[:, 3, :], 0, S)
+        quantize_batch(0, landings[0])
+        gather(quantize_batch(batch, landings[1], plane=2), planes[:, 2, :], 0, S)
+        gather(quantize_batch(2 * batch, landings[2], plane=3), planes[:, 3, :], 0, S)
         lists = []
         for r, pos in enumerate((pos1, pos2, pos3)):
             tile = keep.tile([P, T // LIST], U16, name=f"pos{r}")
             nc.sync.dma_start(tile[:], pos)
             lists.append(tile)
-        staged = interleave_slots(planes, 0, LATE)
-        round_and_interleave(late_x0[:], planes[:, :, LATE:S])
+        staged = interleave_slots(planes, LATE_SLOT)
+        round_and_interleave(late_x0[:], planes[:, :, LATE_SLOT:S])
 
         planes = picked[:, 2 * S:PLACES * S].rearrange("p (j s) -> p j s", j=PACK)
         for j in (2, 3):
@@ -198,69 +201,64 @@ def tile_moe_pre_lin_none_kernel(tc, xT, w, gate, offs, pos1, pos2, pos3, out):
         quantize_slots(0, staged)
         for j in (0, 1):
             gather(load_window(1, j), planes[:, j, :], 0, S)
-        early_w = grouped_pool.tile([P, PASSES * BLOCK], BF16, name="grouped", align_bytes=64)
-        for e in range(LATE_EXPERT - 1, E):
-            column = (e - LATE_EXPERT + 1) * PASSES * BLOCK
-            raw = picked[:, column:column + PASSES * BLOCK].rearrange("p (b c) -> p b c", b=PASSES)
-            nc.sync.dma_start(raw, w_blocks[:, e * PASSES:(e + 1) * PASSES, :])
-            for g in range(PASSES):
-                first = ((e - LATE_EXPERT) * PASSES + g) * BLOCK
-                target = early_w[:, g * BLOCK:(g + 1) * BLOCK] if e < LATE_EXPERT else late_w[:, first:first + BLOCK]
-                round_and_interleave(target, raw[:, g, :].rearrange("p (j n) -> p j n", j=PACK))
-        quantize(early_w, w_words, w_scales, 3 * batch * N, PASSES * N)
-        staged1 = interleave_slots(planes, 0, S)
-        last, start, size = staged1[-1]
-        late_x1 = last[:, PACK * (LATE - start):PACK * size]
-        staged1[-1] = (last, start, LATE - start)
+        expert = PASSES * BLOCK
+        early_w = grouped_pool.tile([P, expert], BF16, name="grouped", align_bytes=64)
+        stage_blocks(early_w, 0, (LATE_EXPERT - 1) * PASSES, PASSES)
+        for i in range(E - LATE_EXPERT):
+            stage_blocks(late_w[:, i * expert:(i + 1) * expert], (i + 1) * expert, (LATE_EXPERT + i) * PASSES, PASSES)
+        quantize_blocks(early_w, (LATE_EXPERT - 1) * PASSES, PASSES)
+        staged = interleave_slots(planes, S)
+        last, start, size = staged[-1]
+        late_x1 = last[:, PACK * (size - C):PACK * size]
+        staged[-1] = (last, start, size - C)
 
-        windows = [load_window(2, j, narrow=j >= 2) for j in range(PACK)]
+        sizes = [experts * C for experts in UNIT_EXPERTS]
+        starts = [sum(sizes[:u]) for u in range(len(sizes))]
+        windows = [load_window(2, j) for j in (0, 1)]
+        for j in (2, 3):
+            windows.append(load_plane(keep.tile([P, sizes[0] + SPARE], F32, name=f"narrow{j}"), 2, j))
         y = window_pool.tile([P, S], F32, name="window")
 
-        def gather_unit(base, s0, n):
-            planes = picked[:, base:base + PACK * n].rearrange("p (j s) -> p j s", j=PACK)
+        def gather_unit(u):
+            base = u % 2 * 2 * S
+            unit = picked[:, base:base + PACK * sizes[u]].rearrange("p (j s) -> p j s", j=PACK)
             for j in range(PACK):
-                gather(windows[j], planes[:, j, :], s0, n)
-            return planes
+                gather(windows[j], unit[:, j, :], starts[u], sizes[u])
+            return unit
 
-        def inside(column, n):
-            return picked[:, column:column + 2 * n].bitcast(BF16)
+        def interleave_unit(u, unit, grouped, a, n):
+            round_and_interleave(grouped, unit[:, :, a:a + n])
+            return (grouped, starts[u] + a, n)
 
-        def interleave_parts(planes, s0, parts):
-            staged = []
-            a = 0
-            for grouped, n in parts:
-                round_and_interleave(grouped, planes[:, :, a:a + n])
-                staged.append((grouped, s0 + a, n))
-                a += n
-            return staged
+        def in_picked(column, slots):
+            return picked[:, column:column + 2 * slots].bitcast(BF16)
 
-        held = keep.tile([P, PACK * 768], BF16, name="held", tag="held", align_bytes=64)
-        planes = gather_unit(0, 0, 1536)
-        quantize_slots(1, staged1)
-        staged_a = interleave_parts(planes, 0, [(inside(4 * S, 1024), 1024), (inside(4 * S + 2048, 512), 512)])
-        planes = gather_unit(2 * S, 1536, 768)
-        staged_b = interleave_parts(planes, 1536, [(held[:], 768)])
-        quantize_slots(2, staged_a)
-        multiply(staged_a)
-        planes = gather_unit(0, 2304, 512)
-        staged_c = interleave_parts(planes, 2304, [(inside(5 * S, 512), 512)])
-        quantize_slots(2, staged_b)
-        multiply(staged_b)
-        planes = gather_unit(2 * S, LATE, 256)
-        staged_d = interleave_parts(planes, LATE, [(inside(5 * S + 1024, 256), 256)])
-        blocks = (E - LATE_EXPERT) * PASSES
-        late_codes.append(keep.tile([P, 2 * (S - LATE) + blocks * N], U32, name="late", tag="held", align_bytes=64))
-        for first, count in ((0, 2), (2, 4)):
-            quantize(late_w[:, first * BLOCK:(first + count) * BLOCK], w_words, w_scales, (LATE_EXPERT * PASSES + first) * N, count * N)
-        quantize_slots(0, [(late_x0, LATE, S - LATE)])
-        quantize_slots(1, [(late_x1, LATE, S - LATE)])
-        quantize(late_w[:, 6 * BLOCK:9 * BLOCK], w_words, w_scales, (LATE_EXPERT * PASSES + 6) * N, 3 * N)
-        grouped = staged_c[0][0]
-        quantize_slots(2, [(grouped[:, 0:PACK * C], 2304, C), (grouped[:, PACK * C:PACK * 2 * C], 2304 + C, C)])
-        multiply(staged_c)
-        grouped = staged_d[0][0]
-        quantize_slots(2, [(grouped[:, 0:PACK * 128], LATE, 128), (grouped[:, PACK * 128:PACK * 256], LATE + 128, 128)])
-        multiply(staged_d)
+        handed_on = keep.tile([P, PACK * sizes[1]], BF16, name="handed_on", tag="handed_on", align_bytes=64)
+        unit = gather_unit(0)
+        quantize_slots(1, staged)
+        first_unit = [
+            interleave_unit(0, unit, in_picked(4 * S + 2 * a, n), a, n) for a, n in quantize_widths(sizes[0])
+        ]
+        second_unit = interleave_unit(1, gather_unit(1), handed_on[:], 0, sizes[1])
+        quantize_slots(2, first_unit)
+        multiply(starts[0], sizes[0])
+        third_unit = interleave_unit(2, gather_unit(2), in_picked(5 * S, sizes[2]), 0, sizes[2])
+        quantize_slots(2, [second_unit])
+        multiply(starts[1], sizes[1])
+        last_unit = interleave_unit(3, gather_unit(3), in_picked(5 * S + 2 * sizes[2], sizes[3]), 0, sizes[3])
+
+        late_blocks = (E - LATE_EXPERT) * PASSES
+        late_codes = keep.tile([P, 2 * C + late_blocks * N], U32, name="late", tag="handed_on", align_bytes=64)
+        third_blocks = UNIT_EXPERTS[2] * PASSES
+        for first, stop in ((0, 2), (2, third_blocks)):
+            quantize_blocks(late_w[:, first * BLOCK:stop * BLOCK], LATE_EXPERT * PASSES + first, stop - first)
+        quantize_slots(0, [(late_x0, LATE_SLOT, C)])
+        quantize_slots(1, [(late_x1, LATE_SLOT, C)])
+        quantize_blocks(late_w[:, third_blocks * BLOCK:late_blocks * BLOCK], (E - 1) * PASSES, PASSES)
+        quantize_slots(2, cut(third_unit, C))
+        multiply(starts[2], sizes[2])
+        quantize_slots(2, cut(last_unit, HALF))
+        multiply(starts[3], sizes[3])
 
         sums = picked[:, 0:3 * T].rearrange("p (r t) -> p r t", r=3)
 

@@ -13,6 +13,7 @@ U8 = mybir.dt.uint8
 FP8X4 = mybir.dt.float8_e4m3fn_x4
 MULT = mybir.AluOpType.mult
 ADD = mybir.AluOpType.add
+COPY = mybir.ActivationFunctionType.Copy
 
 P = 128
 PACK = 4
@@ -24,252 +25,243 @@ FLOPS = 2 * K * S * N
 BYTES = 4 * (K * T + E * K * N + S + N * T) + 2 * (S + 3 * T)
 
 SPARE = 8
-PLACES = 6
+UNIT = 512
+HEAD_SLOTS = 1024
+HEAD_CUTS = [(0, 256), (256, 576), (576, HEAD_SLOTS)]
+VECTOR_SLOTS = 1280
+RING = 5
 W_BLOCKS = E * PASSES
 BLOCK = PACK * N
-W_LOAD = 2
-LOAD = W_LOAD * BLOCK
-PIECE = 1024
-FIRST_CUTS = [(0, 160), (160, 416), (416, 864), (864, 1664), (1664, S)]
-UNIT_EXPERTS = [6, 3, 2, 1]
-LATE_SLOT = S - C
-LATE_EXPERT = E - 3
+W_LOAD = 4
+W_RING = 3
 HALF = C // 2
-EARLY_TOKENS = 640
-LAST_TOKENS = 128
+BANKS = [(a, a + UNIT) for a in range(0, S - UNIT, UNIT)] + [(S - UNIT, S - C), (S - C, S - HALF), (S - HALF, S)]
+TOKEN_CUTS = [0, 192, 608, 896, T]
 
 
-def quantize_widths(width):
-    parts = []
-    start = 0
-    size = PIECE
-    while start < width:
-        if width - start >= size:
-            parts.append((start, size))
-            start += size
-        else:
-            size //= 2
-    return parts
-
-
-def side_by_side(column, loads):
-    return [column + i * LOAD for i in range(loads)]
-
-
-def cut(staged, width):
-    grouped, s0, n = staged
-    return [(grouped[:, PACK * a:PACK * (a + width)], s0 + a, width) for a in range(0, n, width)]
+def scalar_units():
+    first = VECTOR_SLOTS + (S - VECTOR_SLOTS) % UNIT
+    units = [(0, VECTOR_SLOTS, first - VECTOR_SLOTS)] if first > VECTOR_SLOTS else []
+    units = units + [(0, a, UNIT) for a in range(first, S, UNIT)]
+    units = units + [(1, a, UNIT) for a in range(0, S, UNIT)]
+    return units + [(2, a, b - a) for a, b in BANKS]
 
 
 def tile_moe_pre_lin_none_kernel(tc, xT, w, gate, offs, pos1, pos2, pos3, out):
     nc = tc.nc
     with ExitStack() as ctx:
         keep = ctx.enter_context(tc.tile_pool(name="keep", bufs=1))
-        grouped_pool = ctx.enter_context(tc.tile_pool(name="grouped", bufs=S // PIECE))
-        window_pool = ctx.enter_context(tc.tile_pool(name="windows", bufs=3))
-        psum = ctx.enter_context(tc.psum_pool(name="psum", bufs=8))
+        picked_pool = ctx.enter_context(tc.tile_pool(name="picked", bufs=RING))
+        grouped_pool = ctx.enter_context(tc.tile_pool(name="grouped", bufs=4))
+        raw_pool = ctx.enter_context(tc.tile_pool(name="raw", bufs=W_RING))
+        psum = ctx.enter_context(tc.psum_pool(name="psum", bufs=1))
 
         offsets = keep.tile([P, S // LIST], U16, name="offsets")
         nc.sync.dma_start(offsets[:], offs)
         gates = keep.tile([P, S], F32, name="gates")
-        picked = keep.tile([P, PLACES * S], F32, name="picked", align_bytes=64)
-        x_codes = [
-            keep.tile([P, S if g == PASSES - 1 else LATE_SLOT], U32, name=f"x_codes{g}", align_bytes=64)
-            for g in range(PASSES)
-        ]
-        late_x0 = keep.tile([P, PACK * C], BF16, name="late_x0", align_bytes=64)
-        late_w = keep.tile([P, (E - LATE_EXPERT) * PASSES * BLOCK], BF16, name="late_w", align_bytes=64)
+        x_codes = [keep.tile([P, S], U32, name=f"x_codes{g}", align_bytes=64) for g in range(PASSES)]
         x_scales = [keep.tile([P, S], U8, name=f"x_scales{g}", align_bytes=64) for g in range(PASSES)]
-        w_codes = keep.tile([P, LATE_EXPERT * PASSES * N], U32, name="w_codes", align_bytes=64)
+        w_codes = keep.tile([P, W_BLOCKS * N], U32, name="w_codes", align_bytes=64)
         w_scales = keep.tile([P, W_BLOCKS * N], U8, name="w_scales", align_bytes=64)
         w_blocks = w.rearrange("e (g p j) n -> p (e g) (j n)", p=P, j=PACK)
+        accs = [psum.tile([P, b - a], F32, name=f"acc{i}") for i, (a, b) in enumerate(BANKS)]
 
-        def load_plane(window, g, j):
-            rows = xT[g * K_PASS:(g + 1) * K_PASS, :].rearrange("(p j) t -> p j t", j=PACK)
-            nc.sync.dma_start(window[:, 0:T], rows[:, j, :])
-            return window
+        windows = {}
 
         def load_window(g, j):
-            return load_plane(window_pool.tile([P, S + SPARE], F32, name="window"), g, j)
+            window = keep.tile([P, T + SPARE], F32, name=f"window{g}{j}")
+            rows = xT[g * K_PASS:(g + 1) * K_PASS, :].rearrange("(p j) t -> p j t", j=PACK)
+            nc.sync.dma_start(window[:, 0:T], rows[:, j, :])
+            windows[(g, j)] = window
 
-        def gather(window, plane, s0, n):
-            nc.vector.tensor_tensor(
-                plane, window[:].indirect(offsets[:, s0 // LIST:(s0 + n) // LIST]), gates[:, s0:s0 + n], MULT
-            )
+        def tokens(g, j, s0, n):
+            return windows[(g, j)][:].indirect(offsets[:, s0 // LIST:(s0 + n) // LIST])
 
-        def round_and_interleave(grouped, planes):
-            nc.scalar.copy(
-                grouped.rearrange("p (c i j) -> p c j i", i=2, j=PACK),
-                planes.rearrange("p j (c i) -> p c j i", i=2),
-            )
+        raws = []
 
-        def interleave_slots(planes, slots):
-            staged = []
-            for a in range(0, slots, PIECE):
-                size = min(PIECE, slots - a)
-                grouped = grouped_pool.tile([P, size * PACK], BF16, name="grouped", align_bytes=64)
-                round_and_interleave(grouped[:], planes[:, :, a:a + size])
-                staged.append((grouped, a, size))
-            return staged
+        def load_weights():
+            b0 = len(raws) * W_LOAD
+            raw = raw_pool.tile([P, W_LOAD, BLOCK], F32, name="raw")
+            nc.sync.dma_start(raw[:], w_blocks[:, b0:b0 + W_LOAD, :])
+            raws.append(raw)
 
-        def x_words(g, start, stop):
-            if g < PASSES - 1 and start >= LATE_SLOT:
-                return late_codes[:, g * C + start - LATE_SLOT:g * C + stop - LATE_SLOT]
-            return x_codes[g][:, start:stop]
+        def pairs_out(grouped):
+            return grouped.rearrange("p (c i j) -> p c j i", i=2, j=PACK)
 
-        def w_words(start, stop):
-            first_late = LATE_EXPERT * PASSES * N
-            if start >= first_late:
-                return late_codes[:, 2 * C + start - first_late:2 * C + stop - first_late]
-            return w_codes[:, start:stop]
+        def pairs_in(planes):
+            return planes.rearrange("p j (c i) -> p c j i", i=2)
 
-        def quantize(grouped, words, scales, start, size):
-            for a, width in quantize_widths(size):
-                nc.vector.quantize_mx(
-                    out=words(start + a, start + a + width).bitcast(FP8X4),
-                    scales=scales[:, start + a:start + a + width],
-                    in_=grouped[:, PACK * a:PACK * (a + width)],
+        def new_grouped(columns):
+            return grouped_pool.tile([P, columns * PACK], BF16, name="grouped", align_bytes=64)
+
+        slots_done = [set() for g in range(PASSES)]
+        blocks_done = set()
+        issued = set()
+        products = [
+            (i, g, s0, min(C, b - a)) for g in range(PASSES) for i, (a, b) in enumerate(BANKS) for s0 in range(a, b, C)
+        ]
+
+        def multiply():
+            for i, g, s0, n in products:
+                block = s0 // C * PASSES + g
+                ready = block in blocks_done and all(s in slots_done[g] for s in range(s0, s0 + n, HALF))
+                if (g, s0) in issued or not ready:
+                    continue
+                a, b = BANKS[i]
+                before = len([1 for gg, ss in issued if a <= ss < b])
+                total = len([1 for ii, gg, ss, nn in products if ii == i])
+                issued.add((g, s0))
+                nc.tensor.matmul_mx(
+                    out=accs[i][:, s0 - a:s0 - a + n],
+                    lhsT=w_codes[:, block * N:(block + 1) * N].bitcast(FP8X4),
+                    lhsT_scale=w_scales[:, block * N:(block + 1) * N],
+                    rhs=x_codes[g][:, s0:s0 + n].bitcast(FP8X4),
+                    rhs_scale=x_scales[g][:, s0:s0 + n],
+                    start=(before == 0),
+                    stop=(before == total - 1),
                 )
+                if before == total - 1:
+                    if i == len(BANKS) - 2:
+                        nc.vector.tensor_copy(y[:, a:b], accs[i][:])
+                    else:
+                        nc.scalar.copy(y[:, a:b], accs[i][:])
 
-        def quantize_slots(g, staged):
-            for grouped, start, size in staged:
-                quantize(grouped, lambda a, b: x_words(g, a, b), x_scales[g], start, size)
+        def quantize_slots(grouped, g, s0, n):
+            nc.vector.quantize_mx(
+                out=x_codes[g][:, s0:s0 + n].bitcast(FP8X4), scales=x_scales[g][:, s0:s0 + n], in_=grouped[:]
+            )
+            for s in range(s0, s0 + n, HALF):
+                slots_done[g].add(s)
+            multiply()
 
-        def quantize_blocks(grouped, b0, blocks):
-            quantize(grouped, w_words, w_scales, b0 * N, blocks * N)
+        def quantize_weights(grouped, b0):
+            columns = slice(b0 * N, (b0 + W_LOAD) * N)
+            nc.vector.quantize_mx(
+                out=w_codes[:, columns].bitcast(FP8X4), scales=w_scales[:, columns], in_=grouped[:]
+            )
+            for b in range(b0, b0 + W_LOAD):
+                blocks_done.add(b)
+            multiply()
 
-        def stage_blocks(grouped, column, b0, blocks):
-            raw = picked[:, column:column + blocks * BLOCK].rearrange("p (b c) -> p b c", b=blocks)
-            nc.sync.dma_start(raw, w_blocks[:, b0:b0 + blocks, :])
-            for b in range(blocks):
-                block = raw[:, b, :].rearrange("p (j n) -> p j n", j=PACK)
-                round_and_interleave(grouped[:, b * BLOCK:(b + 1) * BLOCK], block)
+        def vector_gather(plane, j, s0, n):
+            nc.vector.tensor_tensor(plane, tokens(0, j, s0, n), gates[:, s0:s0 + n], MULT)
 
-        def quantize_batch(b0, columns, plane=None):
-            grouped = grouped_pool.tile([P, len(columns) * LOAD], BF16, name="grouped", align_bytes=64)
-            window = None
-            for i, column in enumerate(columns):
-                if plane is not None and i == len(columns) // 2:
-                    window = load_window(0, plane)
-                stage_blocks(grouped[:, i * LOAD:(i + 1) * LOAD], column, b0 + i * W_LOAD, W_LOAD)
-            quantize_blocks(grouped, b0, len(columns) * W_LOAD)
-            return window
+        def interleave_slots(planes, s0, n):
+            grouped = new_grouped(n)
+            nc.vector.tensor_copy(pairs_out(grouped[:]), pairs_in(planes))
+            return lambda: quantize_slots(grouped, 0, s0, n)
 
-        def multiply(s0, n):
-            width = HALF if s0 == LATE_SLOT else C
-            for start in range(s0, s0 + n, width):
-                stop = start + width
-                acc = psum.tile([P, width], F32, name="acc")
-                for g in range(PASSES):
-                    first = (start // C * PASSES + g) * N
-                    nc.tensor.matmul_mx(
-                        out=acc[:],
-                        lhsT=w_words(first, first + N).bitcast(FP8X4),
-                        lhsT_scale=w_scales[:, first:first + N],
-                        rhs=x_words(g, start, stop).bitcast(FP8X4),
-                        rhs_scale=x_scales[g][:, start:stop],
-                        start=(g == 0),
-                        stop=(g == PASSES - 1),
-                    )
-                if start == LATE_SLOT:
-                    nc.vector.tensor_copy(y[:, start:stop], acc[:])
-                else:
-                    nc.scalar.copy(y[:, start:stop], acc[:])
+        def interleave_weights(k):
+            grouped = new_grouped(W_LOAD * N)
+            nc.vector.tensor_copy(
+                grouped[:].rearrange("p (b c i j) -> p b c j i", b=W_LOAD, i=2, j=PACK),
+                raws[k][:].rearrange("p b (j c i) -> p b c j i", j=PACK, i=2),
+            )
+            if len(raws) < W_BLOCKS // W_LOAD:
+                load_weights()
+            return lambda: quantize_weights(grouped, k * W_LOAD)
 
-        planes = picked[:, 0:PACK * S].rearrange("p (j s) -> p j s", j=PACK)
-        window = load_window(0, 0)
-        for a, b in FIRST_CUTS:
+        def scalar_unit(g, s0, n):
+            picked = picked_pool.tile([P, PACK, n], F32, name="picked")
+            for j in range(PACK):
+                nc.scalar.activation(picked[:, j, :], tokens(g, j, s0, n), COPY)
+            grouped = new_grouped(n)
+            gate_pairs = gates[:, s0:s0 + n].rearrange("p (c o i) -> p c o i", o=1, i=2)
+            nc.vector.tensor_tensor(
+                pairs_out(grouped[:]), pairs_in(picked[:]), gate_pairs.broadcast_to([P, n // 2, PACK, 2]), MULT
+            )
+            return lambda: quantize_slots(grouped, g, s0, n)
+
+        head = keep.tile([P, PACK, HEAD_SLOTS], F32, name="head", tag="head")
+        load_window(0, 0)
+        for a, b in HEAD_CUTS:
             nc.sync.dma_start(gates[:, a:b], gate[0:P, a:b])
-            gather(window, planes[:, 0, a:b], a, b - a)
-        gather(load_window(0, 1), planes[:, 1, :], 0, S)
-        landings = [side_by_side((i + 2) * S, 3) + side_by_side((PLACES - 1) * S + i * LOAD, 1) for i in range(3)]
-        batch = len(landings[0]) * W_LOAD
-        quantize_batch(0, landings[0])
-        gather(quantize_batch(batch, landings[1], plane=2), planes[:, 2, :], 0, S)
-        gather(quantize_batch(2 * batch, landings[2], plane=3), planes[:, 3, :], 0, S)
+            vector_gather(head[:, 0, a:b], 0, a, b - a)
+        for j in range(1, PACK):
+            load_window(0, j)
+            vector_gather(head[:, j, :], j, 0, HEAD_SLOTS)
+        nc.sync.dma_start(gates[:, HEAD_SLOTS:S], gate[0:P, HEAD_SLOTS:S])
+        load_window(1, 0)
+        load_window(1, 1)
+        load_weights()
+        load_window(1, 2)
+        load_window(1, 3)
+        for k in range(1, W_RING):
+            load_weights()
+        for j in range(PACK):
+            load_window(2, j)
         lists = []
         for r, pos in enumerate((pos1, pos2, pos3)):
             tile = keep.tile([P, T // LIST], U16, name=f"pos{r}")
             nc.sync.dma_start(tile[:], pos)
             lists.append(tile)
-        staged = interleave_slots(planes, LATE_SLOT)
-        round_and_interleave(late_x0[:], planes[:, :, LATE_SLOT:S])
 
-        planes = picked[:, 2 * S:PLACES * S].rearrange("p (j s) -> p j s", j=PACK)
-        for j in (2, 3):
-            gather(load_window(1, j), planes[:, j, :], 0, S)
-        quantize_slots(0, staged)
-        for j in (0, 1):
-            gather(load_window(1, j), planes[:, j, :], 0, S)
-        expert = PASSES * BLOCK
-        early_w = grouped_pool.tile([P, expert], BF16, name="grouped", align_bytes=64)
-        stage_blocks(early_w, 0, (LATE_EXPERT - 1) * PASSES, PASSES)
-        for i in range(E - LATE_EXPERT):
-            stage_blocks(late_w[:, i * expert:(i + 1) * expert], (i + 1) * expert, (LATE_EXPERT + i) * PASSES, PASSES)
-        quantize_blocks(early_w, (LATE_EXPERT - 1) * PASSES, PASSES)
-        staged = interleave_slots(planes, S)
-        last, start, size = staged[-1]
-        late_x1 = last[:, PACK * (size - C):PACK * size]
-        staged[-1] = (last, start, size - C)
+        first_half = interleave_slots(head[:, :, 0:UNIT], 0, UNIT)
+        waiting = interleave_slots(head[:, :, UNIT:HEAD_SLOTS], UNIT, UNIT)
+        first_half()
+        y = keep.tile([P, S], F32, name="y", tag="head")
 
-        sizes = [experts * C for experts in UNIT_EXPERTS]
-        starts = [sum(sizes[:u]) for u in range(len(sizes))]
-        windows = [load_window(2, j) for j in (0, 1)]
-        for j in (2, 3):
-            windows.append(load_plane(keep.tile([P, sizes[0] + SPARE], F32, name=f"narrow{j}"), 2, j))
-        y = window_pool.tile([P, S], F32, name="window")
+        extra = VECTOR_SLOTS - HEAD_SLOTS
+        second = keep.tile([P, PACK, extra], F32, name="second")
 
-        def gather_unit(u):
-            base = u % 2 * 2 * S
-            unit = picked[:, base:base + PACK * sizes[u]].rearrange("p (j s) -> p j s", j=PACK)
+        def gather_second():
             for j in range(PACK):
-                gather(windows[j], unit[:, j, :], starts[u], sizes[u])
-            return unit
+                vector_gather(second[:, j, :], j, HEAD_SLOTS, extra)
+            return None
 
-        def interleave_unit(u, unit, grouped, a, n):
-            round_and_interleave(grouped, unit[:, :, a:a + n])
-            return (grouped, starts[u] + a, n)
+        fillers = [gather_second, lambda: interleave_slots(second[:], HEAD_SLOTS, extra)]
+        fillers = fillers + [lambda k=k: interleave_weights(k) for k in range(W_BLOCKS // W_LOAD)]
+        for i, (g, s0, n) in enumerate(scalar_units()):
+            quantize_unit = scalar_unit(g, s0, n)
+            if waiting is not None:
+                waiting()
+            if i < len(fillers):
+                waiting = fillers[i]()
+                quantize_unit()
+            else:
+                waiting = quantize_unit
+        waiting()
 
-        def in_picked(column, slots):
-            return picked[:, column:column + 2 * slots].bitcast(BF16)
+        first = keep.tile([P, T], F32, name="first", tag="window00")
+        middle = keep.tile([P, T], F32, name="middle", tag="window01")
+        total = keep.tile([P, T], F32, name="total", tag="window02")
 
-        handed_on = keep.tile([P, PACK * sizes[1]], BF16, name="handed_on", tag="handed_on", align_bytes=64)
-        unit = gather_unit(0)
-        quantize_slots(1, staged)
-        first_unit = [
-            interleave_unit(0, unit, in_picked(4 * S + 2 * a, n), a, n) for a, n in quantize_widths(sizes[0])
-        ]
-        second_unit = interleave_unit(1, gather_unit(1), handed_on[:], 0, sizes[1])
-        quantize_slots(2, first_unit)
-        multiply(starts[0], sizes[0])
-        third_unit = interleave_unit(2, gather_unit(2), in_picked(5 * S, sizes[2]), 0, sizes[2])
-        quantize_slots(2, [second_unit])
-        multiply(starts[1], sizes[1])
-        last_unit = interleave_unit(3, gather_unit(3), in_picked(5 * S + 2 * sizes[2], sizes[3]), 0, sizes[3])
+        def fetch(r, a, b):
+            return y[:].indirect(lists[r][:, a // LIST:b // LIST])
 
-        late_blocks = (E - LATE_EXPERT) * PASSES
-        late_codes = keep.tile([P, 2 * C + late_blocks * N], U32, name="late", tag="handed_on", align_bytes=64)
-        third_blocks = UNIT_EXPERTS[2] * PASSES
-        for first, stop in ((0, 2), (2, third_blocks)):
-            quantize_blocks(late_w[:, first * BLOCK:stop * BLOCK], LATE_EXPERT * PASSES + first, stop - first)
-        quantize_slots(0, [(late_x0, LATE_SLOT, C)])
-        quantize_slots(1, [(late_x1, LATE_SLOT, C)])
-        quantize_blocks(late_w[:, third_blocks * BLOCK:late_blocks * BLOCK], (E - 1) * PASSES, PASSES)
-        quantize_slots(2, cut(third_unit, C))
-        multiply(starts[2], sizes[2])
-        quantize_slots(2, cut(last_unit, HALF))
-        multiply(starts[3], sizes[3])
+        runs = [(a, b) for a, b in zip(TOKEN_CUTS[:-1], TOKEN_CUTS[1:])]
+        own, shared = runs[0], runs[1:]
 
-        sums = picked[:, 0:3 * T].rearrange("p (r t) -> p r t", r=3)
+        def scalar_fetch(tile, r, run):
+            a, b = run
+            nc.scalar.activation(tile[:, a:b], fetch(r, a, b), COPY)
 
-        def fetch(r, start, stop):
-            return y[:].indirect(lists[r][:, start // LIST:stop // LIST])
+        def gather_add(tile, r, other, run):
+            a, b = run
+            nc.vector.tensor_tensor(tile[:, a:b], fetch(r, a, b), other[:, a:b], ADD)
 
-        runs = [(0, EARLY_TOKENS), (EARLY_TOKENS, T)]
-        for a, b in runs:
-            nc.vector.tensor_copy(sums[:, 0, a:b], fetch(0, a, b))
-        for a, b in runs:
-            nc.vector.tensor_tensor(sums[:, 1, a:b], fetch(1, a, b), sums[:, 0, a:b], ADD)
-        for a, b in [runs[0], (EARLY_TOKENS, T - LAST_TOKENS), (T - LAST_TOKENS, T)]:
-            nc.vector.tensor_tensor(sums[:, 2, a:b], fetch(2, a, b), sums[:, 1, a:b], ADD)
-            nc.sync.dma_start(out[:, a:b], sums[:, 2, a:b])
+        def store(run):
+            a, b = run
+            nc.sync.dma_start(out[:, a:b], total[:, a:b])
+
+        def finish(run):
+            a, b = run
+            nc.vector.tensor_tensor(total[:, a:b], total[:, a:b], middle[:, a:b], ADD)
+            store(run)
+
+        scalar_fetch(first, 0, shared[0])
+        scalar_fetch(first, 0, shared[1])
+        scalar_fetch(middle, 1, shared[0])
+        scalar_fetch(first, 0, shared[2])
+        scalar_fetch(middle, 1, shared[1])
+        scalar_fetch(middle, 1, shared[2])
+        nc.vector.tensor_copy(first[:, own[0]:own[1]], fetch(0, own[0], own[1]))
+        gather_add(middle, 1, first, own)
+        gather_add(total, 2, first, shared[0])
+        gather_add(total, 2, middle, own)
+        store(own)
+        gather_add(total, 2, first, shared[1])
+        finish(shared[0])
+        gather_add(total, 2, first, shared[2])
+        finish(shared[1])
+        finish(shared[2])

@@ -1,6 +1,7 @@
 from contextlib import ExitStack
 
 import concourse.mybir as mybir
+from concourse.masks import make_identity
 
 K, T, E, C, N = 1536, 1024, 12, 256, 128
 S = E * C
@@ -28,22 +29,25 @@ SPARE = 8
 UNIT = 512
 HEAD_SLOTS = 1024
 HEAD_CUTS = [(0, 256), (256, 576), (576, HEAD_SLOTS)]
-VECTOR_SLOTS = 1280
-RING = 5
+SECOND_SLOTS = 896
+SECOND_STEP = 2
+RING = 6
 W_BLOCKS = E * PASSES
 BLOCK = PACK * N
-W_LOAD = 4
 W_RING = 3
+BANK_COUNT = 8
+GATE_BANKS = 2
 HALF = C // 2
 BANKS = [(a, a + UNIT) for a in range(0, S - UNIT, UNIT)] + [(S - UNIT, S - C), (S - C, S - HALF), (S - HALF, S)]
 TOKEN_CUTS = [0, 192, 608, 896, T]
 
 
 def scalar_units():
-    first = VECTOR_SLOTS + (S - VECTOR_SLOTS) % UNIT
-    units = [(0, VECTOR_SLOTS, first - VECTOR_SLOTS)] if first > VECTOR_SLOTS else []
-    units = units + [(0, a, UNIT) for a in range(first, S, UNIT)]
-    units = units + [(1, a, UNIT) for a in range(0, S, UNIT)]
+    units = [(0, a, UNIT) for a in range(HEAD_SLOTS, S, UNIT)]
+    first = SECOND_SLOTS + (S - SECOND_SLOTS) % UNIT
+    if first > SECOND_SLOTS:
+        units = units + [(1, SECOND_SLOTS, first - SECOND_SLOTS)]
+    units = units + [(1, a, UNIT) for a in range(first, S, UNIT)]
     return units + [(2, a, b - a) for a, b in BANKS]
 
 
@@ -55,16 +59,20 @@ def tile_moe_pre_lin_none_kernel(tc, xT, w, gate, offs, pos1, pos2, pos3, out):
         grouped_pool = ctx.enter_context(tc.tile_pool(name="grouped", bufs=4))
         raw_pool = ctx.enter_context(tc.tile_pool(name="raw", bufs=W_RING))
         psum = ctx.enter_context(tc.psum_pool(name="psum", bufs=1))
+        gate_psum = ctx.enter_context(tc.psum_pool(name="gate_psum", bufs=GATE_BANKS))
 
         offsets = keep.tile([P, S // LIST], U16, name="offsets")
         nc.sync.dma_start(offsets[:], offs)
-        gates = keep.tile([P, S], F32, name="gates")
+        gates = keep.tile([P, HEAD_SLOTS], F32, name="gates")
         x_codes = [keep.tile([P, S], U32, name=f"x_codes{g}", align_bytes=64) for g in range(PASSES)]
         x_scales = [keep.tile([P, S], U8, name=f"x_scales{g}", align_bytes=64) for g in range(PASSES)]
         w_codes = keep.tile([P, W_BLOCKS * N], U32, name="w_codes", align_bytes=64)
         w_scales = keep.tile([P, W_BLOCKS * N], U8, name="w_scales", align_bytes=64)
-        w_blocks = w.rearrange("e (g p j) n -> p (e g) (j n)", p=P, j=PACK)
-        accs = [psum.tile([P, b - a], F32, name=f"acc{i}") for i, (a, b) in enumerate(BANKS)]
+        w_blocks = w.rearrange("e (g p j) n -> p e g (j n)", p=P, j=PACK)
+        sum_banks = BANK_COUNT - GATE_BANKS
+        accs = {i: psum.tile([P, b - a], F32, name=f"acc{i}") for i, (a, b) in enumerate(BANKS[:sum_banks])}
+        identity = keep.tile([P, P], F32, name="identity")
+        make_identity(nc, identity[:])
 
         windows = {}
 
@@ -80,9 +88,8 @@ def tile_moe_pre_lin_none_kernel(tc, xT, w, gate, offs, pos1, pos2, pos3, out):
         raws = []
 
         def load_weights():
-            b0 = len(raws) * W_LOAD
-            raw = raw_pool.tile([P, W_LOAD, BLOCK], F32, name="raw")
-            nc.sync.dma_start(raw[:], w_blocks[:, b0:b0 + W_LOAD, :])
+            raw = raw_pool.tile([P, PASSES, BLOCK], F32, name="raw")
+            nc.sync.dma_start(raw[:], w_blocks[:, len(raws), :, :])
             raws.append(raw)
 
         def pairs_out(grouped):
@@ -105,7 +112,7 @@ def tile_moe_pre_lin_none_kernel(tc, xT, w, gate, offs, pos1, pos2, pos3, out):
             for i, g, s0, n in products:
                 block = s0 // C * PASSES + g
                 ready = block in blocks_done and all(s in slots_done[g] for s in range(s0, s0 + n, HALF))
-                if (g, s0) in issued or not ready:
+                if (g, s0) in issued or not ready or i not in accs:
                     continue
                 a, b = BANKS[i]
                 before = len([1 for gg, ss in issued if a <= ss < b])
@@ -125,6 +132,9 @@ def tile_moe_pre_lin_none_kernel(tc, xT, w, gate, offs, pos1, pos2, pos3, out):
                         nc.vector.tensor_copy(y[:, a:b], accs[i][:])
                     else:
                         nc.scalar.copy(y[:, a:b], accs[i][:])
+                    if i + sum_banks < len(BANKS):
+                        c, d = BANKS[i + sum_banks]
+                        accs[i + sum_banks] = psum.tile([P, d - c], F32, name=f"late{i}", tag=f"acc{i}")
 
         def quantize_slots(grouped, g, s0, n):
             nc.vector.quantize_mx(
@@ -134,41 +144,51 @@ def tile_moe_pre_lin_none_kernel(tc, xT, w, gate, offs, pos1, pos2, pos3, out):
                 slots_done[g].add(s)
             multiply()
 
-        def quantize_weights(grouped, b0):
-            columns = slice(b0 * N, (b0 + W_LOAD) * N)
+        def quantize_weights(grouped, e):
+            columns = slice(e * PASSES * N, (e + 1) * PASSES * N)
             nc.vector.quantize_mx(
                 out=w_codes[:, columns].bitcast(FP8X4), scales=w_scales[:, columns], in_=grouped[:]
             )
-            for b in range(b0, b0 + W_LOAD):
+            for b in range(e * PASSES, (e + 1) * PASSES):
                 blocks_done.add(b)
             multiply()
 
-        def vector_gather(plane, j, s0, n):
-            nc.vector.tensor_tensor(plane, tokens(0, j, s0, n), gates[:, s0:s0 + n], MULT)
+        def vector_gather(plane, g, j, s0, n):
+            nc.vector.tensor_tensor(plane, tokens(g, j, s0, n), gates[:, s0:s0 + n], MULT)
 
-        def interleave_slots(planes, s0, n):
-            grouped = new_grouped(n)
+        def handed(columns):
+            return keep.tile([P, columns * PACK], BF16, name="handed", tag="handed", align_bytes=64)
+
+        def interleave_slots(grouped, planes, g, s0, n):
             nc.vector.tensor_copy(pairs_out(grouped[:]), pairs_in(planes))
-            return lambda: quantize_slots(grouped, 0, s0, n)
+            return lambda: quantize_slots(grouped, g, s0, n)
 
-        def interleave_weights(k):
-            grouped = new_grouped(W_LOAD * N)
-            nc.vector.tensor_copy(
-                grouped[:].rearrange("p (b c i j) -> p b c j i", b=W_LOAD, i=2, j=PACK),
-                raws[k][:].rearrange("p b (j c i) -> p b c j i", j=PACK, i=2),
+        def interleave_weights(e):
+            grouped = handed(PASSES * N)
+            nc.gpsimd.tensor_scalar(
+                grouped[:].rearrange("p (b n j) -> p b n j", b=PASSES, j=PACK),
+                raws[e][:].rearrange("p b (j n) -> p b n j", j=PACK),
+                1.0, 0.0, MULT, ADD,
             )
-            if len(raws) < W_BLOCKS // W_LOAD:
+            if len(raws) < E:
                 load_weights()
-            return lambda: quantize_weights(grouped, k * W_LOAD)
+            return lambda: quantize_weights(grouped, e)
 
         def scalar_unit(g, s0, n):
             picked = picked_pool.tile([P, PACK, n], F32, name="picked")
             for j in range(PACK):
                 nc.scalar.activation(picked[:, j, :], tokens(g, j, s0, n), COPY)
+            return [(picked[:, :, a:min(a + UNIT, n)], g, s0 + a, min(UNIT, n - a)) for a in range(0, n, UNIT)]
+
+        def apply_gate(planes, g, s0, n):
             grouped = new_grouped(n)
-            gate_pairs = gates[:, s0:s0 + n].rearrange("p (c o i) -> p c o i", o=1, i=2)
+            spread = gate_psum.tile([P, n], F32, name="spread")
+            for a in range(0, n, P):
+                c = (s0 + a) // P
+                nc.tensor.transpose(spread[:, a:a + P], gate_columns[:, c:c + 1].to_broadcast([P, P]), identity[:])
+            gate_pairs = spread[:].rearrange("p (c o i) -> p c o i", o=1, i=2)
             nc.vector.tensor_tensor(
-                pairs_out(grouped[:]), pairs_in(picked[:]), gate_pairs.broadcast_to([P, n // 2, PACK, 2]), MULT
+                pairs_out(grouped[:]), pairs_in(planes), gate_pairs.broadcast_to([P, n // 2, PACK, 2]), MULT
             )
             return lambda: quantize_slots(grouped, g, s0, n)
 
@@ -176,55 +196,68 @@ def tile_moe_pre_lin_none_kernel(tc, xT, w, gate, offs, pos1, pos2, pos3, out):
         load_window(0, 0)
         for a, b in HEAD_CUTS:
             nc.sync.dma_start(gates[:, a:b], gate[0:P, a:b])
-            vector_gather(head[:, 0, a:b], 0, a, b - a)
+            vector_gather(head[:, 0, a:b], 0, 0, a, b - a)
         for j in range(1, PACK):
             load_window(0, j)
-            vector_gather(head[:, j, :], j, 0, HEAD_SLOTS)
-        nc.sync.dma_start(gates[:, HEAD_SLOTS:S], gate[0:P, HEAD_SLOTS:S])
-        load_window(1, 0)
-        load_window(1, 1)
-        load_weights()
-        load_window(1, 2)
-        load_window(1, 3)
-        for k in range(1, W_RING):
+            vector_gather(head[:, j, :], 0, j, 0, HEAD_SLOTS)
+        gate_rows = keep.tile([P, P], F32, name="gate_rows")
+        nc.sync.dma_start(gate_rows[:], gate.rearrange("k (c p) -> (k c) p", p=P)[0:P, :])
+        turned = gate_psum.tile([P, P], F32, name="spread")
+        nc.tensor.transpose(turned[:], gate_rows[:], identity[:])
+        gate_columns = keep.tile([P, S // P], F32, name="gate_columns")
+        nc.scalar.copy(gate_columns[:], turned[:, 0:S // P])
+        for k in range(W_RING):
             load_weights()
-        for j in range(PACK):
-            load_window(2, j)
+        for g in (1, 2):
+            for j in range(PACK):
+                load_window(g, j)
         lists = []
         for r, pos in enumerate((pos1, pos2, pos3)):
             tile = keep.tile([P, T // LIST], U16, name=f"pos{r}")
             nc.sync.dma_start(tile[:], pos)
             lists.append(tile)
 
-        first_half = interleave_slots(head[:, :, 0:UNIT], 0, UNIT)
-        waiting = interleave_slots(head[:, :, UNIT:HEAD_SLOTS], UNIT, UNIT)
+        first_half = interleave_slots(new_grouped(UNIT), head[:, :, 0:UNIT], 0, 0, UNIT)
+        second_half = interleave_slots(handed(UNIT), head[:, :, UNIT:HEAD_SLOTS], 0, UNIT, UNIT)
         first_half()
-        y = keep.tile([P, S], F32, name="y", tag="head")
+        second_half()
 
-        extra = VECTOR_SLOTS - HEAD_SLOTS
-        second = keep.tile([P, PACK, extra], F32, name="second")
+        second = keep.tile([P, PACK, SECOND_SLOTS], F32, name="second", tag="head")
+        late = []
 
-        def gather_second():
-            for j in range(PACK):
-                vector_gather(second[:, j, :], j, HEAD_SLOTS, extra)
-            return None
+        def interleave_second(a, n):
+            late.append(interleave_slots(new_grouped(n), second[:, :, a:a + n], 1, a, n))
 
-        fillers = [gather_second, lambda: interleave_slots(second[:], HEAD_SLOTS, extra)]
-        fillers = fillers + [lambda k=k: interleave_weights(k) for k in range(W_BLOCKS // W_LOAD)]
-        for i, (g, s0, n) in enumerate(scalar_units()):
-            quantize_unit = scalar_unit(g, s0, n)
-            if waiting is not None:
-                waiting()
-            if i < len(fillers):
-                waiting = fillers[i]()
-                quantize_unit()
-            else:
-                waiting = quantize_unit
-        waiting()
+        fillers = [lambda j=j: vector_gather(second[:, j, :], 1, j, 0, SECOND_SLOTS) for j in range(PACK)]
+        fillers = fillers + [
+            lambda a=a: interleave_second(a, min(UNIT, SECOND_SLOTS - a)) for a in range(0, SECOND_SLOTS, UNIT)
+        ]
+        step = 0
+        experts_done = 0
+        for unit in scalar_units():
+            if unit[:2] == (2, 0):
+                y = keep.tile([P, S], F32, name="y", tag="head")
+            for piece in scalar_unit(*unit):
+                wide = piece[3] == UNIT and experts_done < E
+                quantize_expert = interleave_weights(experts_done) if wide else None
+                experts_done = experts_done + (1 if wide else 0)
+                quantize_piece = apply_gate(*piece)
+                waiting = list(late)
+                late.clear()
+                for call in waiting:
+                    call()
+                if 0 <= step - SECOND_STEP < len(fillers):
+                    fillers[step - SECOND_STEP]()
+                late.append(quantize_piece)
+                if quantize_expert is not None:
+                    quantize_expert()
+                step = step + 1
+        for call in late:
+            call()
 
-        first = keep.tile([P, T], F32, name="first", tag="window00")
-        middle = keep.tile([P, T], F32, name="middle", tag="window01")
-        total = keep.tile([P, T], F32, name="total", tag="window02")
+        first = keep.tile([P, T], F32, name="first", tag="window10")
+        middle = keep.tile([P, T], F32, name="middle", tag="window11")
+        total = keep.tile([P, T], F32, name="total", tag="window12")
 
         def fetch(r, a, b):
             return y[:].indirect(lists[r][:, a // LIST:b // LIST])

@@ -29,9 +29,11 @@ SPARE = 8
 UNIT = 512
 HEAD_SLOTS = 1024
 HEAD_CUTS = [(0, 256), (256, 576), (576, HEAD_SLOTS)]
-SECOND_SLOTS = 896
-SECOND_STEP = 2
-RING = 6
+SECOND_SLOTS = 768
+SECOND_STEP = 1
+WIDE = 768
+PIECE = 384
+RING = 4
 W_BLOCKS = E * PASSES
 BLOCK = PACK * N
 W_RING = 3
@@ -43,12 +45,21 @@ TOKEN_CUTS = [0, 192, 608, 896, T]
 
 
 def scalar_units():
-    units = [(0, a, UNIT) for a in range(HEAD_SLOTS, S, UNIT)]
-    first = SECOND_SLOTS + (S - SECOND_SLOTS) % UNIT
-    if first > SECOND_SLOTS:
-        units = units + [(1, SECOND_SLOTS, first - SECOND_SLOTS)]
-    units = units + [(1, a, UNIT) for a in range(first, S, UNIT)]
-    return units + [(2, a, b - a) for a, b in BANKS]
+    units = [(0, HEAD_SLOTS, UNIT)] + [(0, a, WIDE) for a in range(HEAD_SLOTS + UNIT, S, WIDE)]
+    units = units + [(1, a, WIDE) for a in range(SECOND_SLOTS, S, WIDE)]
+    units = units + [(2, a, WIDE) for a in range(0, S - WIDE, WIDE)]
+    return units + [(2, S - WIDE, UNIT), (2, S - C, HALF), (2, S - HALF, HALF)]
+
+
+def weight_batches():
+    batches = []
+    first = 0
+    for g, s0, n in scalar_units():
+        blocks = {WIDE: 4, UNIT: 2}.get(n, 0)
+        batches.append((first, blocks))
+        first = first + blocks
+    assert first == W_BLOCKS
+    return batches
 
 
 def tile_moe_pre_lin_none_kernel(tc, xT, w, gate, offs, pos1, pos2, pos3, out):
@@ -56,7 +67,7 @@ def tile_moe_pre_lin_none_kernel(tc, xT, w, gate, offs, pos1, pos2, pos3, out):
     with ExitStack() as ctx:
         keep = ctx.enter_context(tc.tile_pool(name="keep", bufs=1))
         picked_pool = ctx.enter_context(tc.tile_pool(name="picked", bufs=RING))
-        grouped_pool = ctx.enter_context(tc.tile_pool(name="grouped", bufs=4))
+        grouped_pool = ctx.enter_context(tc.tile_pool(name="grouped", bufs=5))
         raw_pool = ctx.enter_context(tc.tile_pool(name="raw", bufs=W_RING))
         psum = ctx.enter_context(tc.psum_pool(name="psum", bufs=1))
         gate_psum = ctx.enter_context(tc.psum_pool(name="gate_psum", bufs=GATE_BANKS))
@@ -68,7 +79,7 @@ def tile_moe_pre_lin_none_kernel(tc, xT, w, gate, offs, pos1, pos2, pos3, out):
         x_scales = [keep.tile([P, S], U8, name=f"x_scales{g}", align_bytes=64) for g in range(PASSES)]
         w_codes = keep.tile([P, W_BLOCKS * N], U32, name="w_codes", align_bytes=64)
         w_scales = keep.tile([P, W_BLOCKS * N], U8, name="w_scales", align_bytes=64)
-        w_blocks = w.rearrange("e (g p j) n -> p e g (j n)", p=P, j=PACK)
+        w_blocks = w.rearrange("e (g p j) n -> p (e g) (j n)", p=P, j=PACK)
         sum_banks = BANK_COUNT - GATE_BANKS
         accs = {i: psum.tile([P, b - a], F32, name=f"acc{i}") for i, (a, b) in enumerate(BANKS[:sum_banks])}
         identity = keep.tile([P, P], F32, name="identity")
@@ -87,9 +98,12 @@ def tile_moe_pre_lin_none_kernel(tc, xT, w, gate, offs, pos1, pos2, pos3, out):
 
         raws = []
 
+        batches = [batch for batch in weight_batches() if batch[1] > 0]
+
         def load_weights():
-            raw = raw_pool.tile([P, PASSES, BLOCK], F32, name="raw")
-            nc.sync.dma_start(raw[:], w_blocks[:, len(raws), :, :])
+            b0, blocks = batches[len(raws)]
+            raw = raw_pool.tile([P, blocks, BLOCK], F32, name="raw")
+            nc.sync.dma_start(raw[:], w_blocks[:, b0:b0 + blocks, :])
             raws.append(raw)
 
         def pairs_out(grouped):
@@ -144,12 +158,12 @@ def tile_moe_pre_lin_none_kernel(tc, xT, w, gate, offs, pos1, pos2, pos3, out):
                 slots_done[g].add(s)
             multiply()
 
-        def quantize_weights(grouped, e):
-            columns = slice(e * PASSES * N, (e + 1) * PASSES * N)
+        def quantize_weights(grouped, b0, blocks):
+            columns = slice(b0 * N, (b0 + blocks) * N)
             nc.vector.quantize_mx(
                 out=w_codes[:, columns].bitcast(FP8X4), scales=w_scales[:, columns], in_=grouped[:]
             )
-            for b in range(e * PASSES, (e + 1) * PASSES):
+            for b in range(b0, b0 + blocks):
                 blocks_done.add(b)
             multiply()
 
@@ -163,22 +177,24 @@ def tile_moe_pre_lin_none_kernel(tc, xT, w, gate, offs, pos1, pos2, pos3, out):
             nc.vector.tensor_copy(pairs_out(grouped[:]), pairs_in(planes))
             return lambda: quantize_slots(grouped, g, s0, n)
 
-        def interleave_weights(e):
-            grouped = handed(PASSES * N)
+        def interleave_weights(k):
+            b0, blocks = batches[k]
+            grouped = handed(blocks * N)
             nc.gpsimd.tensor_scalar(
-                grouped[:].rearrange("p (b n j) -> p b n j", b=PASSES, j=PACK),
-                raws[e][:].rearrange("p b (j n) -> p b n j", j=PACK),
+                grouped[:].rearrange("p (b n j) -> p b n j", b=blocks, j=PACK),
+                raws[k][:].rearrange("p b (j n) -> p b n j", j=PACK),
                 1.0, 0.0, MULT, ADD,
             )
-            if len(raws) < E:
+            if len(raws) < len(batches):
                 load_weights()
-            return lambda: quantize_weights(grouped, e)
+            return lambda: quantize_weights(grouped, b0, blocks)
 
         def scalar_unit(g, s0, n):
             picked = picked_pool.tile([P, PACK, n], F32, name="picked")
             for j in range(PACK):
                 nc.scalar.activation(picked[:, j, :], tokens(g, j, s0, n), COPY)
-            return [(picked[:, :, a:min(a + UNIT, n)], g, s0 + a, min(UNIT, n - a)) for a in range(0, n, UNIT)]
+            width = PIECE if n == WIDE else n
+            return [(picked[:, :, a:a + width], g, s0 + a, width) for a in range(0, n, width)]
 
         def apply_gate(planes, g, s0, n):
             grouped = new_grouped(n)
@@ -206,21 +222,23 @@ def tile_moe_pre_lin_none_kernel(tc, xT, w, gate, offs, pos1, pos2, pos3, out):
         nc.tensor.transpose(turned[:], gate_rows[:], identity[:])
         gate_columns = keep.tile([P, S // P], F32, name="gate_columns")
         nc.scalar.copy(gate_columns[:], turned[:, 0:S // P])
-        for k in range(W_RING):
+        for k in range(W_RING - 1):
             load_weights()
-        for g in (1, 2):
-            for j in range(PACK):
-                load_window(g, j)
+        for j in range(PACK):
+            load_window(1, j)
+        load_weights()
+        for j in range(PACK):
+            load_window(2, j)
         lists = []
         for r, pos in enumerate((pos1, pos2, pos3)):
             tile = keep.tile([P, T // LIST], U16, name=f"pos{r}")
             nc.sync.dma_start(tile[:], pos)
             lists.append(tile)
 
-        first_half = interleave_slots(new_grouped(UNIT), head[:, :, 0:UNIT], 0, 0, UNIT)
         second_half = interleave_slots(handed(UNIT), head[:, :, UNIT:HEAD_SLOTS], 0, UNIT, UNIT)
-        first_half()
+        first_half = interleave_slots(new_grouped(UNIT), head[:, :, 0:UNIT], 0, 0, UNIT)
         second_half()
+        first_half()
 
         second = keep.tile([P, PACK, SECOND_SLOTS], F32, name="second", tag="head")
         late = []
@@ -232,26 +250,23 @@ def tile_moe_pre_lin_none_kernel(tc, xT, w, gate, offs, pos1, pos2, pos3, out):
         fillers = fillers + [
             lambda a=a: interleave_second(a, min(UNIT, SECOND_SLOTS - a)) for a in range(0, SECOND_SLOTS, UNIT)
         ]
-        step = 0
-        experts_done = 0
-        for unit in scalar_units():
+        for step, unit in enumerate(scalar_units()):
             if unit[:2] == (2, 0):
                 y = keep.tile([P, S], F32, name="y", tag="head")
-            for piece in scalar_unit(*unit):
-                wide = piece[3] == UNIT and experts_done < E
-                quantize_expert = interleave_weights(experts_done) if wide else None
-                experts_done = experts_done + (1 if wide else 0)
-                quantize_piece = apply_gate(*piece)
-                waiting = list(late)
-                late.clear()
-                for call in waiting:
-                    call()
-                if 0 <= step - SECOND_STEP < len(fillers):
-                    fillers[step - SECOND_STEP]()
-                late.append(quantize_piece)
-                if quantize_expert is not None:
-                    quantize_expert()
-                step = step + 1
+            pieces = scalar_unit(*unit)
+            quantize_batch = interleave_weights(step) if step < len(batches) else None
+            waiting = list(late)
+            late.clear()
+            fresh = [apply_gate(*piece) for piece in pieces]
+            for call in waiting[:-1]:
+                call()
+            if 0 <= step - SECOND_STEP < len(fillers):
+                fillers[step - SECOND_STEP]()
+            if quantize_batch is not None:
+                quantize_batch()
+            for call in waiting[-1:]:
+                call()
+            late.extend(fresh)
         for call in late:
             call()
 

@@ -27,10 +27,11 @@ BYTES = 4 * (K * T + E * K * N + S + N * T) + 2 * (S + 3 * T)
 
 SPARE = 8
 UNIT = 512
-HEAD_SLOTS = 1024
-HEAD_CUTS = [(0, 256), (256, 576), (576, HEAD_SLOTS)]
+HEAD_SLOTS = 768
+HEAD_CUTS = [(0, 256), (256, HEAD_SLOTS)]
+RUN = 4
 SECOND_SLOTS = 768
-SECOND_STEP = 1
+EARLY_PLANES = 2
 WIDE = 768
 PIECE = 384
 RING = 4
@@ -45,7 +46,7 @@ TOKEN_CUTS = [0, 192, 608, 896, T]
 
 
 def scalar_units():
-    units = [(0, HEAD_SLOTS, UNIT)] + [(0, a, WIDE) for a in range(HEAD_SLOTS + UNIT, S, WIDE)]
+    units = [(0, a, WIDE) for a in range(HEAD_SLOTS, S, WIDE)]
     units = units + [(1, a, WIDE) for a in range(SECOND_SLOTS, S, WIDE)]
     units = units + [(2, a, WIDE) for a in range(0, S - WIDE, WIDE)]
     return units + [(2, S - WIDE, UNIT), (2, S - C, HALF), (2, S - HALF, HALF)]
@@ -55,7 +56,7 @@ def weight_batches():
     batches = []
     first = 0
     for g, s0, n in scalar_units():
-        blocks = {WIDE: 4, UNIT: 2}.get(n, 0)
+        blocks = 4 if n == WIDE else 0
         batches.append((first, blocks))
         first = first + blocks
     assert first == W_BLOCKS
@@ -107,10 +108,10 @@ def tile_moe_pre_lin_none_kernel(tc, xT, w, gate, offs, pos1, pos2, pos3, out):
             raws.append(raw)
 
         def pairs_out(grouped):
-            return grouped.rearrange("p (c i j) -> p c j i", i=2, j=PACK)
+            return grouped.rearrange("p (c i j) -> p c j i", i=RUN, j=PACK)
 
         def pairs_in(planes):
-            return planes.rearrange("p j (c i) -> p c j i", i=2)
+            return planes.rearrange("p j (c i) -> p c j i", i=RUN)
 
         def new_grouped(columns):
             return grouped_pool.tile([P, columns * PACK], BF16, name="grouped", align_bytes=64)
@@ -202,9 +203,9 @@ def tile_moe_pre_lin_none_kernel(tc, xT, w, gate, offs, pos1, pos2, pos3, out):
             for a in range(0, n, P):
                 c = (s0 + a) // P
                 nc.tensor.transpose(spread[:, a:a + P], gate_columns[:, c:c + 1].to_broadcast([P, P]), identity[:])
-            gate_pairs = spread[:].rearrange("p (c o i) -> p c o i", o=1, i=2)
+            gate_pairs = spread[:].rearrange("p (c o i) -> p c o i", o=1, i=RUN)
             nc.vector.tensor_tensor(
-                pairs_out(grouped[:]), pairs_in(planes), gate_pairs.broadcast_to([P, n // 2, PACK, 2]), MULT
+                pairs_out(grouped[:]), pairs_in(planes), gate_pairs.broadcast_to([P, n // RUN, PACK, RUN]), MULT
             )
             return lambda: quantize_slots(grouped, g, s0, n)
 
@@ -216,17 +217,19 @@ def tile_moe_pre_lin_none_kernel(tc, xT, w, gate, offs, pos1, pos2, pos3, out):
         for j in range(1, PACK):
             load_window(0, j)
             vector_gather(head[:, j, :], 0, j, 0, HEAD_SLOTS)
+        for j in range(EARLY_PLANES):
+            load_window(1, j)
         gate_rows = keep.tile([P, P], F32, name="gate_rows")
         nc.sync.dma_start(gate_rows[:], gate.rearrange("k (c p) -> (k c) p", p=P)[0:P, :])
         turned = gate_psum.tile([P, P], F32, name="spread")
         nc.tensor.transpose(turned[:], gate_rows[:], identity[:])
         gate_columns = keep.tile([P, S // P], F32, name="gate_columns")
-        nc.scalar.copy(gate_columns[:], turned[:, 0:S // P])
-        for k in range(W_RING - 1):
-            load_weights()
-        for j in range(PACK):
-            load_window(1, j)
+        nc.vector.tensor_copy(gate_columns[:], turned[:, 0:S // P])
         load_weights()
+        for j in range(EARLY_PLANES, PACK):
+            load_window(1, j)
+        for k in range(1, W_RING):
+            load_weights()
         for j in range(PACK):
             load_window(2, j)
         lists = []
@@ -235,23 +238,23 @@ def tile_moe_pre_lin_none_kernel(tc, xT, w, gate, offs, pos1, pos2, pos3, out):
             nc.sync.dma_start(tile[:], pos)
             lists.append(tile)
 
-        second_half = interleave_slots(handed(UNIT), head[:, :, UNIT:HEAD_SLOTS], 0, UNIT, UNIT)
-        first_half = interleave_slots(new_grouped(UNIT), head[:, :, 0:UNIT], 0, 0, UNIT)
-        second_half()
-        first_half()
-
+        first_half = interleave_slots(new_grouped(PIECE), head[:, :, 0:PIECE], 0, 0, PIECE)
+        second_half = interleave_slots(handed(PIECE), head[:, :, PIECE:HEAD_SLOTS], 0, PIECE, PIECE)
         second = keep.tile([P, PACK, SECOND_SLOTS], F32, name="second", tag="head")
+        for j, quantize_half in enumerate((first_half, second_half)):
+            quantize_half()
+            vector_gather(second[:, j, :], 1, j, 0, SECOND_SLOTS)
         late = []
 
         def interleave_second(a, n):
             late.append(interleave_slots(new_grouped(n), second[:, :, a:a + n], 1, a, n))
 
-        fillers = [lambda j=j: vector_gather(second[:, j, :], 1, j, 0, SECOND_SLOTS) for j in range(PACK)]
+        fillers = [lambda j=j: vector_gather(second[:, j, :], 1, j, 0, SECOND_SLOTS) for j in range(EARLY_PLANES, PACK)]
         fillers = fillers + [
-            lambda a=a: interleave_second(a, min(UNIT, SECOND_SLOTS - a)) for a in range(0, SECOND_SLOTS, UNIT)
+            lambda a=a: interleave_second(a, PIECE) for a in range(0, SECOND_SLOTS, PIECE)
         ]
         for step, unit in enumerate(scalar_units()):
-            if unit[:2] == (2, 0):
+            if unit[:2] == (2, WIDE):
                 y = keep.tile([P, S], F32, name="y", tag="head")
             pieces = scalar_unit(*unit)
             quantize_batch = interleave_weights(step) if step < len(batches) else None
@@ -260,8 +263,8 @@ def tile_moe_pre_lin_none_kernel(tc, xT, w, gate, offs, pos1, pos2, pos3, out):
             fresh = [apply_gate(*piece) for piece in pieces]
             for call in waiting[:-1]:
                 call()
-            if 0 <= step - SECOND_STEP < len(fillers):
-                fillers[step - SECOND_STEP]()
+            if step < len(fillers):
+                fillers[step]()
             if quantize_batch is not None:
                 quantize_batch()
             for call in waiting[-1:]:

@@ -27,17 +27,18 @@ BYTES = 4 * (K * T + E * K * N + S + N * T) + 2 * (S + 3 * T)
 
 SPARE = 8
 UNIT = 512
-HEAD_SLOTS = 768
-HEAD_CUTS = [(0, 256), (256, HEAD_SLOTS)]
+HEAD_SLOTS = 1024
+HEAD_CUTS = [(0, 256), (256, 576), (576, HEAD_SLOTS)]
 RUN = 4
-SECOND_SLOTS = 768
+SECOND_SLOTS = 1024
 EARLY_PLANES = 2
-WIDE = 768
-PIECE = 384
-RING = 4
+WIDE = 1024
+PIECE = 512
+RING = 3
+BATCH = 6
 W_BLOCKS = E * PASSES
 BLOCK = PACK * N
-W_RING = 3
+W_RING = 2
 BANK_COUNT = 8
 GATE_BANKS = 2
 HALF = C // 2
@@ -49,14 +50,14 @@ def scalar_units():
     units = [(0, a, WIDE) for a in range(HEAD_SLOTS, S, WIDE)]
     units = units + [(1, a, WIDE) for a in range(SECOND_SLOTS, S, WIDE)]
     units = units + [(2, a, WIDE) for a in range(0, S - WIDE, WIDE)]
-    return units + [(2, S - WIDE, UNIT), (2, S - C, HALF), (2, S - HALF, HALF)]
+    return units + [(2, a, b - a) for a, b in BANKS if a >= S - WIDE]
 
 
 def weight_batches():
     batches = []
     first = 0
     for g, s0, n in scalar_units():
-        blocks = 4 if n == WIDE else 0
+        blocks = BATCH if n == WIDE else 0
         batches.append((first, blocks))
         first = first + blocks
     assert first == W_BLOCKS
@@ -68,7 +69,7 @@ def tile_moe_pre_lin_none_kernel(tc, xT, w, gate, offs, pos1, pos2, pos3, out):
     with ExitStack() as ctx:
         keep = ctx.enter_context(tc.tile_pool(name="keep", bufs=1))
         picked_pool = ctx.enter_context(tc.tile_pool(name="picked", bufs=RING))
-        grouped_pool = ctx.enter_context(tc.tile_pool(name="grouped", bufs=5))
+        grouped_pool = ctx.enter_context(tc.tile_pool(name="grouped", bufs=3))
         raw_pool = ctx.enter_context(tc.tile_pool(name="raw", bufs=W_RING))
         psum = ctx.enter_context(tc.psum_pool(name="psum", bufs=1))
         gate_psum = ctx.enter_context(tc.psum_pool(name="gate_psum", bufs=GATE_BANKS))
@@ -89,7 +90,7 @@ def tile_moe_pre_lin_none_kernel(tc, xT, w, gate, offs, pos1, pos2, pos3, out):
         windows = {}
 
         def load_window(g, j):
-            window = keep.tile([P, T + SPARE], F32, name=f"window{g}{j}")
+            window = keep.tile([P, T + SPARE], F32, name=f"window{g}{j}", tag=f"window{g % 2}{j}")
             rows = xT[g * K_PASS:(g + 1) * K_PASS, :].rearrange("(p j) t -> p j t", j=PACK)
             nc.sync.dma_start(window[:, 0:T], rows[:, j, :])
             windows[(g, j)] = window
@@ -160,10 +161,13 @@ def tile_moe_pre_lin_none_kernel(tc, xT, w, gate, offs, pos1, pos2, pos3, out):
             multiply()
 
         def quantize_weights(grouped, b0, blocks):
-            columns = slice(b0 * N, (b0 + blocks) * N)
-            nc.vector.quantize_mx(
-                out=w_codes[:, columns].bitcast(FP8X4), scales=w_scales[:, columns], in_=grouped[:]
-            )
+            for a, b in ((0, PIECE // N), (PIECE // N, blocks)):
+                columns = slice((b0 + a) * N, (b0 + b) * N)
+                nc.vector.quantize_mx(
+                    out=w_codes[:, columns].bitcast(FP8X4),
+                    scales=w_scales[:, columns],
+                    in_=grouped[:, a * BLOCK:b * BLOCK],
+                )
             for b in range(b0, b0 + blocks):
                 blocks_done.add(b)
             multiply()
@@ -194,19 +198,24 @@ def tile_moe_pre_lin_none_kernel(tc, xT, w, gate, offs, pos1, pos2, pos3, out):
             picked = picked_pool.tile([P, PACK, n], F32, name="picked")
             for j in range(PACK):
                 nc.scalar.activation(picked[:, j, :], tokens(g, j, s0, n), COPY)
-            width = PIECE if n == WIDE else n
-            return [(picked[:, :, a:a + width], g, s0 + a, width) for a in range(0, n, width)]
+            return picked
 
-        def apply_gate(planes, g, s0, n):
+        def apply_gate(picked, g, s0, n):
             grouped = new_grouped(n)
-            spread = gate_psum.tile([P, n], F32, name="spread")
-            for a in range(0, n, P):
-                c = (s0 + a) // P
-                nc.tensor.transpose(spread[:, a:a + P], gate_columns[:, c:c + 1].to_broadcast([P, P]), identity[:])
-            gate_pairs = spread[:].rearrange("p (c o i) -> p c o i", o=1, i=RUN)
-            nc.vector.tensor_tensor(
-                pairs_out(grouped[:]), pairs_in(planes), gate_pairs.broadcast_to([P, n // RUN, PACK, RUN]), MULT
-            )
+            width = min(n, PIECE)
+            for first in range(0, n, width):
+                spread = gate_psum.tile([P, width], F32, name="spread")
+                for a in range(0, width, P):
+                    c = (s0 + first + a) // P
+                    column = gate_columns[:, c:c + 1].to_broadcast([P, P])
+                    nc.tensor.transpose(spread[:, a:a + P], column, identity[:])
+                gate_runs = spread[:].rearrange("p (c o i) -> p c o i", o=1, i=RUN)
+                nc.vector.tensor_tensor(
+                    pairs_out(grouped[:, first * PACK:(first + width) * PACK]),
+                    pairs_in(picked[:, :, first:first + width]),
+                    gate_runs.broadcast_to([P, width // RUN, PACK, RUN]),
+                    MULT,
+                )
             return lambda: quantize_slots(grouped, g, s0, n)
 
         head = keep.tile([P, PACK, HEAD_SLOTS], F32, name="head", tag="head")
@@ -230,8 +239,6 @@ def tile_moe_pre_lin_none_kernel(tc, xT, w, gate, offs, pos1, pos2, pos3, out):
             load_window(1, j)
         for k in range(1, W_RING):
             load_weights()
-        for j in range(PACK):
-            load_window(2, j)
         lists = []
         for r, pos in enumerate((pos1, pos2, pos3)):
             tile = keep.tile([P, T // LIST], U16, name=f"pos{r}")
@@ -250,17 +257,18 @@ def tile_moe_pre_lin_none_kernel(tc, xT, w, gate, offs, pos1, pos2, pos3, out):
             late.append(interleave_slots(new_grouped(n), second[:, :, a:a + n], 1, a, n))
 
         fillers = [lambda j=j: vector_gather(second[:, j, :], 1, j, 0, SECOND_SLOTS) for j in range(EARLY_PLANES, PACK)]
-        fillers = fillers + [
-            lambda a=a: interleave_second(a, PIECE) for a in range(0, SECOND_SLOTS, PIECE)
-        ]
+        fillers = fillers + [lambda: interleave_second(0, SECOND_SLOTS)]
         for step, unit in enumerate(scalar_units()):
+            if unit[:2] == (1, SECOND_SLOTS):
+                for j in range(PACK):
+                    load_window(2, j)
             if unit[:2] == (2, WIDE):
                 y = keep.tile([P, S], F32, name="y", tag="head")
-            pieces = scalar_unit(*unit)
+            picked = scalar_unit(*unit)
             quantize_batch = interleave_weights(step) if step < len(batches) else None
             waiting = list(late)
             late.clear()
-            fresh = [apply_gate(*piece) for piece in pieces]
+            fresh = [apply_gate(picked, *unit)]
             for call in waiting[:-1]:
                 call()
             if step < len(fillers):

@@ -86,6 +86,10 @@ def tile_moe_pre_lin_none_kernel(tc, xT, w, gate, offs, pos1, pos2, pos3, out):
         accs = {i: psum.tile([P, b - a], F32, name=f"acc{i}") for i, (a, b) in enumerate(BANKS[:sum_banks])}
         identity = keep.tile([P, P], F32, name="identity")
         make_identity(nc, identity[:])
+        cold = keep.tile([P, 8], F32, name="cold")
+        nc.vector.memset(cold[:], 0.0)
+        warm = keep.tile([P, 8], F32, name="warm")
+        nc.scalar.activation(warm[:], cold[:], COPY)
 
         windows = {}
 

@@ -26,64 +26,38 @@ FLOPS = 2 * K * S * N
 BYTES = 4 * (K * T + E * K * N + S + N * T) + 2 * (S + 3 * T)
 
 SPARE = 8
-UNIT = 512
-HEAD_SLOTS = 1024
-HEAD_CUTS = [(0, 256), (256, 576), (576, HEAD_SLOTS)]
 RUN = 4
-SECOND_SLOTS = 1024
-EARLY_PLANES = 2
+BANK = 512
+HALF = C // 2
 WIDE = 1024
-PIECE = 512
-RING = 3
+PIECE = 256
 BATCH = 6
-W_BLOCKS = E * PASSES
+HEAD_BLOCKS = 2
 BLOCK = PACK * N
-W_RING = 2
+RING = 3
+PLACE = PACK * WIDE * 4
 BANK_COUNT = 8
 GATE_BANKS = 2
-HALF = C // 2
-BANKS = [(a, a + UNIT) for a in range(0, S - UNIT, UNIT)] + [(S - UNIT, S - C), (S - C, S - HALF), (S - HALF, S)]
+OWN_SLOTS = 1024
+GROUPS = [(a, a + BANK) for a in range(0, S - BANK, BANK)] + [(S - BANK, S - C), (S - C, S - HALF), (S - HALF, S)]
+REUSED = {6: 1, 7: 2}
+UNITS = [(0, 1024), (0, 2048), (1, 1024), (1, 2048), (2, 256), (2, 1280)]
+TAPER = [(2304, 384), (2688, 256), (2944, 128)]
+PIECES = [(0, 0), (0, 768), (1, 512), (1, 768), (1, 0), (1, 256), (2, 0)]
+KEPT = (256, 512)
 TOKEN_CUTS = [0, 192, 608, 896, T]
-
-
-def scalar_units():
-    units = [(0, a, WIDE) for a in range(HEAD_SLOTS, S, WIDE)]
-    units = units + [(1, a, WIDE) for a in range(SECOND_SLOTS, S, WIDE)]
-    units = units + [(2, a, WIDE) for a in range(0, S - WIDE, WIDE)]
-    return units + [(2, a, b - a) for a, b in BANKS if a >= S - WIDE]
-
-
-def weight_batches():
-    batches = []
-    first = 0
-    for g, s0, n in scalar_units():
-        blocks = BATCH if n == WIDE else 0
-        batches.append((first, blocks))
-        first = first + blocks
-    assert first == W_BLOCKS
-    return batches
 
 
 def tile_moe_pre_lin_none_kernel(tc, xT, w, gate, offs, pos1, pos2, pos3, out):
     nc = tc.nc
     with ExitStack() as ctx:
         keep = ctx.enter_context(tc.tile_pool(name="keep", bufs=1))
-        picked_pool = ctx.enter_context(tc.tile_pool(name="picked", bufs=RING))
-        grouped_pool = ctx.enter_context(tc.tile_pool(name="grouped", bufs=3))
-        raw_pool = ctx.enter_context(tc.tile_pool(name="raw", bufs=W_RING))
+        picked_pool = ctx.enter_context(tc.tile_pool(name="picked", bufs=1))
         psum = ctx.enter_context(tc.psum_pool(name="psum", bufs=1))
         gate_psum = ctx.enter_context(tc.psum_pool(name="gate_psum", bufs=GATE_BANKS))
 
         offsets = keep.tile([P, S // LIST], U16, name="offsets")
         nc.sync.dma_start(offsets[:], offs)
-        gates = keep.tile([P, HEAD_SLOTS], F32, name="gates")
-        x_codes = [keep.tile([P, S], U32, name=f"x_codes{g}", align_bytes=64) for g in range(PASSES)]
-        x_scales = [keep.tile([P, S], U8, name=f"x_scales{g}", align_bytes=64) for g in range(PASSES)]
-        w_codes = keep.tile([P, W_BLOCKS * N], U32, name="w_codes", align_bytes=64)
-        w_scales = keep.tile([P, W_BLOCKS * N], U8, name="w_scales", align_bytes=64)
-        w_blocks = w.rearrange("e (g p j) n -> p (e g) (j n)", p=P, j=PACK)
-        sum_banks = BANK_COUNT - GATE_BANKS
-        accs = {i: psum.tile([P, b - a], F32, name=f"acc{i}") for i, (a, b) in enumerate(BANKS[:sum_banks])}
         identity = keep.tile([P, P], F32, name="identity")
         make_identity(nc, identity[:])
         cold = keep.tile([P, 8], F32, name="cold")
@@ -91,6 +65,10 @@ def tile_moe_pre_lin_none_kernel(tc, xT, w, gate, offs, pos1, pos2, pos3, out):
         warm = keep.tile([P, 8], F32, name="warm")
         nc.scalar.activation(warm[:], cold[:], COPY)
 
+        w_blocks = w.rearrange("e (g p j) n -> p (e g) (j n)", p=P, j=PACK)
+        sum_banks = BANK_COUNT - GATE_BANKS
+        accs = {i: psum.tile([P, b - a], F32, name=f"acc{i}") for i, (a, b) in enumerate(GROUPS[:sum_banks])}
+        y = keep.tile([P, S], F32, name="y")
         windows = {}
 
         def load_window(g, j):
@@ -99,191 +77,207 @@ def tile_moe_pre_lin_none_kernel(tc, xT, w, gate, offs, pos1, pos2, pos3, out):
             nc.sync.dma_start(window[:, 0:T], rows[:, j, :])
             windows[(g, j)] = window
 
+        def load_blocks(b0, blocks, tag):
+            raw = keep.tile([P, blocks, BLOCK], F32, name=f"raw{b0}", tag=tag)
+            nc.sync.dma_start(raw[:], w_blocks[:, b0:b0 + blocks, :])
+            return raw
+
         def tokens(g, j, s0, n):
             return windows[(g, j)][:].indirect(offsets[:, s0 // LIST:(s0 + n) // LIST])
 
-        raws = []
+        def staging(which, columns):
+            return keep.tile([P, columns], BF16, name="staging", tag=f"staging{which % 2}", align_bytes=64)
 
-        batches = [batch for batch in weight_batches() if batch[1] > 0]
+        def new_codes(name, words):
+            codes = keep.tile([P, words], U32, name=f"codes_{name}", align_bytes=64)
+            scales = keep.tile([P, words], U8, name=f"scales_{name}", align_bytes=64)
+            return codes, scales
 
-        def load_weights():
-            b0, blocks = batches[len(raws)]
-            raw = raw_pool.tile([P, blocks, BLOCK], F32, name="raw")
-            nc.sync.dma_start(raw[:], w_blocks[:, b0:b0 + blocks, :])
-            raws.append(raw)
-
-        def pairs_out(grouped):
-            return grouped.rearrange("p (c i j) -> p c j i", i=RUN, j=PACK)
-
-        def pairs_in(planes):
-            return planes.rearrange("p j (c i) -> p c j i", i=RUN)
-
-        def new_grouped(columns):
-            return grouped_pool.tile([P, columns * PACK], BF16, name="grouped", align_bytes=64)
-
-        slots_done = [set() for g in range(PASSES)]
-        blocks_done = set()
+        x_at = {}
+        w_at = {}
         issued = set()
         products = [
-            (i, g, s0, min(C, b - a)) for g in range(PASSES) for i, (a, b) in enumerate(BANKS) for s0 in range(a, b, C)
+            (i, g, s0, min(C, b - a)) for g in range(PASSES) for i, (a, b) in enumerate(GROUPS) for s0 in range(a, b, C)
         ]
 
         def multiply():
             for i, g, s0, n in products:
                 block = s0 // C * PASSES + g
-                ready = block in blocks_done and all(s in slots_done[g] for s in range(s0, s0 + n, HALF))
+                ready = block in w_at and all((g, s) in x_at for s in range(s0, s0 + n, HALF))
                 if (g, s0) in issued or not ready or i not in accs:
                     continue
-                a, b = BANKS[i]
+                a, b = GROUPS[i]
                 before = len([1 for gg, ss in issued if a <= ss < b])
                 total = len([1 for ii, gg, ss, nn in products if ii == i])
                 issued.add((g, s0))
+                w_codes, w_scales, wc = w_at[block]
+                x_codes, x_scales, xc = x_at[(g, s0)]
                 nc.tensor.matmul_mx(
                     out=accs[i][:, s0 - a:s0 - a + n],
-                    lhsT=w_codes[:, block * N:(block + 1) * N].bitcast(FP8X4),
-                    lhsT_scale=w_scales[:, block * N:(block + 1) * N],
-                    rhs=x_codes[g][:, s0:s0 + n].bitcast(FP8X4),
-                    rhs_scale=x_scales[g][:, s0:s0 + n],
+                    lhsT=w_codes[:, wc:wc + N].bitcast(FP8X4),
+                    lhsT_scale=w_scales[:, wc:wc + N],
+                    rhs=x_codes[:, xc:xc + n].bitcast(FP8X4),
+                    rhs_scale=x_scales[:, xc:xc + n],
                     start=(before == 0),
                     stop=(before == total - 1),
                 )
                 if before == total - 1:
-                    if i == len(BANKS) - 2:
+                    if i == len(GROUPS) - 2:
                         nc.vector.tensor_copy(y[:, a:b], accs[i][:])
                     else:
                         nc.scalar.copy(y[:, a:b], accs[i][:])
-                    if i + sum_banks < len(BANKS):
-                        c, d = BANKS[i + sum_banks]
-                        accs[i + sum_banks] = psum.tile([P, d - c], F32, name=f"late{i}", tag=f"acc{i}")
+                    for late, bank in REUSED.items():
+                        if bank == i:
+                            c, d = GROUPS[late]
+                            accs[late] = psum.tile([P, d - c], F32, name=f"late{late}", tag=f"acc{i}")
 
-        def quantize_slots(grouped, g, s0, n):
+        def quantize(pair, first, source, slots, blocks):
+            codes, scales = pair
+            words = sum([n for g, s0, n in slots]) + len(blocks) * N
             nc.vector.quantize_mx(
-                out=x_codes[g][:, s0:s0 + n].bitcast(FP8X4), scales=x_scales[g][:, s0:s0 + n], in_=grouped[:]
+                out=codes[:, first:first + words].bitcast(FP8X4), scales=scales[:, first:first + words], in_=source
             )
-            for s in range(s0, s0 + n, HALF):
-                slots_done[g].add(s)
+            at = first
+            for b in blocks:
+                w_at[b] = (codes, scales, at)
+                at = at + N
+            for g, s0, n in slots:
+                for s in range(0, n, HALF):
+                    x_at[(g, s0 + s)] = (codes, scales, at + s)
+                at = at + n
             multiply()
 
-        def quantize_weights(grouped, b0, blocks):
-            for a, b in ((0, PIECE // N), (PIECE // N, blocks)):
-                columns = slice((b0 + a) * N, (b0 + b) * N)
-                nc.vector.quantize_mx(
-                    out=w_codes[:, columns].bitcast(FP8X4),
-                    scales=w_scales[:, columns],
-                    in_=grouped[:, a * BLOCK:b * BLOCK],
-                )
-            for b in range(b0, b0 + blocks):
-                blocks_done.add(b)
-            multiply()
+        def vector_gather(planes, g, j, s0, n):
+            nc.vector.tensor_copy(planes[:, j, :], tokens(g, j, s0, n))
 
-        def vector_gather(plane, g, j, s0, n):
-            nc.vector.tensor_tensor(plane, tokens(g, j, s0, n), gates[:, s0:s0 + n], MULT)
-
-        def handed(columns):
-            return keep.tile([P, columns * PACK], BF16, name="handed", tag="handed", align_bytes=64)
-
-        def interleave_slots(grouped, planes, g, s0, n):
-            nc.vector.tensor_copy(pairs_out(grouped[:]), pairs_in(planes))
-            return lambda: quantize_slots(grouped, g, s0, n)
-
-        def interleave_weights(k):
-            b0, blocks = batches[k]
-            grouped = handed(blocks * N)
-            nc.gpsimd.tensor_scalar(
-                grouped[:].rearrange("p (b n j) -> p b n j", b=blocks, j=PACK),
-                raws[k][:].rearrange("p b (j n) -> p b n j", j=PACK),
-                1.0, 0.0, MULT, ADD,
-            )
-            if len(raws) < len(batches):
-                load_weights()
-            return lambda: quantize_weights(grouped, b0, blocks)
-
-        def scalar_unit(g, s0, n):
-            picked = picked_pool.tile([P, PACK, n], F32, name="picked")
+        def scalar_unit(picked, g, s0, n):
             for j in range(PACK):
                 nc.scalar.activation(picked[:, j, :], tokens(g, j, s0, n), COPY)
             return picked
 
-        def apply_gate(picked, g, s0, n):
-            grouped = new_grouped(n)
-            width = min(n, PIECE)
+        def vector_gate(grouped, planes, s0, n):
+            width = min(n, BANK)
             for first in range(0, n, width):
                 spread = gate_psum.tile([P, width], F32, name="spread")
                 for a in range(0, width, P):
                     c = (s0 + first + a) // P
-                    column = gate_columns[:, c:c + 1].to_broadcast([P, P])
-                    nc.tensor.transpose(spread[:, a:a + P], column, identity[:])
+                    nc.tensor.transpose(spread[:, a:a + P], gate_columns[:, c:c + 1].to_broadcast([P, P]), identity[:])
                 gate_runs = spread[:].rearrange("p (c o i) -> p c o i", o=1, i=RUN)
                 nc.vector.tensor_tensor(
-                    pairs_out(grouped[:, first * PACK:(first + width) * PACK]),
-                    pairs_in(picked[:, :, first:first + width]),
+                    grouped[:, first * PACK:(first + width) * PACK].rearrange("p (c i j) -> p c j i", i=RUN, j=PACK),
+                    planes[:, :, first:first + width].rearrange("p j (c i) -> p c j i", i=RUN),
                     gate_runs.broadcast_to([P, width // RUN, PACK, RUN]),
                     MULT,
                 )
-            return lambda: quantize_slots(grouped, g, s0, n)
 
-        head = keep.tile([P, PACK, HEAD_SLOTS], F32, name="head", tag="head")
-        load_window(0, 0)
-        for a, b in HEAD_CUTS:
-            nc.sync.dma_start(gates[:, a:b], gate[0:P, a:b])
-            vector_gather(head[:, 0, a:b], 0, 0, a, b - a)
-        for j in range(1, PACK):
+        def pool_gate(grouped, planes, s0, n):
+            nc.gpsimd.tensor_tensor(
+                grouped.rearrange("p (s j) -> p s j", j=PACK),
+                planes.rearrange("p j s -> p s j"),
+                gates[:, s0:s0 + n].rearrange("p (s o) -> p s o", o=1).broadcast_to([P, n, PACK]),
+                MULT,
+            )
+
+        def pool_weights(grouped, raw, blocks):
+            nc.gpsimd.tensor_scalar(
+                grouped.rearrange("p (b n j) -> p b n j", b=blocks, j=PACK),
+                raw[:].rearrange("p b (j n) -> p b n j", j=PACK),
+                1.0, 0.0, MULT, ADD,
+            )
+
+        def new_picked(u, n):
+            place = u % RING
+            return picked_pool.tile([P, PACK, n], F32, name="picked", tag=f"picked{place}", offset=place * PLACE)
+
+        def new_piece(k):
+            return keep.tile([P, PACK, PIECE], F32, name=f"piece{k}", tag=f"piece{k % 2}")
+
+        batch_words = BATCH * N + PIECE
+        pieces = {0: new_piece(0), 1: new_piece(1)}
+        kept = keep.tile([P, PACK, KEPT[1]], F32, name="kept")
+        handed = staging(1, batch_words * PACK)
+        first_unit = new_picked(0, WIDE)
+        for j in range(PACK):
             load_window(0, j)
-            vector_gather(head[:, j, :], 0, j, 0, HEAD_SLOTS)
-        for j in range(EARLY_PLANES):
+            vector_gather(pieces[0], 0, j, PIECES[0][1], PIECE)
+            vector_gather(kept, 0, j, KEPT[0], KEPT[1])
+            vector_gather(pieces[1], 0, j, PIECES[1][1], PIECE)
+            nc.scalar.activation(first_unit[:, j, :], tokens(0, j, UNITS[0][1], WIDE), COPY)
+            if j == 1:
+                gate_rows = keep.tile([P, P], F32, name="gate_rows")
+                nc.sync.dma_start(gate_rows[:], gate.rearrange("k (c p) -> (k c) p", p=P)[0:P, :])
+                turned = gate_psum.tile([P, P], F32, name="spread")
+                nc.tensor.transpose(turned[:], gate_rows[:], identity[:])
+                gate_columns = keep.tile([P, S // P], F32, name="gate_columns")
+                nc.vector.tensor_copy(gate_columns[:], turned[:, 0:S // P])
+            if j * HEAD_BLOCKS < BATCH:
+                b0 = j * HEAD_BLOCKS
+                raw = picked_pool.tile([P, HEAD_BLOCKS, BLOCK], F32, name=f"early{j}", offset=PLACE + b0 * BLOCK * 4)
+                nc.sync.dma_start(raw[:], w_blocks[:, b0:b0 + HEAD_BLOCKS, :])
+                pool_weights(handed[:, b0 * BLOCK:(b0 + HEAD_BLOCKS) * BLOCK], raw, HEAD_BLOCKS)
+        gates = keep.tile([P, OWN_SLOTS], F32, name="gates")
+        nc.sync.dma_start(gates[:], gate[0:P, 0:OWN_SLOTS])
+        raws = {1: load_blocks(BATCH, BATCH, "raw1")}
+        for j in range(PACK):
             load_window(1, j)
-        gate_rows = keep.tile([P, P], F32, name="gate_rows")
-        nc.sync.dma_start(gate_rows[:], gate.rearrange("k (c p) -> (k c) p", p=P)[0:P, :])
-        turned = gate_psum.tile([P, P], F32, name="spread")
-        nc.tensor.transpose(turned[:], gate_rows[:], identity[:])
-        gate_columns = keep.tile([P, S // P], F32, name="gate_columns")
-        nc.vector.tensor_copy(gate_columns[:], turned[:, 0:S // P])
-        load_weights()
-        for j in range(EARLY_PLANES, PACK):
-            load_window(1, j)
-        for k in range(1, W_RING):
-            load_weights()
+        raws[2] = load_blocks(2 * BATCH, BATCH, "raw0")
         lists = []
         for r, pos in enumerate((pos1, pos2, pos3)):
             tile = keep.tile([P, T // LIST], U16, name=f"pos{r}")
             nc.sync.dma_start(tile[:], pos)
             lists.append(tile)
 
-        first_half = interleave_slots(new_grouped(PIECE), head[:, :, 0:PIECE], 0, 0, PIECE)
-        second_half = interleave_slots(handed(PIECE), head[:, :, PIECE:HEAD_SLOTS], 0, PIECE, PIECE)
-        second = keep.tile([P, PACK, SECOND_SLOTS], F32, name="second", tag="head")
-        for j, quantize_half in enumerate((first_half, second_half)):
-            quantize_half()
-            vector_gather(second[:, j, :], 1, j, 0, SECOND_SLOTS)
-        late = []
+        pool_gate(handed[:, BATCH * BLOCK:], pieces[0][:], PIECES[0][1], PIECE)
+        grouped = staging(0, PIECE * PACK)
+        vector_gate(grouped, kept[:, :, PIECE:2 * PIECE], KEPT[0] + PIECE, PIECE)
+        quantize(new_codes("kept", PIECE), 0, grouped[:], [(0, KEPT[0] + PIECE, PIECE)], [])
+        quantize(new_codes("batch0", batch_words), 0, handed[:], [(0, PIECES[0][1], PIECE)], list(range(BATCH)))
 
-        def interleave_second(a, n):
-            late.append(interleave_slots(new_grouped(n), second[:, :, a:a + n], 1, a, n))
-
-        fillers = [lambda j=j: vector_gather(second[:, j, :], 1, j, 0, SECOND_SLOTS) for j in range(EARLY_PLANES, PACK)]
-        fillers = fillers + [lambda: interleave_second(0, SECOND_SLOTS)]
-        for step, unit in enumerate(scalar_units()):
-            if unit[:2] == (1, SECOND_SLOTS):
+        picked = first_unit
+        for k in range(1, len(UNITS)):
+            if k == 2:
                 for j in range(PACK):
                     load_window(2, j)
-            if unit[:2] == (2, WIDE):
-                y = keep.tile([P, S], F32, name="y", tag="head")
-            picked = scalar_unit(*unit)
-            quantize_batch = interleave_weights(step) if step < len(batches) else None
-            waiting = list(late)
-            late.clear()
-            fresh = [apply_gate(picked, *unit)]
-            for call in waiting[:-1]:
-                call()
-            if step < len(fillers):
-                fillers[step]()
-            if quantize_batch is not None:
-                quantize_batch()
-            for call in waiting[-1:]:
-                call()
-            late.extend(fresh)
-        for call in late:
-            call()
+            ahead = scalar_unit(new_picked(k, WIDE), UNITS[k][0], UNITS[k][1], WIDE)
+            handed = staging(k + 1, batch_words * PACK)
+            pool_weights(handed[:, 0:BATCH * BLOCK], raws[k], BATCH)
+            if k + 2 < len(UNITS):
+                raws[k + 2] = load_blocks((k + 2) * BATCH, BATCH, f"raw{k % 2}")
+            pool_gate(handed[:, BATCH * BLOCK:], pieces[k][:], PIECES[k][1], PIECE)
+            pieces[k + 1] = new_piece(k + 1)
+            g, s0 = PIECES[k + 1]
+            for j in range(PACK // 2):
+                vector_gather(pieces[k + 1], g, j, s0, PIECE)
+            grouped = staging(k, WIDE * PACK)
+            vector_gate(grouped, picked, UNITS[k - 1][1], WIDE)
+            for j in range(PACK // 2, PACK):
+                vector_gather(pieces[k + 1], g, j, s0, PIECE)
+            quantize(new_codes(f"unit{k - 1}", WIDE), 0, grouped[:], [UNITS[k - 1] + (WIDE,)], [])
+            blocks = list(range(k * BATCH, (k + 1) * BATCH))
+            quantize(new_codes(f"batch{k}", batch_words), 0, handed[:], [PIECES[k] + (PIECE,)], blocks)
+            picked = ahead
+
+        last = PASSES - 1
+        k = len(UNITS)
+        (s_a, n_a), (s_b, n_b), (s_c, n_c) = TAPER
+        taper_a = scalar_unit(new_picked(k, n_a), last, s_a, n_a)
+        taper_b = scalar_unit(keep.tile([P, PACK, n_b], F32, name="taper_b", tag="window13"), last, s_b, n_b)
+        taper_c = scalar_unit(keep.tile([P, PACK, n_c], F32, name="taper_c", tag="raw1"), last, s_c, n_c)
+        handed = staging(k + 1, 2 * PIECE * PACK)
+        pool_gate(handed[:, 0:PIECE * PACK], kept[:, :, 0:PIECE], KEPT[0], PIECE)
+        pool_gate(handed[:, PIECE * PACK:], pieces[k][:], PIECES[k][1], PIECE)
+        grouped = staging(k, (WIDE + n_a) * PACK)
+        vector_gate(grouped[:, 0:WIDE * PACK], picked, UNITS[k - 1][1], WIDE)
+        vector_gate(grouped[:, WIDE * PACK:], taper_a, s_a, n_a)
+        taper_codes = new_codes("taper", n_a + n_b + n_c)
+        quantize(new_codes(f"unit{k - 1}", WIDE), 0, grouped[:, 0:WIDE * PACK], [UNITS[k - 1] + (WIDE,)], [])
+        quantize(new_codes(f"batch{k}", 2 * PIECE), 0, handed[:], [(0, KEPT[0], PIECE), PIECES[k] + (PIECE,)], [])
+        quantize(taper_codes, 0, grouped[:, WIDE * PACK:], [(last, s_a, n_a)], [])
+        grouped = staging(k + 1, (n_b + n_c) * PACK)
+        vector_gate(grouped[:, 0:n_b * PACK], taper_b, s_b, n_b)
+        vector_gate(grouped[:, n_b * PACK:], taper_c, s_c, n_c)
+        quantize(taper_codes, n_a, grouped[:, 0:n_b * PACK], [(last, s_b, n_b)], [])
+        quantize(taper_codes, n_a + n_b, grouped[:, n_b * PACK:], [(last, s_c, n_c)], [])
 
         first = keep.tile([P, T], F32, name="first", tag="window10")
         middle = keep.tile([P, T], F32, name="middle", tag="window11")

@@ -172,9 +172,9 @@ def tile_moe_pre_lin_none_kernel(tc, xT, w, gate, offs, pos1, pos2, pos3, out):
 
         def pool_gate(grouped, planes, s0, n):
             nc.gpsimd.tensor_tensor(
-                grouped.rearrange("p (s j) -> p s j", j=PACK),
-                planes.rearrange("p j s -> p s j"),
-                gates[:, s0:s0 + n].rearrange("p (s o) -> p s o", o=1).broadcast_to([P, n, PACK]),
+                grouped.rearrange("p (c i j) -> p c j i", i=RUN, j=PACK),
+                planes.rearrange("p j (c i) -> p c j i", i=RUN),
+                gates[:, s0:s0 + n].rearrange("p (c o i) -> p c o i", o=1, i=RUN).broadcast_to([P, n // RUN, PACK, RUN]),
                 MULT,
             )
 

@@ -25,26 +25,28 @@ LIST = 16
 FLOPS = 2 * K * S * N
 BYTES = 4 * (K * T + E * K * N + S + N * T) + 2 * (S + 3 * T)
 
+FIRST = 1152
 SPARE = 8
 RUN = 4
 BANK = 512
 HALF = C // 2
 WIDE = 1024
 PIECE = 256
-BATCH = 6
+BATCH = 5
+HEAD_BATCH = 6
 HEAD_BLOCKS = 2
 BLOCK = PACK * N
 RING = 3
-PLACE = PACK * WIDE * 4
+PLACES = [0, PACK * FIRST * 4, PACK * (FIRST + WIDE) * 4]
 BANK_COUNT = 8
 GATE_BANKS = 2
 OWN_SLOTS = 1024
 GROUPS = [(a, a + BANK) for a in range(0, S - BANK, BANK)] + [(S - BANK, S - C), (S - C, S - HALF), (S - HALF, S)]
 REUSED = {6: 1, 7: 2}
-UNITS = [(0, 1024), (0, 2048), (1, 1024), (1, 2048), (2, 256), (2, 1280)]
+UNITS = [(0, 896, FIRST), (0, 2048, WIDE), (1, 1024, WIDE), (1, 2048, WIDE), (2, 256, WIDE), (2, 1280, WIDE)]
 TAPER = [(2304, 384), (2688, 256), (2944, 128)]
-PIECES = [(0, 0), (0, 768), (1, 512), (1, 768), (1, 0), (1, 256), (2, 0)]
-KEPT = (256, 512)
+PIECES = [(0, 0), (0, 640), (1, 512), (1, 768), (1, 0), (1, 256), (2, 0)]
+KEPT = 384
 TOKEN_CUTS = [0, 192, 608, 896, T]
 
 
@@ -53,6 +55,7 @@ def tile_moe_pre_lin_none_kernel(tc, xT, w, gate, offs, pos1, pos2, pos3, out):
     with ExitStack() as ctx:
         keep = ctx.enter_context(tc.tile_pool(name="keep", bufs=1))
         picked_pool = ctx.enter_context(tc.tile_pool(name="picked", bufs=1))
+        own_pool = ctx.enter_context(tc.tile_pool(name="own", bufs=1))
         psum = ctx.enter_context(tc.psum_pool(name="psum", bufs=1))
         gate_psum = ctx.enter_context(tc.psum_pool(name="gate_psum", bufs=GATE_BANKS))
 
@@ -72,7 +75,7 @@ def tile_moe_pre_lin_none_kernel(tc, xT, w, gate, offs, pos1, pos2, pos3, out):
         windows = {}
 
         def load_window(g, j):
-            window = keep.tile([P, T + SPARE], F32, name=f"window{g}{j}", tag=f"window{g % 2}{j}")
+            window = keep.tile([P, (T if g % 2 else FIRST) + SPARE], F32, name=f"window{g}{j}", tag=f"window{g % 2}{j}")
             rows = xT[g * K_PASS:(g + 1) * K_PASS, :].rearrange("(p j) t -> p j t", j=PACK)
             nc.sync.dma_start(window[:, 0:T], rows[:, j, :])
             windows[(g, j)] = window
@@ -91,48 +94,59 @@ def tile_moe_pre_lin_none_kernel(tc, xT, w, gate, offs, pos1, pos2, pos3, out):
         def new_codes(name, words):
             codes = keep.tile([P, words], U32, name=f"codes_{name}", align_bytes=64)
             scales = keep.tile([P, words], U8, name=f"scales_{name}", align_bytes=64)
-            return codes, scales
+            return codes, scales, name
 
         x_at = {}
         w_at = {}
         issued = set()
-        products = [
-            (i, g, s0, min(C, b - a)) for g in range(PASSES) for i, (a, b) in enumerate(GROUPS) for s0 in range(a, b, C)
-        ]
+
+        def passes_done(s0):
+            return len([1 for g in range(PASSES) if (g, s0) in issued])
+
+        def ready(g, s0):
+            return (g, s0) in x_at and (g, s0) not in issued and s0 // C * PASSES + g in w_at
+
+        def joined(g, s0):
+            s1 = s0 + HALF
+            if s0 % C or not ready(g, s1) or (passes_done(s0) == 0) != (passes_done(s1) == 0):
+                return False
+            return x_at[(g, s0)][3] == x_at[(g, s1)][3] and x_at[(g, s0)][2] + HALF == x_at[(g, s1)][2]
 
         def multiply():
-            for i, g, s0, n in products:
-                block = s0 // C * PASSES + g
-                ready = block in w_at and all((g, s) in x_at for s in range(s0, s0 + n, HALF))
-                if (g, s0) in issued or not ready or i not in accs:
-                    continue
-                a, b = GROUPS[i]
-                before = len([1 for gg, ss in issued if a <= ss < b])
-                total = len([1 for ii, gg, ss, nn in products if ii == i])
-                issued.add((g, s0))
-                w_codes, w_scales, wc = w_at[block]
-                x_codes, x_scales, xc = x_at[(g, s0)]
-                nc.tensor.matmul_mx(
-                    out=accs[i][:, s0 - a:s0 - a + n],
-                    lhsT=w_codes[:, wc:wc + N].bitcast(FP8X4),
-                    lhsT_scale=w_scales[:, wc:wc + N],
-                    rhs=x_codes[:, xc:xc + n].bitcast(FP8X4),
-                    rhs_scale=x_scales[:, xc:xc + n],
-                    start=(before == 0),
-                    stop=(before == total - 1),
-                )
-                if before == total - 1:
-                    if i == len(GROUPS) - 2:
-                        nc.vector.tensor_copy(y[:, a:b], accs[i][:])
-                    else:
-                        nc.scalar.copy(y[:, a:b], accs[i][:])
-                    for late, bank in REUSED.items():
-                        if bank == i:
-                            c, d = GROUPS[late]
-                            accs[late] = psum.tile([P, d - c], F32, name=f"late{late}", tag=f"acc{i}")
+            for g in range(PASSES):
+                for i, (a, b) in enumerate(GROUPS):
+                    for s0 in range(a, b, HALF):
+                        if i in accs and ready(g, s0):
+                            one_pass(i, a, b, g, s0, C if s0 + C <= b and joined(g, s0) else HALF)
+
+        def one_pass(i, a, b, g, s0, n):
+            before = sum([passes_done(s) for s in range(a, b, HALF)])
+            closes = before + n // HALF == PASSES * (b - a) // HALF
+            for s in range(s0, s0 + n, HALF):
+                issued.add((g, s))
+            w_codes, w_scales, wc = w_at[s0 // C * PASSES + g]
+            x_codes, x_scales, xc, x_name = x_at[(g, s0)]
+            nc.tensor.matmul_mx(
+                out=accs[i][:, s0 - a:s0 - a + n],
+                lhsT=w_codes[:, wc:wc + N].bitcast(FP8X4),
+                lhsT_scale=w_scales[:, wc:wc + N],
+                rhs=x_codes[:, xc:xc + n].bitcast(FP8X4),
+                rhs_scale=x_scales[:, xc:xc + n],
+                start=(before == 0),
+                stop=closes,
+            )
+            if closes:
+                if i == len(GROUPS) - 2:
+                    nc.vector.tensor_copy(y[:, a:b], accs[i][:])
+                else:
+                    nc.scalar.copy(y[:, a:b], accs[i][:])
+                for late, bank in REUSED.items():
+                    if bank == i:
+                        c, d = GROUPS[late]
+                        accs[late] = psum.tile([P, d - c], F32, name=f"late{late}", tag=f"acc{i}")
 
         def quantize(pair, first, source, slots, blocks):
-            codes, scales = pair
+            codes, scales, name = pair
             words = sum([n for g, s0, n in slots]) + len(blocks) * N
             nc.vector.quantize_mx(
                 out=codes[:, first:first + words].bitcast(FP8X4), scales=scales[:, first:first + words], in_=source
@@ -143,7 +157,7 @@ def tile_moe_pre_lin_none_kernel(tc, xT, w, gate, offs, pos1, pos2, pos3, out):
                 at = at + N
             for g, s0, n in slots:
                 for s in range(0, n, HALF):
-                    x_at[(g, s0 + s)] = (codes, scales, at + s)
+                    x_at[(g, s0 + s)] = (codes, scales, at + s, name)
                 at = at + n
             multiply()
 
@@ -156,7 +170,7 @@ def tile_moe_pre_lin_none_kernel(tc, xT, w, gate, offs, pos1, pos2, pos3, out):
             return picked
 
         def vector_gate(grouped, planes, s0, n):
-            width = min(n, BANK)
+            width = n // ((n + BANK - 1) // BANK)
             for first in range(0, n, width):
                 spread = gate_psum.tile([P, width], F32, name="spread")
                 for a in range(0, width, P):
@@ -170,11 +184,14 @@ def tile_moe_pre_lin_none_kernel(tc, xT, w, gate, offs, pos1, pos2, pos3, out):
                     MULT,
                 )
 
+        def gate_row(s0, n):
+            return first_gates[:, s0:s0 + n] if s0 < PIECE else gates[:, s0 - PIECE:s0 - PIECE + n]
+
         def pool_gate(grouped, planes, s0, n):
             nc.gpsimd.tensor_tensor(
                 grouped.rearrange("p (c i j) -> p c j i", i=RUN, j=PACK),
                 planes.rearrange("p j (c i) -> p c j i", i=RUN),
-                gates[:, s0:s0 + n].rearrange("p (c o i) -> p c o i", o=1, i=RUN).broadcast_to([P, n // RUN, PACK, RUN]),
+                gate_row(s0, n).rearrange("p (c o i) -> p c o i", o=1, i=RUN).broadcast_to([P, n // RUN, PACK, RUN]),
                 MULT,
             )
 
@@ -187,22 +204,22 @@ def tile_moe_pre_lin_none_kernel(tc, xT, w, gate, offs, pos1, pos2, pos3, out):
 
         def new_picked(u, n):
             place = u % RING
-            return picked_pool.tile([P, PACK, n], F32, name="picked", tag=f"picked{place}", offset=place * PLACE)
+            return picked_pool.tile([P, PACK, n], F32, name="picked", tag=f"picked{place}", offset=PLACES[place])
 
         def new_piece(k):
-            return keep.tile([P, PACK, PIECE], F32, name=f"piece{k}", tag=f"piece{k % 2}")
+            offset = 0 if k % 2 else PACK * (KEPT + PIECE) * 4
+            return own_pool.tile([P, PACK, PIECE], F32, name=f"piece{k}", tag=f"piece{k % 2}", offset=offset)
 
-        batch_words = BATCH * N + PIECE
-        pieces = {0: new_piece(0), 1: new_piece(1)}
-        kept = keep.tile([P, PACK, KEPT[1]], F32, name="kept")
-        handed = staging(1, batch_words * PACK)
-        first_unit = new_picked(0, WIDE)
+        opening = picked_pool.tile([P, PACK, PIECE], F32, name="opening", offset=PLACES[2])
+        kept = own_pool.tile([P, PACK, KEPT + PIECE], F32, name="kept", offset=0)
+        pieces = {0: opening[:], 1: kept[:, :, KEPT:]}
+        handed = staging(1, (HEAD_BATCH * N + PIECE) * PACK)
+        picked = new_picked(0, FIRST)
         for j in range(PACK):
             load_window(0, j)
-            vector_gather(pieces[0], 0, j, PIECES[0][1], PIECE)
-            vector_gather(kept, 0, j, KEPT[0], KEPT[1])
-            vector_gather(pieces[1], 0, j, PIECES[1][1], PIECE)
-            nc.scalar.activation(first_unit[:, j, :], tokens(0, j, UNITS[0][1], WIDE), COPY)
+            vector_gather(opening, 0, j, 0, PIECE)
+            vector_gather(kept, 0, j, PIECE, KEPT + PIECE)
+            nc.scalar.activation(picked[:, j, :], tokens(0, j, UNITS[0][1], FIRST), COPY)
             if j == 1:
                 gate_rows = keep.tile([P, P], F32, name="gate_rows")
                 nc.sync.dma_start(gate_rows[:], gate.rearrange("k (c p) -> (k c) p", p=P)[0:P, :])
@@ -210,51 +227,75 @@ def tile_moe_pre_lin_none_kernel(tc, xT, w, gate, offs, pos1, pos2, pos3, out):
                 nc.tensor.transpose(turned[:], gate_rows[:], identity[:])
                 gate_columns = keep.tile([P, S // P], F32, name="gate_columns")
                 nc.vector.tensor_copy(gate_columns[:], turned[:, 0:S // P])
-            if j * HEAD_BLOCKS < BATCH:
+            if j * HEAD_BLOCKS < HEAD_BATCH:
                 b0 = j * HEAD_BLOCKS
-                raw = picked_pool.tile([P, HEAD_BLOCKS, BLOCK], F32, name=f"early{j}", offset=PLACE + b0 * BLOCK * 4)
+                raw = picked_pool.tile([P, HEAD_BLOCKS, BLOCK], F32, name=f"early{j}", offset=PLACES[1] + b0 * BLOCK * 4)
                 nc.sync.dma_start(raw[:], w_blocks[:, b0:b0 + HEAD_BLOCKS, :])
                 pool_weights(handed[:, b0 * BLOCK:(b0 + HEAD_BLOCKS) * BLOCK], raw, HEAD_BLOCKS)
-        gates = keep.tile([P, OWN_SLOTS], F32, name="gates")
-        nc.sync.dma_start(gates[:], gate[0:P, 0:OWN_SLOTS])
-        raws = {1: load_blocks(BATCH, BATCH, "raw1")}
-        for j in range(PACK):
+        first_gates = keep.tile([P, PIECE], F32, name="first_gates")
+        nc.sync.dma_start(first_gates[:], gate[0:P, 0:PIECE])
+        load_window(1, 0)
+        raws = {1: load_blocks(HEAD_BATCH, BATCH, "raw1")}
+        load_window(1, 1)
+        gates = keep.tile([P, OWN_SLOTS - PIECE], F32, name="gates")
+        nc.sync.dma_start(gates[:], gate[0:P, PIECE:OWN_SLOTS])
+        for j in range(2, PACK):
             load_window(1, j)
-        raws[2] = load_blocks(2 * BATCH, BATCH, "raw0")
+        raws[2] = load_blocks(HEAD_BATCH + BATCH, BATCH, "raw0")
         lists = []
         for r, pos in enumerate((pos1, pos2, pos3)):
             tile = keep.tile([P, T // LIST], U16, name=f"pos{r}")
             nc.sync.dma_start(tile[:], pos)
             lists.append(tile)
 
-        pool_gate(handed[:, BATCH * BLOCK:], pieces[0][:], PIECES[0][1], PIECE)
-        grouped = staging(0, PIECE * PACK)
-        vector_gate(grouped, kept[:, :, PIECE:2 * PIECE], KEPT[0] + PIECE, PIECE)
-        quantize(new_codes("kept", PIECE), 0, grouped[:], [(0, KEPT[0] + PIECE, PIECE)], [])
-        quantize(new_codes("batch0", batch_words), 0, handed[:], [(0, PIECES[0][1], PIECE)], list(range(BATCH)))
+        def gather_piece(k, planes):
+            for j in planes:
+                vector_gather(pieces[k], PIECES[k][0], j, PIECES[k][1], PIECE)
 
-        picked = first_unit
+        pool_gate(handed[:, HEAD_BATCH * BLOCK:], pieces[0], 0, PIECE)
+        grouped = staging(0, KEPT * PACK)
+        vector_gate(grouped, kept[:, :, 0:KEPT], PIECE, KEPT)
+        pieces[2] = new_piece(2)[:]
+        gather_piece(2, [0])
+        quantize(new_codes("kept", KEPT), 0, grouped[:], [(0, PIECE, KEPT)], [])
+        quantize(new_codes("batch0", HEAD_BATCH * N + PIECE), 0, handed[:], [(0, 0, PIECE)], list(range(HEAD_BATCH)))
+
+        def pool_batch(k):
+            handed = staging(k + 1, (BATCH * N + PIECE) * PACK)
+            pool_weights(handed[:, 0:BATCH * BLOCK], raws[k], BATCH)
+            if k + 2 <= len(UNITS):
+                raws[k + 2] = load_blocks(HEAD_BATCH + (k + 1) * BATCH, BATCH, f"raw{k % 2}")
+            pool_gate(handed[:, BATCH * BLOCK:], pieces[k], PIECES[k][1], PIECE)
+            codes = new_codes(f"batch{k}", BATCH * N + PIECE)
+            b0 = HEAD_BATCH + (k - 1) * BATCH
+            cut = BATCH - 1
+            front = lambda: quantize(codes, 0, handed[:, 0:cut * BLOCK], [], list(range(b0, b0 + cut)))
+            back = lambda: quantize(codes, cut * N, handed[:, cut * BLOCK:], [PIECES[k] + (PIECE,)], [b0 + cut])
+            return front, back
+
+        def quantize_unit(u, grouped):
+            g, s0, n = UNITS[u]
+            codes = new_codes(f"unit{u}", n)
+            quantize(codes, 0, grouped[:, 0:WIDE * PACK], [(g, s0, WIDE)], [])
+            if n > WIDE:
+                quantize(codes, WIDE, grouped[:, WIDE * PACK:n * PACK], [(g, s0 + WIDE, n - WIDE)], [])
+
         for k in range(1, len(UNITS)):
             if k == 2:
                 for j in range(PACK):
                     load_window(2, j)
             ahead = scalar_unit(new_picked(k, WIDE), UNITS[k][0], UNITS[k][1], WIDE)
-            handed = staging(k + 1, batch_words * PACK)
-            pool_weights(handed[:, 0:BATCH * BLOCK], raws[k], BATCH)
-            if k + 2 < len(UNITS):
-                raws[k + 2] = load_blocks((k + 2) * BATCH, BATCH, f"raw{k % 2}")
-            pool_gate(handed[:, BATCH * BLOCK:], pieces[k][:], PIECES[k][1], PIECE)
-            pieces[k + 1] = new_piece(k + 1)
-            g, s0 = PIECES[k + 1]
-            for j in range(PACK // 2):
-                vector_gather(pieces[k + 1], g, j, s0, PIECE)
-            grouped = staging(k, WIDE * PACK)
-            vector_gate(grouped, picked, UNITS[k - 1][1], WIDE)
-            for j in range(PACK // 2, PACK):
-                vector_gather(pieces[k + 1], g, j, s0, PIECE)
-            quantize(new_codes(f"unit{k - 1}", WIDE), 0, grouped[:], [UNITS[k - 1] + (WIDE,)], [])
-            blocks = list(range(k * BATCH, (k + 1) * BATCH))
-            quantize(new_codes(f"batch{k}", batch_words), 0, handed[:], [PIECES[k] + (PIECE,)], blocks)
+            front, back = pool_batch(k)
+            if k > 1:
+                pieces[k + 1] = new_piece(k + 1)[:]
+            gather_piece(k + 1, [1] if k == 1 else [0, 1])
+            g, s0, n = UNITS[k - 1]
+            grouped = staging(k, n * PACK)
+            vector_gate(grouped, picked, s0, n)
+            gather_piece(k + 1, [2] if k == len(UNITS) - 1 else [2, 3])
+            front()
+            quantize_unit(k - 1, grouped)
+            back()
             picked = ahead
 
         last = PASSES - 1
@@ -263,15 +304,15 @@ def tile_moe_pre_lin_none_kernel(tc, xT, w, gate, offs, pos1, pos2, pos3, out):
         taper_a = scalar_unit(new_picked(k, n_a), last, s_a, n_a)
         taper_b = scalar_unit(keep.tile([P, PACK, n_b], F32, name="taper_b", tag="window13"), last, s_b, n_b)
         taper_c = scalar_unit(keep.tile([P, PACK, n_c], F32, name="taper_c", tag="raw1"), last, s_c, n_c)
-        handed = staging(k + 1, 2 * PIECE * PACK)
-        pool_gate(handed[:, 0:PIECE * PACK], kept[:, :, 0:PIECE], KEPT[0], PIECE)
-        pool_gate(handed[:, PIECE * PACK:], pieces[k][:], PIECES[k][1], PIECE)
+        gather_piece(k, [3])
+        front, back = pool_batch(k)
         grouped = staging(k, (WIDE + n_a) * PACK)
         vector_gate(grouped[:, 0:WIDE * PACK], picked, UNITS[k - 1][1], WIDE)
         vector_gate(grouped[:, WIDE * PACK:], taper_a, s_a, n_a)
         taper_codes = new_codes("taper", n_a + n_b + n_c)
-        quantize(new_codes(f"unit{k - 1}", WIDE), 0, grouped[:, 0:WIDE * PACK], [UNITS[k - 1] + (WIDE,)], [])
-        quantize(new_codes(f"batch{k}", 2 * PIECE), 0, handed[:], [(0, KEPT[0], PIECE), PIECES[k] + (PIECE,)], [])
+        front()
+        quantize_unit(k - 1, grouped)
+        back()
         quantize(taper_codes, 0, grouped[:, WIDE * PACK:], [(last, s_a, n_a)], [])
         grouped = staging(k + 1, (n_b + n_c) * PACK)
         vector_gate(grouped[:, 0:n_b * PACK], taper_b, s_b, n_b)

@@ -20,42 +20,50 @@ P = 128
 PACK = 4
 K_PASS = P * PACK
 PASSES = K // K_PASS
+LAST = PASSES - 1
 LIST = 16
+WORD = 4
+BLOCK = PACK * N
+HALF = C // 2
+BANK = 512
+RUN = 4
 
 FLOPS = 2 * K * S * N
 BYTES = 4 * (K * T + E * K * N + S + N * T) + 2 * (S + 3 * T)
 
-FIRST = 1152
-SPARE = 8
-RUN = 4
-BANK = 512
-HALF = C // 2
-WIDE = 1024
 PIECE = 256
-BATCH = 5
-HEAD_BATCH = 6
-HEAD_BLOCKS = 2
-BLOCK = PACK * N
-RING = 3
-PLACES = [0, PACK * FIRST * 4, PACK * (FIRST + WIDE) * 4]
-BANK_COUNT = 8
-GATE_BANKS = 2
-OWN_SLOTS = 1024
-GROUPS = [(a, a + BANK) for a in range(0, S - BANK, BANK)] + [(S - BANK, S - C), (S - C, S - HALF), (S - HALF, S)]
-REUSED = {6: 1, 7: 2}
-UNITS = [(0, 896, FIRST), (0, 2048, WIDE), (1, 1024, WIDE), (1, 2048, WIDE), (2, 256, WIDE), (2, 1280, WIDE)]
-TAPER = [(2304, 384), (2688, 256), (2944, 128)]
-PIECES = [(0, 0), (0, 640), (1, 512), (1, 768), (1, 0), (1, 256), (2, 0)]
 KEPT = 384
+HEAD = PIECE + KEPT + PIECE
+OWN = 4 * PIECE
+WIDE = 1024
+FIRST = S - HEAD - WIDE
+PIECES = [(0, 0), (0, PIECE + KEPT), (1, 2 * PIECE), (1, 3 * PIECE), (1, 0), (1, PIECE), (LAST, 0)]
+TAPER = [(S - BANK - C - HALF, BANK), (S - C - HALF, C), (S - HALF, HALF)]
+UNITS = [(0, HEAD, FIRST), (0, HEAD + FIRST, WIDE), (1, OWN, WIDE), (1, OWN + WIDE, WIDE), (LAST, PIECE, WIDE)]
+UNITS = UNITS + [(LAST, PIECE + WIDE, TAPER[0][0] - PIECE - WIDE)]
+STEPS = len(UNITS)
+BATCHES = [6, 5, 5, 5, 5, 4, 5, 1]
+EARLY = 2
+SPARE = 8
+RING = 3
+PLACES = [0, PACK * FIRST * WORD, PACK * (FIRST + WIDE) * WORD]
+
+GATE_BANKS = 2
+SUM_BANKS = 6
+GROUPS = [(a, a + BANK) for a in range(0, S - BANK, BANK)] + [(S - BANK, S - C), (S - C, S - HALF), (S - HALF, S)]
+REUSED = {1: 6, 2: 7}
+BY_VECTOR = (4, 6)
 TOKEN_CUTS = [0, 192, 608, 896, T]
+
+assert sum(BATCHES) == E * PASSES
 
 
 def tile_moe_pre_lin_none_kernel(tc, xT, w, gate, offs, pos1, pos2, pos3, out):
     nc = tc.nc
     with ExitStack() as ctx:
         keep = ctx.enter_context(tc.tile_pool(name="keep", bufs=1))
-        picked_pool = ctx.enter_context(tc.tile_pool(name="picked", bufs=1))
-        own_pool = ctx.enter_context(tc.tile_pool(name="own", bufs=1))
+        unit_pool = ctx.enter_context(tc.tile_pool(name="picked", bufs=1))
+        piece_pool = ctx.enter_context(tc.tile_pool(name="own", bufs=1))
         psum = ctx.enter_context(tc.psum_pool(name="psum", bufs=1))
         gate_psum = ctx.enter_context(tc.psum_pool(name="gate_psum", bufs=GATE_BANKS))
 
@@ -63,33 +71,34 @@ def tile_moe_pre_lin_none_kernel(tc, xT, w, gate, offs, pos1, pos2, pos3, out):
         nc.sync.dma_start(offsets[:], offs)
         identity = keep.tile([P, P], F32, name="identity")
         make_identity(nc, identity[:])
-        cold = keep.tile([P, 8], F32, name="cold")
+        cold = keep.tile([P, SPARE], F32, name="cold")
         nc.vector.memset(cold[:], 0.0)
-        warm = keep.tile([P, 8], F32, name="warm")
+        warm = keep.tile([P, SPARE], F32, name="warm")
         nc.scalar.activation(warm[:], cold[:], COPY)
 
         w_blocks = w.rearrange("e (g p j) n -> p (e g) (j n)", p=P, j=PACK)
-        sum_banks = BANK_COUNT - GATE_BANKS
-        accs = {i: psum.tile([P, b - a], F32, name=f"acc{i}") for i, (a, b) in enumerate(GROUPS[:sum_banks])}
+        sums = {i: psum.tile([P, b - a], F32, name=f"acc{i}") for i, (a, b) in enumerate(GROUPS[:SUM_BANKS])}
         y = keep.tile([P, S], F32, name="y")
         windows = {}
 
         def load_window(g, j):
-            window = keep.tile([P, (T if g % 2 else FIRST) + SPARE], F32, name=f"window{g}{j}", tag=f"window{g % 2}{j}")
+            columns = (T if g % 2 else FIRST) + SPARE
+            window = keep.tile([P, columns], F32, name=f"window{g}{j}", tag=f"window{g % 2}{j}")
             rows = xT[g * K_PASS:(g + 1) * K_PASS, :].rearrange("(p j) t -> p j t", j=PACK)
             nc.sync.dma_start(window[:, 0:T], rows[:, j, :])
             windows[(g, j)] = window
 
-        def load_blocks(b0, blocks, tag):
-            raw = keep.tile([P, blocks, BLOCK], F32, name=f"raw{b0}", tag=tag)
-            nc.sync.dma_start(raw[:], w_blocks[:, b0:b0 + blocks, :])
+        def load_batches(first, end):
+            b0, b1 = sum(BATCHES[:first]), sum(BATCHES[:end])
+            raw = keep.tile([P, b1 - b0, BLOCK], F32, name=f"raw{b0}", tag=f"raw{first % 2}")
+            nc.sync.dma_start(raw[:], w_blocks[:, b0:b1, :])
             return raw
 
         def tokens(g, j, s0, n):
             return windows[(g, j)][:].indirect(offsets[:, s0 // LIST:(s0 + n) // LIST])
 
-        def staging(which, columns):
-            return keep.tile([P, columns], BF16, name="staging", tag=f"staging{which % 2}", align_bytes=64)
+        def staging(k, columns):
+            return keep.tile([P, columns], BF16, name="staging", tag=f"staging{k % 2}", align_bytes=64)
 
         def new_codes(name, words):
             codes = keep.tile([P, words], U32, name=f"codes_{name}", align_bytes=64)
@@ -99,6 +108,7 @@ def tile_moe_pre_lin_none_kernel(tc, xT, w, gate, offs, pos1, pos2, pos3, out):
         x_at = {}
         w_at = {}
         issued = set()
+        closed = []
 
         def passes_done(s0):
             return len([1 for g in range(PASSES) if (g, s0) in issued])
@@ -110,116 +120,125 @@ def tile_moe_pre_lin_none_kernel(tc, xT, w, gate, offs, pos1, pos2, pos3, out):
             s1 = s0 + HALF
             if s0 % C or not ready(g, s1) or (passes_done(s0) == 0) != (passes_done(s1) == 0):
                 return False
-            return x_at[(g, s0)][3] == x_at[(g, s1)][3] and x_at[(g, s0)][2] + HALF == x_at[(g, s1)][2]
+            (tiles0, at0), (tiles1, at1) = x_at[(g, s0)], x_at[(g, s1)]
+            return tiles0[2] == tiles1[2] and at0 + HALF == at1
 
         def multiply():
             for g in range(PASSES):
                 for i, (a, b) in enumerate(GROUPS):
                     for s0 in range(a, b, HALF):
-                        if i in accs and ready(g, s0):
-                            one_pass(i, a, b, g, s0, C if s0 + C <= b and joined(g, s0) else HALF)
+                        if i in sums and ready(g, s0):
+                            one_pass(i, g, s0, C if s0 + C <= b and joined(g, s0) else HALF)
 
-        def one_pass(i, a, b, g, s0, n):
+        def one_pass(i, g, s0, n):
+            a, b = GROUPS[i]
             before = sum([passes_done(s) for s in range(a, b, HALF)])
             closes = before + n // HALF == PASSES * (b - a) // HALF
             for s in range(s0, s0 + n, HALF):
                 issued.add((g, s))
-            w_codes, w_scales, wc = w_at[s0 // C * PASSES + g]
-            x_codes, x_scales, xc, x_name = x_at[(g, s0)]
+            w_tiles, w_first = w_at[s0 // C * PASSES + g]
+            x_tiles, x_first = x_at[(g, s0)]
             nc.tensor.matmul_mx(
-                out=accs[i][:, s0 - a:s0 - a + n],
-                lhsT=w_codes[:, wc:wc + N].bitcast(FP8X4),
-                lhsT_scale=w_scales[:, wc:wc + N],
-                rhs=x_codes[:, xc:xc + n].bitcast(FP8X4),
-                rhs_scale=x_scales[:, xc:xc + n],
+                out=sums[i][:, s0 - a:s0 - a + n],
+                lhsT=w_tiles[0][:, w_first:w_first + N].bitcast(FP8X4),
+                lhsT_scale=w_tiles[1][:, w_first:w_first + N],
+                rhs=x_tiles[0][:, x_first:x_first + n].bitcast(FP8X4),
+                rhs_scale=x_tiles[1][:, x_first:x_first + n],
                 start=(before == 0),
                 stop=closes,
             )
-            if closes:
-                if i == len(GROUPS) - 2:
-                    nc.vector.tensor_copy(y[:, a:b], accs[i][:])
-                else:
-                    nc.scalar.copy(y[:, a:b], accs[i][:])
-                for late, bank in REUSED.items():
-                    if bank == i:
-                        c, d = GROUPS[late]
-                        accs[late] = psum.tile([P, d - c], F32, name=f"late{late}", tag=f"acc{i}")
+            if closes and i in BY_VECTOR:
+                closed.append(i)
+            elif closes:
+                nc.scalar.copy(y[:, a:b], sums[i][:])
+                if i in REUSED:
+                    c, d = GROUPS[REUSED[i]]
+                    sums[REUSED[i]] = psum.tile([P, d - c], F32, name=f"late{REUSED[i]}", tag=f"acc{i}")
 
-        def quantize(pair, first, source, slots, blocks):
-            codes, scales, name = pair
+        def quantize(tiles, first, source, slots, blocks):
+            codes, scales, name = tiles
             words = sum([n for g, s0, n in slots]) + len(blocks) * N
             nc.vector.quantize_mx(
                 out=codes[:, first:first + words].bitcast(FP8X4), scales=scales[:, first:first + words], in_=source
             )
             at = first
             for b in blocks:
-                w_at[b] = (codes, scales, at)
+                w_at[b] = (tiles, at)
                 at = at + N
             for g, s0, n in slots:
                 for s in range(0, n, HALF):
-                    x_at[(g, s0 + s)] = (codes, scales, at + s, name)
+                    x_at[(g, s0 + s)] = (tiles, at + s)
                 at = at + n
             multiply()
 
         def vector_gather(planes, g, j, s0, n):
             nc.vector.tensor_copy(planes[:, j, :], tokens(g, j, s0, n))
 
-        def scalar_unit(picked, g, s0, n):
+        def scalar_gather(planes, g, j, s0, n):
+            nc.scalar.activation(planes[:, j, :], tokens(g, j, s0, n), COPY)
+
+        def scalar_unit(planes, g, s0, n):
             for j in range(PACK):
-                nc.scalar.activation(picked[:, j, :], tokens(g, j, s0, n), COPY)
-            return picked
+                scalar_gather(planes, g, j, s0, n)
+            return planes
+
+        def side_by_side(grouped):
+            return grouped.rearrange("p (c i j) -> p c j i", i=RUN, j=PACK)
+
+        def in_runs(planes):
+            return planes.rearrange("p j (c i) -> p c j i", i=RUN)
+
+        def for_all_planes(row, n):
+            return row.rearrange("p (c o i) -> p c o i", o=1, i=RUN).broadcast_to([P, n // RUN, PACK, RUN])
 
         def vector_gate(grouped, planes, s0, n):
-            width = n // ((n + BANK - 1) // BANK)
-            for first in range(0, n, width):
+            stride = n // 3 if n == FIRST else BANK
+            for first in range(0, n, stride):
+                width = min(stride, n - first)
                 spread = gate_psum.tile([P, width], F32, name="spread")
                 for a in range(0, width, P):
                     c = (s0 + first + a) // P
                     nc.tensor.transpose(spread[:, a:a + P], gate_columns[:, c:c + 1].to_broadcast([P, P]), identity[:])
-                gate_runs = spread[:].rearrange("p (c o i) -> p c o i", o=1, i=RUN)
                 nc.vector.tensor_tensor(
-                    grouped[:, first * PACK:(first + width) * PACK].rearrange("p (c i j) -> p c j i", i=RUN, j=PACK),
-                    planes[:, :, first:first + width].rearrange("p j (c i) -> p c j i", i=RUN),
-                    gate_runs.broadcast_to([P, width // RUN, PACK, RUN]),
+                    side_by_side(grouped[:, first * PACK:(first + width) * PACK]),
+                    in_runs(planes[:, :, first:first + width]),
+                    for_all_planes(spread[:], width),
                     MULT,
                 )
 
-        def gate_row(s0, n):
-            return first_gates[:, s0:s0 + n] if s0 < PIECE else gates[:, s0 - PIECE:s0 - PIECE + n]
+        def gpsimd_gate(grouped, k):
+            s0 = PIECES[k][1]
+            row = first_gates[:, s0:s0 + PIECE] if s0 < PIECE else gates[:, s0 - PIECE:s0]
+            nc.gpsimd.tensor_tensor(side_by_side(grouped), in_runs(pieces[k]), for_all_planes(row, PIECE), MULT)
 
-        def pool_gate(grouped, planes, s0, n):
-            nc.gpsimd.tensor_tensor(
-                grouped.rearrange("p (c i j) -> p c j i", i=RUN, j=PACK),
-                planes.rearrange("p j (c i) -> p c j i", i=RUN),
-                gate_row(s0, n).rearrange("p (c o i) -> p c o i", o=1, i=RUN).broadcast_to([P, n // RUN, PACK, RUN]),
-                MULT,
-            )
-
-        def pool_weights(grouped, raw, blocks):
-            nc.gpsimd.tensor_scalar(
+        def gpsimd_weights(grouped, raw, blocks):
+            nc.gpsimd.tensor_copy(
                 grouped.rearrange("p (b n j) -> p b n j", b=blocks, j=PACK),
-                raw[:].rearrange("p b (j n) -> p b n j", j=PACK),
-                1.0, 0.0, MULT, ADD,
+                raw.rearrange("p b (j n) -> p b n j", j=PACK),
             )
 
-        def new_picked(u, n):
+        def new_unit(u, n):
             place = u % RING
-            return picked_pool.tile([P, PACK, n], F32, name="picked", tag=f"picked{place}", offset=PLACES[place])
+            return unit_pool.tile([P, PACK, n], F32, name="picked", tag=f"picked{place}", offset=PLACES[place])
 
         def new_piece(k):
-            offset = 0 if k % 2 else PACK * (KEPT + PIECE) * 4
-            return own_pool.tile([P, PACK, PIECE], F32, name=f"piece{k}", tag=f"piece{k % 2}", offset=offset)
+            offset = 0 if k % 2 else PACK * (KEPT + PIECE) * WORD
+            return piece_pool.tile([P, PACK, PIECE], F32, name=f"piece{k}", tag=f"piece{k % 2}", offset=offset)
 
-        opening = picked_pool.tile([P, PACK, PIECE], F32, name="opening", offset=PLACES[2])
-        kept = own_pool.tile([P, PACK, KEPT + PIECE], F32, name="kept", offset=0)
+        def gather_piece(k, planes):
+            for j in planes:
+                vector_gather(pieces[k], PIECES[k][0], j, PIECES[k][1], PIECE)
+
+        opening = unit_pool.tile([P, PACK, PIECE], F32, name="opening", offset=PLACES[2])
+        kept = piece_pool.tile([P, PACK, KEPT + PIECE], F32, name="kept", offset=0)
         pieces = {0: opening[:], 1: kept[:, :, KEPT:]}
-        handed = staging(1, (HEAD_BATCH * N + PIECE) * PACK)
-        picked = new_picked(0, FIRST)
+        handed = staging(1, (BATCHES[0] * N + PIECE) * PACK)
+        picked = new_unit(0, FIRST)
         for j in range(PACK):
             load_window(0, j)
-            vector_gather(opening, 0, j, 0, PIECE)
+            gather_piece(0, [j])
             vector_gather(kept, 0, j, PIECE, KEPT + PIECE)
-            nc.scalar.activation(picked[:, j, :], tokens(0, j, UNITS[0][1], FIRST), COPY)
+            scalar_gather(picked, 0, j, HEAD, FIRST)
             if j == 1:
                 gate_rows = keep.tile([P, P], F32, name="gate_rows")
                 nc.sync.dma_start(gate_rows[:], gate.rearrange("k (c p) -> (k c) p", p=P)[0:P, :])
@@ -227,108 +246,108 @@ def tile_moe_pre_lin_none_kernel(tc, xT, w, gate, offs, pos1, pos2, pos3, out):
                 nc.tensor.transpose(turned[:], gate_rows[:], identity[:])
                 gate_columns = keep.tile([P, S // P], F32, name="gate_columns")
                 nc.vector.tensor_copy(gate_columns[:], turned[:, 0:S // P])
-            if j * HEAD_BLOCKS < HEAD_BATCH:
-                b0 = j * HEAD_BLOCKS
-                raw = picked_pool.tile([P, HEAD_BLOCKS, BLOCK], F32, name=f"early{j}", offset=PLACES[1] + b0 * BLOCK * 4)
-                nc.sync.dma_start(raw[:], w_blocks[:, b0:b0 + HEAD_BLOCKS, :])
-                pool_weights(handed[:, b0 * BLOCK:(b0 + HEAD_BLOCKS) * BLOCK], raw, HEAD_BLOCKS)
+            if j * EARLY < BATCHES[0]:
+                b0 = j * EARLY
+                raw = unit_pool.tile([P, EARLY, BLOCK], F32, name=f"early{j}", offset=PLACES[1] + b0 * BLOCK * WORD)
+                nc.sync.dma_start(raw[:], w_blocks[:, b0:b0 + EARLY, :])
+                gpsimd_weights(handed[:, b0 * BLOCK:(b0 + EARLY) * BLOCK], raw[:], EARLY)
         first_gates = keep.tile([P, PIECE], F32, name="first_gates")
         nc.sync.dma_start(first_gates[:], gate[0:P, 0:PIECE])
         load_window(1, 0)
-        raws = {1: load_blocks(HEAD_BATCH, BATCH, "raw1")}
+        raws = {1: load_batches(1, 2)}
         load_window(1, 1)
-        gates = keep.tile([P, OWN_SLOTS - PIECE], F32, name="gates")
-        nc.sync.dma_start(gates[:], gate[0:P, PIECE:OWN_SLOTS])
+        gates = keep.tile([P, OWN - PIECE], F32, name="gates")
+        nc.sync.dma_start(gates[:], gate[0:P, PIECE:OWN])
         for j in range(2, PACK):
             load_window(1, j)
-        raws[2] = load_blocks(HEAD_BATCH + BATCH, BATCH, "raw0")
+        raws[2] = load_batches(2, 3)
         lists = []
         for r, pos in enumerate((pos1, pos2, pos3)):
             tile = keep.tile([P, T // LIST], U16, name=f"pos{r}")
             nc.sync.dma_start(tile[:], pos)
             lists.append(tile)
 
-        def gather_piece(k, planes):
-            for j in planes:
-                vector_gather(pieces[k], PIECES[k][0], j, PIECES[k][1], PIECE)
-
-        pool_gate(handed[:, HEAD_BATCH * BLOCK:], pieces[0], 0, PIECE)
+        gpsimd_gate(handed[:, BATCHES[0] * BLOCK:], 0)
         grouped = staging(0, KEPT * PACK)
         vector_gate(grouped, kept[:, :, 0:KEPT], PIECE, KEPT)
         pieces[2] = new_piece(2)[:]
         gather_piece(2, [0])
         quantize(new_codes("kept", KEPT), 0, grouped[:], [(0, PIECE, KEPT)], [])
-        quantize(new_codes("batch0", HEAD_BATCH * N + PIECE), 0, handed[:], [(0, 0, PIECE)], list(range(HEAD_BATCH)))
+        quantize(new_codes("batch0", BATCHES[0] * N + PIECE), 0, handed[:], [(0, 0, PIECE)], list(range(BATCHES[0])))
 
-        def pool_batch(k):
-            handed = staging(k + 1, (BATCH * N + PIECE) * PACK)
-            pool_weights(handed[:, 0:BATCH * BLOCK], raws[k], BATCH)
-            if k + 2 <= len(UNITS):
-                raws[k + 2] = load_blocks(HEAD_BATCH + (k + 1) * BATCH, BATCH, f"raw{k % 2}")
-            pool_gate(handed[:, BATCH * BLOCK:], pieces[k], PIECES[k][1], PIECE)
-            codes = new_codes(f"batch{k}", BATCH * N + PIECE)
-            b0 = HEAD_BATCH + (k - 1) * BATCH
-            cut = BATCH - 1
-            front = lambda: quantize(codes, 0, handed[:, 0:cut * BLOCK], [], list(range(b0, b0 + cut)))
-            back = lambda: quantize(codes, cut * N, handed[:, cut * BLOCK:], [PIECES[k] + (PIECE,)], [b0 + cut])
-            return front, back
+        def gpsimd_batch(k):
+            blocks = BATCHES[k]
+            filled = staging(k + 1, (blocks * N + PIECE) * PACK)
+            gpsimd_weights(filled[:, 0:blocks * BLOCK], raws[k][:, 0:blocks, :], blocks)
+            if k + 2 <= STEPS:
+                raws[k + 2] = load_batches(k + 2, k + 3 if k + 2 < STEPS else len(BATCHES))
+            gpsimd_gate(filled[:, blocks * BLOCK:], k)
+            tiles = new_codes(f"batch{k}", blocks * N + PIECE)
+            b0 = sum(BATCHES[:k])
+            cut = blocks - 1
+            return (
+                lambda: quantize(tiles, 0, filled[:, 0:cut * BLOCK], [], list(range(b0, b0 + cut))),
+                lambda: quantize(tiles, cut * N, filled[:, cut * BLOCK:], [PIECES[k] + (PIECE,)], [b0 + cut]),
+            )
 
-        def quantize_unit(u, grouped):
-            g, s0, n = UNITS[u]
-            codes = new_codes(f"unit{u}", n)
-            quantize(codes, 0, grouped[:, 0:WIDE * PACK], [(g, s0, WIDE)], [])
-            if n > WIDE:
-                quantize(codes, WIDE, grouped[:, WIDE * PACK:n * PACK], [(g, s0 + WIDE, n - WIDE)], [])
-
-        for k in range(1, len(UNITS)):
+        for k in range(1, STEPS):
             if k == 2:
                 for j in range(PACK):
-                    load_window(2, j)
-            ahead = scalar_unit(new_picked(k, WIDE), UNITS[k][0], UNITS[k][1], WIDE)
-            front, back = pool_batch(k)
+                    load_window(LAST, j)
+            ahead = scalar_unit(new_unit(k, UNITS[k][2]), *UNITS[k])
+            quantize_front, quantize_back = gpsimd_batch(k)
             if k > 1:
                 pieces[k + 1] = new_piece(k + 1)[:]
             gather_piece(k + 1, [1] if k == 1 else [0, 1])
             g, s0, n = UNITS[k - 1]
             grouped = staging(k, n * PACK)
             vector_gate(grouped, picked, s0, n)
-            gather_piece(k + 1, [2] if k == len(UNITS) - 1 else [2, 3])
-            front()
-            quantize_unit(k - 1, grouped)
-            back()
+            gather_piece(k + 1, [2] if k == STEPS - 1 else [2, 3])
+            quantize_front()
+            tiles = new_codes(f"unit{k - 1}", n)
+            quantize(tiles, 0, grouped[:, 0:WIDE * PACK], [(g, s0, WIDE)], [])
+            if n > WIDE:
+                quantize(tiles, WIDE, grouped[:, WIDE * PACK:n * PACK], [(g, s0 + WIDE, n - WIDE)], [])
+            quantize_back()
             picked = ahead
 
-        last = PASSES - 1
-        k = len(UNITS)
         (s_a, n_a), (s_b, n_b), (s_c, n_c) = TAPER
-        taper_a = scalar_unit(new_picked(k, n_a), last, s_a, n_a)
-        taper_b = scalar_unit(keep.tile([P, PACK, n_b], F32, name="taper_b", tag="window13"), last, s_b, n_b)
-        taper_c = scalar_unit(keep.tile([P, PACK, n_c], F32, name="taper_c", tag="raw1"), last, s_c, n_c)
-        gather_piece(k, [3])
-        front, back = pool_batch(k)
-        grouped = staging(k, (WIDE + n_a) * PACK)
-        vector_gate(grouped[:, 0:WIDE * PACK], picked, UNITS[k - 1][1], WIDE)
-        vector_gate(grouped[:, WIDE * PACK:], taper_a, s_a, n_a)
-        taper_codes = new_codes("taper", n_a + n_b + n_c)
-        front()
-        quantize_unit(k - 1, grouped)
-        back()
-        quantize(taper_codes, 0, grouped[:, WIDE * PACK:], [(last, s_a, n_a)], [])
-        grouped = staging(k + 1, (n_b + n_c) * PACK)
-        vector_gate(grouped[:, 0:n_b * PACK], taper_b, s_b, n_b)
-        vector_gate(grouped[:, n_b * PACK:], taper_c, s_c, n_c)
-        quantize(taper_codes, n_a, grouped[:, 0:n_b * PACK], [(last, s_b, n_b)], [])
-        quantize(taper_codes, n_a + n_b, grouped[:, n_b * PACK:], [(last, s_c, n_c)], [])
+        taper_a = scalar_unit(new_unit(STEPS, n_a), LAST, s_a, n_a)
+        taper_b = scalar_unit(keep.tile([P, PACK, n_b], F32, name="taper_b", tag="window13"), LAST, s_b, n_b)
+        taper_c = keep.tile([P, PACK, n_c], F32, name="taper_c", tag="raw1")
+        for j in range(PACK - 1):
+            scalar_gather(taper_c, LAST, j, s_c, n_c)
+        gather_piece(STEPS, [PACK - 1])
+        quantize_front, quantize_back = gpsimd_batch(STEPS)
+        g, s0, n = UNITS[-1]
+        grouped = staging(STEPS, (n + n_a) * PACK)
+        vector_gate(grouped[:, 0:n * PACK], picked, s0, n)
+        vector_gate(grouped[:, n * PACK:], taper_a, s_a, n_a)
+        tiles = new_codes("taper", S - s0)
+        quantize_front()
+        quantize(tiles, 0, grouped[:, 0:WIDE * PACK], [(g, s0, WIDE)], [])
+        quantize_back()
+        quantize(tiles, WIDE, grouped[:, WIDE * PACK:], [(g, s0 + WIDE, n + n_a - WIDE)], [])
 
-        first = keep.tile([P, T], F32, name="first", tag="window10")
+        handed = staging(STEPS, BATCHES[-1] * BLOCK)
+        gpsimd_weights(handed[:], raws[STEPS][:, BATCHES[STEPS]:, :], BATCHES[-1])
+        grouped = staging(STEPS + 1, (n_b + n_c) * PACK)
+        last_blocks = list(range(sum(BATCHES[:-1]), sum(BATCHES)))
+        vector_gather(taper_c, LAST, PACK - 1, s_c, n_c)
+        vector_gate(grouped[:, 0:n_b * PACK], taper_b, s_b, n_b)
+        quantize(new_codes("last_blocks", BATCHES[-1] * N), 0, handed[:], [], last_blocks)
+        vector_gate(grouped[:, n_b * PACK:], taper_c, s_c, n_c)
+        quantize(tiles, s_b - s0, grouped[:, 0:n_b * PACK], [(g, s_b, n_b)], [])
+        quantize(tiles, s_c - s0, grouped[:, n_b * PACK:], [(g, s_c, n_c)], [])
+        for i in closed:
+            nc.vector.tensor_copy(y[:, GROUPS[i][0]:GROUPS[i][1]], sums[i][:])
+
+        term = keep.tile([P, T], F32, name="first", tag="window10")
         middle = keep.tile([P, T], F32, name="middle", tag="window11")
         total = keep.tile([P, T], F32, name="total", tag="window12")
 
         def fetch(r, a, b):
             return y[:].indirect(lists[r][:, a // LIST:b // LIST])
-
-        runs = [(a, b) for a, b in zip(TOKEN_CUTS[:-1], TOKEN_CUTS[1:])]
-        own, shared = runs[0], runs[1:]
 
         def scalar_fetch(tile, r, run):
             a, b = run
@@ -347,19 +366,18 @@ def tile_moe_pre_lin_none_kernel(tc, xT, w, gate, offs, pos1, pos2, pos3, out):
             nc.vector.tensor_tensor(total[:, a:b], total[:, a:b], middle[:, a:b], ADD)
             store(run)
 
-        scalar_fetch(first, 0, shared[0])
-        scalar_fetch(first, 0, shared[1])
-        scalar_fetch(middle, 1, shared[0])
-        scalar_fetch(first, 0, shared[2])
-        scalar_fetch(middle, 1, shared[1])
-        scalar_fetch(middle, 1, shared[2])
-        nc.vector.tensor_copy(first[:, own[0]:own[1]], fetch(0, own[0], own[1]))
-        gather_add(middle, 1, first, own)
-        gather_add(total, 2, first, shared[0])
-        gather_add(total, 2, middle, own)
-        store(own)
-        gather_add(total, 2, first, shared[1])
-        finish(shared[0])
-        gather_add(total, 2, first, shared[2])
-        finish(shared[1])
-        finish(shared[2])
+        alone, *shared = list(zip(TOKEN_CUTS[:-1], TOKEN_CUTS[1:]))
+        scalar_fetch(term, 0, shared[0])
+        for run, following in zip(shared, shared[1:] + [None]):
+            if following is not None:
+                scalar_fetch(term, 0, following)
+            scalar_fetch(middle, 1, run)
+        nc.vector.tensor_copy(term[:, alone[0]:alone[1]], fetch(0, alone[0], alone[1]))
+        gather_add(middle, 1, term, alone)
+        gather_add(total, 2, term, shared[0])
+        gather_add(total, 2, middle, alone)
+        store(alone)
+        for run, following in zip(shared, shared[1:] + [None]):
+            if following is not None:
+                gather_add(total, 2, term, following)
+            finish(run)

@@ -20,50 +20,43 @@ P = 128
 PACK = 4
 K_PASS = P * PACK
 PASSES = K // K_PASS
-LAST = PASSES - 1
 LIST = 16
-WORD = 4
-BLOCK = PACK * N
-HALF = C // 2
-BANK = 512
-RUN = 4
 
 FLOPS = 2 * K * S * N
 BYTES = 4 * (K * T + E * K * N + S + N * T) + 2 * (S + 3 * T)
 
-PIECE = 256
-KEPT = 384
-HEAD = PIECE + KEPT + PIECE
-OWN = 4 * PIECE
-WIDE = 1024
-FIRST = S - HEAD - WIDE
-PIECES = [(0, 0), (0, PIECE + KEPT), (1, 2 * PIECE), (1, 3 * PIECE), (1, 0), (1, PIECE), (LAST, 0)]
-TAPER = [(S - BANK - C - HALF, BANK), (S - C - HALF, C), (S - HALF, HALF)]
-UNITS = [(0, HEAD, FIRST), (0, HEAD + FIRST, WIDE), (1, OWN, WIDE), (1, OWN + WIDE, WIDE), (LAST, PIECE, WIDE)]
-UNITS = UNITS + [(LAST, PIECE + WIDE, TAPER[0][0] - PIECE - WIDE)]
-STEPS = len(UNITS)
-BATCHES = [6, 5, 5, 5, 5, 4, 5, 1]
-EARLY = 2
+FIRST = 1152
 SPARE = 8
+RUN = 4
+BANK = 512
+HALF = C // 2
+WIDE = 1024
+PIECE = 256
+BATCHES = [6, 5, 5, 5, 5, 4, 5, 1]
+HEAD_BATCH = BATCHES[0]
+HEAD_BLOCKS = 2
+BLOCK = PACK * N
 RING = 3
-PLACES = [0, PACK * FIRST * WORD, PACK * (FIRST + WIDE) * WORD]
-
+PLACES = [0, PACK * FIRST * 4, PACK * (FIRST + WIDE) * 4]
+BANK_COUNT = 8
 GATE_BANKS = 2
-SUM_BANKS = 6
+OWN_SLOTS = 1024
 GROUPS = [(a, a + BANK) for a in range(0, S - BANK, BANK)] + [(S - BANK, S - C), (S - C, S - HALF), (S - HALF, S)]
-REUSED = {1: 6, 2: 7}
+REUSED = {6: 1, 7: 2}
+UNITS = [(0, 896, FIRST), (0, 2048, WIDE), (1, 1024, WIDE), (1, 2048, WIDE), (2, 256, WIDE), (2, 1280, 896)]
+TAPER = [(2176, 512), (2688, 256), (2944, 128)]
 BY_VECTOR = (4, 6)
+PIECES = [(0, 0), (0, 640), (1, 512), (1, 768), (1, 0), (1, 256), (2, 0)]
+KEPT = 384
 TOKEN_CUTS = [0, 192, 608, 896, T]
-
-assert sum(BATCHES) == E * PASSES
 
 
 def tile_moe_pre_lin_none_kernel(tc, xT, w, gate, offs, pos1, pos2, pos3, out):
     nc = tc.nc
     with ExitStack() as ctx:
         keep = ctx.enter_context(tc.tile_pool(name="keep", bufs=1))
-        unit_pool = ctx.enter_context(tc.tile_pool(name="picked", bufs=1))
-        piece_pool = ctx.enter_context(tc.tile_pool(name="own", bufs=1))
+        picked_pool = ctx.enter_context(tc.tile_pool(name="picked", bufs=1))
+        own_pool = ctx.enter_context(tc.tile_pool(name="own", bufs=1))
         psum = ctx.enter_context(tc.psum_pool(name="psum", bufs=1))
         gate_psum = ctx.enter_context(tc.psum_pool(name="gate_psum", bufs=GATE_BANKS))
 
@@ -71,34 +64,33 @@ def tile_moe_pre_lin_none_kernel(tc, xT, w, gate, offs, pos1, pos2, pos3, out):
         nc.sync.dma_start(offsets[:], offs)
         identity = keep.tile([P, P], F32, name="identity")
         make_identity(nc, identity[:])
-        cold = keep.tile([P, SPARE], F32, name="cold")
+        cold = keep.tile([P, 8], F32, name="cold")
         nc.vector.memset(cold[:], 0.0)
-        warm = keep.tile([P, SPARE], F32, name="warm")
+        warm = keep.tile([P, 8], F32, name="warm")
         nc.scalar.activation(warm[:], cold[:], COPY)
 
         w_blocks = w.rearrange("e (g p j) n -> p (e g) (j n)", p=P, j=PACK)
-        sums = {i: psum.tile([P, b - a], F32, name=f"acc{i}") for i, (a, b) in enumerate(GROUPS[:SUM_BANKS])}
+        sum_banks = BANK_COUNT - GATE_BANKS
+        accs = {i: psum.tile([P, b - a], F32, name=f"acc{i}") for i, (a, b) in enumerate(GROUPS[:sum_banks])}
         y = keep.tile([P, S], F32, name="y")
         windows = {}
 
         def load_window(g, j):
-            columns = (T if g % 2 else FIRST) + SPARE
-            window = keep.tile([P, columns], F32, name=f"window{g}{j}", tag=f"window{g % 2}{j}")
+            window = keep.tile([P, (T if g % 2 else FIRST) + SPARE], F32, name=f"window{g}{j}", tag=f"window{g % 2}{j}")
             rows = xT[g * K_PASS:(g + 1) * K_PASS, :].rearrange("(p j) t -> p j t", j=PACK)
             nc.sync.dma_start(window[:, 0:T], rows[:, j, :])
             windows[(g, j)] = window
 
-        def load_batches(first, end):
-            b0, b1 = sum(BATCHES[:first]), sum(BATCHES[:end])
-            raw = keep.tile([P, b1 - b0, BLOCK], F32, name=f"raw{b0}", tag=f"raw{first % 2}")
-            nc.sync.dma_start(raw[:], w_blocks[:, b0:b1, :])
+        def load_blocks(b0, blocks, tag):
+            raw = keep.tile([P, blocks, BLOCK], F32, name=f"raw{b0}", tag=tag)
+            nc.sync.dma_start(raw[:], w_blocks[:, b0:b0 + blocks, :])
             return raw
 
         def tokens(g, j, s0, n):
             return windows[(g, j)][:].indirect(offsets[:, s0 // LIST:(s0 + n) // LIST])
 
-        def staging(k, columns):
-            return keep.tile([P, columns], BF16, name="staging", tag=f"staging{k % 2}", align_bytes=64)
+        def staging(which, columns):
+            return keep.tile([P, columns], BF16, name="staging", tag=f"staging{which % 2}", align_bytes=64)
 
         def new_codes(name, words):
             codes = keep.tile([P, words], U32, name=f"codes_{name}", align_bytes=64)
@@ -120,125 +112,117 @@ def tile_moe_pre_lin_none_kernel(tc, xT, w, gate, offs, pos1, pos2, pos3, out):
             s1 = s0 + HALF
             if s0 % C or not ready(g, s1) or (passes_done(s0) == 0) != (passes_done(s1) == 0):
                 return False
-            (tiles0, at0), (tiles1, at1) = x_at[(g, s0)], x_at[(g, s1)]
-            return tiles0[2] == tiles1[2] and at0 + HALF == at1
+            return x_at[(g, s0)][3] == x_at[(g, s1)][3] and x_at[(g, s0)][2] + HALF == x_at[(g, s1)][2]
 
         def multiply():
             for g in range(PASSES):
                 for i, (a, b) in enumerate(GROUPS):
                     for s0 in range(a, b, HALF):
-                        if i in sums and ready(g, s0):
-                            one_pass(i, g, s0, C if s0 + C <= b and joined(g, s0) else HALF)
+                        if i in accs and ready(g, s0):
+                            one_pass(i, a, b, g, s0, C if s0 + C <= b and joined(g, s0) else HALF)
 
-        def one_pass(i, g, s0, n):
-            a, b = GROUPS[i]
+        def one_pass(i, a, b, g, s0, n):
             before = sum([passes_done(s) for s in range(a, b, HALF)])
             closes = before + n // HALF == PASSES * (b - a) // HALF
             for s in range(s0, s0 + n, HALF):
                 issued.add((g, s))
-            w_tiles, w_first = w_at[s0 // C * PASSES + g]
-            x_tiles, x_first = x_at[(g, s0)]
+            w_codes, w_scales, wc = w_at[s0 // C * PASSES + g]
+            x_codes, x_scales, xc, x_name = x_at[(g, s0)]
             nc.tensor.matmul_mx(
-                out=sums[i][:, s0 - a:s0 - a + n],
-                lhsT=w_tiles[0][:, w_first:w_first + N].bitcast(FP8X4),
-                lhsT_scale=w_tiles[1][:, w_first:w_first + N],
-                rhs=x_tiles[0][:, x_first:x_first + n].bitcast(FP8X4),
-                rhs_scale=x_tiles[1][:, x_first:x_first + n],
+                out=accs[i][:, s0 - a:s0 - a + n],
+                lhsT=w_codes[:, wc:wc + N].bitcast(FP8X4),
+                lhsT_scale=w_scales[:, wc:wc + N],
+                rhs=x_codes[:, xc:xc + n].bitcast(FP8X4),
+                rhs_scale=x_scales[:, xc:xc + n],
                 start=(before == 0),
                 stop=closes,
             )
-            if closes and i in BY_VECTOR:
-                closed.append(i)
-            elif closes:
-                nc.scalar.copy(y[:, a:b], sums[i][:])
-                if i in REUSED:
-                    c, d = GROUPS[REUSED[i]]
-                    sums[REUSED[i]] = psum.tile([P, d - c], F32, name=f"late{REUSED[i]}", tag=f"acc{i}")
+            if closes:
+                if i in BY_VECTOR:
+                    closed.append(i)
+                else:
+                    nc.scalar.copy(y[:, a:b], accs[i][:])
+                for late, bank in REUSED.items():
+                    if bank == i:
+                        c, d = GROUPS[late]
+                        accs[late] = psum.tile([P, d - c], F32, name=f"late{late}", tag=f"acc{i}")
 
-        def quantize(tiles, first, source, slots, blocks):
-            codes, scales, name = tiles
+        def quantize(pair, first, source, slots, blocks):
+            codes, scales, name = pair
             words = sum([n for g, s0, n in slots]) + len(blocks) * N
             nc.vector.quantize_mx(
                 out=codes[:, first:first + words].bitcast(FP8X4), scales=scales[:, first:first + words], in_=source
             )
             at = first
             for b in blocks:
-                w_at[b] = (tiles, at)
+                w_at[b] = (codes, scales, at)
                 at = at + N
             for g, s0, n in slots:
                 for s in range(0, n, HALF):
-                    x_at[(g, s0 + s)] = (tiles, at + s)
+                    x_at[(g, s0 + s)] = (codes, scales, at + s, name)
                 at = at + n
             multiply()
 
         def vector_gather(planes, g, j, s0, n):
             nc.vector.tensor_copy(planes[:, j, :], tokens(g, j, s0, n))
 
-        def scalar_gather(planes, g, j, s0, n):
-            nc.scalar.activation(planes[:, j, :], tokens(g, j, s0, n), COPY)
-
-        def scalar_unit(planes, g, s0, n):
+        def scalar_unit(picked, g, s0, n):
             for j in range(PACK):
-                scalar_gather(planes, g, j, s0, n)
-            return planes
-
-        def side_by_side(grouped):
-            return grouped.rearrange("p (c i j) -> p c j i", i=RUN, j=PACK)
-
-        def in_runs(planes):
-            return planes.rearrange("p j (c i) -> p c j i", i=RUN)
-
-        def for_all_planes(row, n):
-            return row.rearrange("p (c o i) -> p c o i", o=1, i=RUN).broadcast_to([P, n // RUN, PACK, RUN])
+                nc.scalar.activation(picked[:, j, :], tokens(g, j, s0, n), COPY)
+            return picked
 
         def vector_gate(grouped, planes, s0, n):
-            stride = n // 3 if n == FIRST else BANK
-            for first in range(0, n, stride):
-                width = min(stride, n - first)
+            step = n // 3 if n == FIRST else BANK
+            for first in range(0, n, step):
+                width = min(step, n - first)
                 spread = gate_psum.tile([P, width], F32, name="spread")
                 for a in range(0, width, P):
                     c = (s0 + first + a) // P
                     nc.tensor.transpose(spread[:, a:a + P], gate_columns[:, c:c + 1].to_broadcast([P, P]), identity[:])
+                gate_runs = spread[:].rearrange("p (c o i) -> p c o i", o=1, i=RUN)
                 nc.vector.tensor_tensor(
-                    side_by_side(grouped[:, first * PACK:(first + width) * PACK]),
-                    in_runs(planes[:, :, first:first + width]),
-                    for_all_planes(spread[:], width),
+                    grouped[:, first * PACK:(first + width) * PACK].rearrange("p (c i j) -> p c j i", i=RUN, j=PACK),
+                    planes[:, :, first:first + width].rearrange("p j (c i) -> p c j i", i=RUN),
+                    gate_runs.broadcast_to([P, width // RUN, PACK, RUN]),
                     MULT,
                 )
 
-        def gpsimd_gate(grouped, k):
-            s0 = PIECES[k][1]
-            row = first_gates[:, s0:s0 + PIECE] if s0 < PIECE else gates[:, s0 - PIECE:s0]
-            nc.gpsimd.tensor_tensor(side_by_side(grouped), in_runs(pieces[k]), for_all_planes(row, PIECE), MULT)
+        def gate_row(s0, n):
+            return first_gates[:, s0:s0 + n] if s0 < PIECE else gates[:, s0 - PIECE:s0 - PIECE + n]
 
-        def gpsimd_weights(grouped, raw, blocks):
-            nc.gpsimd.tensor_copy(
-                grouped.rearrange("p (b n j) -> p b n j", b=blocks, j=PACK),
-                raw.rearrange("p b (j n) -> p b n j", j=PACK),
+        def pool_gate(grouped, planes, s0, n):
+            nc.gpsimd.tensor_tensor(
+                grouped.rearrange("p (c i j) -> p c j i", i=RUN, j=PACK),
+                planes.rearrange("p j (c i) -> p c j i", i=RUN),
+                gate_row(s0, n).rearrange("p (c o i) -> p c o i", o=1, i=RUN).broadcast_to([P, n // RUN, PACK, RUN]),
+                MULT,
             )
 
-        def new_unit(u, n):
+        def pool_weights(grouped, raw, blocks):
+            nc.gpsimd.tensor_scalar(
+                grouped.rearrange("p (b n j) -> p b n j", b=blocks, j=PACK),
+                raw.rearrange("p b (j n) -> p b n j", j=PACK),
+                1.0, 0.0, MULT, ADD,
+            )
+
+        def new_picked(u, n):
             place = u % RING
-            return unit_pool.tile([P, PACK, n], F32, name="picked", tag=f"picked{place}", offset=PLACES[place])
+            return picked_pool.tile([P, PACK, n], F32, name="picked", tag=f"picked{place}", offset=PLACES[place])
 
         def new_piece(k):
-            offset = 0 if k % 2 else PACK * (KEPT + PIECE) * WORD
-            return piece_pool.tile([P, PACK, PIECE], F32, name=f"piece{k}", tag=f"piece{k % 2}", offset=offset)
+            offset = 0 if k % 2 else PACK * (KEPT + PIECE) * 4
+            return own_pool.tile([P, PACK, PIECE], F32, name=f"piece{k}", tag=f"piece{k % 2}", offset=offset)
 
-        def gather_piece(k, planes):
-            for j in planes:
-                vector_gather(pieces[k], PIECES[k][0], j, PIECES[k][1], PIECE)
-
-        opening = unit_pool.tile([P, PACK, PIECE], F32, name="opening", offset=PLACES[2])
-        kept = piece_pool.tile([P, PACK, KEPT + PIECE], F32, name="kept", offset=0)
+        opening = picked_pool.tile([P, PACK, PIECE], F32, name="opening", offset=PLACES[2])
+        kept = own_pool.tile([P, PACK, KEPT + PIECE], F32, name="kept", offset=0)
         pieces = {0: opening[:], 1: kept[:, :, KEPT:]}
-        handed = staging(1, (BATCHES[0] * N + PIECE) * PACK)
-        picked = new_unit(0, FIRST)
+        handed = staging(1, (HEAD_BATCH * N + PIECE) * PACK)
+        picked = new_picked(0, FIRST)
         for j in range(PACK):
             load_window(0, j)
-            gather_piece(0, [j])
+            vector_gather(opening, 0, j, 0, PIECE)
             vector_gather(kept, 0, j, PIECE, KEPT + PIECE)
-            scalar_gather(picked, 0, j, HEAD, FIRST)
+            nc.scalar.activation(picked[:, j, :], tokens(0, j, UNITS[0][1], FIRST), COPY)
             if j == 1:
                 gate_rows = keep.tile([P, P], F32, name="gate_rows")
                 nc.sync.dma_start(gate_rows[:], gate.rearrange("k (c p) -> (k c) p", p=P)[0:P, :])
@@ -246,108 +230,117 @@ def tile_moe_pre_lin_none_kernel(tc, xT, w, gate, offs, pos1, pos2, pos3, out):
                 nc.tensor.transpose(turned[:], gate_rows[:], identity[:])
                 gate_columns = keep.tile([P, S // P], F32, name="gate_columns")
                 nc.vector.tensor_copy(gate_columns[:], turned[:, 0:S // P])
-            if j * EARLY < BATCHES[0]:
-                b0 = j * EARLY
-                raw = unit_pool.tile([P, EARLY, BLOCK], F32, name=f"early{j}", offset=PLACES[1] + b0 * BLOCK * WORD)
-                nc.sync.dma_start(raw[:], w_blocks[:, b0:b0 + EARLY, :])
-                gpsimd_weights(handed[:, b0 * BLOCK:(b0 + EARLY) * BLOCK], raw[:], EARLY)
+            if j * HEAD_BLOCKS < HEAD_BATCH:
+                b0 = j * HEAD_BLOCKS
+                raw = picked_pool.tile([P, HEAD_BLOCKS, BLOCK], F32, name=f"early{j}", offset=PLACES[1] + b0 * BLOCK * 4)
+                nc.sync.dma_start(raw[:], w_blocks[:, b0:b0 + HEAD_BLOCKS, :])
+                pool_weights(handed[:, b0 * BLOCK:(b0 + HEAD_BLOCKS) * BLOCK], raw[:], HEAD_BLOCKS)
         first_gates = keep.tile([P, PIECE], F32, name="first_gates")
         nc.sync.dma_start(first_gates[:], gate[0:P, 0:PIECE])
         load_window(1, 0)
-        raws = {1: load_batches(1, 2)}
+        raws = {1: load_blocks(HEAD_BATCH, BATCHES[1], "raw1")}
         load_window(1, 1)
-        gates = keep.tile([P, OWN - PIECE], F32, name="gates")
-        nc.sync.dma_start(gates[:], gate[0:P, PIECE:OWN])
+        gates = keep.tile([P, OWN_SLOTS - PIECE], F32, name="gates")
+        nc.sync.dma_start(gates[:], gate[0:P, PIECE:OWN_SLOTS])
         for j in range(2, PACK):
             load_window(1, j)
-        raws[2] = load_batches(2, 3)
+        raws[2] = load_blocks(sum(BATCHES[:2]), BATCHES[2], "raw0")
         lists = []
         for r, pos in enumerate((pos1, pos2, pos3)):
             tile = keep.tile([P, T // LIST], U16, name=f"pos{r}")
             nc.sync.dma_start(tile[:], pos)
             lists.append(tile)
 
-        gpsimd_gate(handed[:, BATCHES[0] * BLOCK:], 0)
+        def gather_piece(k, planes):
+            for j in planes:
+                vector_gather(pieces[k], PIECES[k][0], j, PIECES[k][1], PIECE)
+
+        pool_gate(handed[:, HEAD_BATCH * BLOCK:], pieces[0], 0, PIECE)
         grouped = staging(0, KEPT * PACK)
         vector_gate(grouped, kept[:, :, 0:KEPT], PIECE, KEPT)
         pieces[2] = new_piece(2)[:]
         gather_piece(2, [0])
         quantize(new_codes("kept", KEPT), 0, grouped[:], [(0, PIECE, KEPT)], [])
-        quantize(new_codes("batch0", BATCHES[0] * N + PIECE), 0, handed[:], [(0, 0, PIECE)], list(range(BATCHES[0])))
+        quantize(new_codes("batch0", HEAD_BATCH * N + PIECE), 0, handed[:], [(0, 0, PIECE)], list(range(HEAD_BATCH)))
 
-        def gpsimd_batch(k):
+        def pool_batch(k):
             blocks = BATCHES[k]
-            filled = staging(k + 1, (blocks * N + PIECE) * PACK)
-            gpsimd_weights(filled[:, 0:blocks * BLOCK], raws[k][:, 0:blocks, :], blocks)
-            if k + 2 <= STEPS:
-                raws[k + 2] = load_batches(k + 2, k + 3 if k + 2 < STEPS else len(BATCHES))
-            gpsimd_gate(filled[:, blocks * BLOCK:], k)
-            tiles = new_codes(f"batch{k}", blocks * N + PIECE)
+            handed = staging(k + 1, (blocks * N + PIECE) * PACK)
+            pool_weights(handed[:, 0:blocks * BLOCK], raws[k][:, 0:blocks, :], blocks)
+            if k + 2 <= len(UNITS):
+                first = sum(BATCHES[:k + 2])
+                count = BATCHES[k + 2] if k + 2 < len(UNITS) else sum(BATCHES[k + 2:])
+                raws[k + 2] = load_blocks(first, count, f"raw{k % 2}")
+            pool_gate(handed[:, blocks * BLOCK:], pieces[k], PIECES[k][1], PIECE)
+            codes = new_codes(f"batch{k}", blocks * N + PIECE)
             b0 = sum(BATCHES[:k])
             cut = blocks - 1
-            return (
-                lambda: quantize(tiles, 0, filled[:, 0:cut * BLOCK], [], list(range(b0, b0 + cut))),
-                lambda: quantize(tiles, cut * N, filled[:, cut * BLOCK:], [PIECES[k] + (PIECE,)], [b0 + cut]),
-            )
+            front = lambda: quantize(codes, 0, handed[:, 0:cut * BLOCK], [], list(range(b0, b0 + cut)))
+            back = lambda: quantize(codes, cut * N, handed[:, cut * BLOCK:], [PIECES[k] + (PIECE,)], [b0 + cut])
+            return front, back
 
-        for k in range(1, STEPS):
+        def quantize_unit(u, grouped):
+            g, s0, n = UNITS[u]
+            codes = new_codes(f"unit{u}", n)
+            quantize(codes, 0, grouped[:, 0:WIDE * PACK], [(g, s0, WIDE)], [])
+            if n > WIDE:
+                quantize(codes, WIDE, grouped[:, WIDE * PACK:n * PACK], [(g, s0 + WIDE, n - WIDE)], [])
+
+        for k in range(1, len(UNITS)):
             if k == 2:
                 for j in range(PACK):
-                    load_window(LAST, j)
-            ahead = scalar_unit(new_unit(k, UNITS[k][2]), *UNITS[k])
-            quantize_front, quantize_back = gpsimd_batch(k)
+                    load_window(2, j)
+            ahead = scalar_unit(new_picked(k, UNITS[k][2]), *UNITS[k])
+            front, back = pool_batch(k)
             if k > 1:
                 pieces[k + 1] = new_piece(k + 1)[:]
             gather_piece(k + 1, [1] if k == 1 else [0, 1])
             g, s0, n = UNITS[k - 1]
             grouped = staging(k, n * PACK)
             vector_gate(grouped, picked, s0, n)
-            gather_piece(k + 1, [2] if k == STEPS - 1 else [2, 3])
-            quantize_front()
-            tiles = new_codes(f"unit{k - 1}", n)
-            quantize(tiles, 0, grouped[:, 0:WIDE * PACK], [(g, s0, WIDE)], [])
-            if n > WIDE:
-                quantize(tiles, WIDE, grouped[:, WIDE * PACK:n * PACK], [(g, s0 + WIDE, n - WIDE)], [])
-            quantize_back()
+            gather_piece(k + 1, [2] if k == len(UNITS) - 1 else [2, 3])
+            front()
+            quantize_unit(k - 1, grouped)
+            back()
             picked = ahead
 
+        last = PASSES - 1
+        k = len(UNITS)
         (s_a, n_a), (s_b, n_b), (s_c, n_c) = TAPER
-        taper_a = scalar_unit(new_unit(STEPS, n_a), LAST, s_a, n_a)
-        taper_b = scalar_unit(keep.tile([P, PACK, n_b], F32, name="taper_b", tag="window13"), LAST, s_b, n_b)
-        taper_c = keep.tile([P, PACK, n_c], F32, name="taper_c", tag="raw1")
-        for j in range(PACK - 1):
-            scalar_gather(taper_c, LAST, j, s_c, n_c)
-        gather_piece(STEPS, [PACK - 1])
-        quantize_front, quantize_back = gpsimd_batch(STEPS)
-        g, s0, n = UNITS[-1]
-        grouped = staging(STEPS, (n + n_a) * PACK)
+        taper_a = scalar_unit(new_picked(k, n_a), last, s_a, n_a)
+        taper_b = scalar_unit(keep.tile([P, PACK, n_b], F32, name="taper_b", tag="window13"), last, s_b, n_b)
+        taper_c = scalar_unit(keep.tile([P, PACK, n_c], F32, name="taper_c", tag="raw1"), last, s_c, n_c)
+        gather_piece(k, [3])
+        front, back = pool_batch(k)
+        g, s0, n = UNITS[k - 1]
+        grouped = staging(k, (n + n_a) * PACK)
         vector_gate(grouped[:, 0:n * PACK], picked, s0, n)
         vector_gate(grouped[:, n * PACK:], taper_a, s_a, n_a)
-        tiles = new_codes("taper", S - s0)
-        quantize_front()
-        quantize(tiles, 0, grouped[:, 0:WIDE * PACK], [(g, s0, WIDE)], [])
-        quantize_back()
-        quantize(tiles, WIDE, grouped[:, WIDE * PACK:], [(g, s0 + WIDE, n + n_a - WIDE)], [])
-
-        handed = staging(STEPS, BATCHES[-1] * BLOCK)
-        gpsimd_weights(handed[:], raws[STEPS][:, BATCHES[STEPS]:, :], BATCHES[-1])
-        grouped = staging(STEPS + 1, (n_b + n_c) * PACK)
-        last_blocks = list(range(sum(BATCHES[:-1]), sum(BATCHES)))
-        vector_gather(taper_c, LAST, PACK - 1, s_c, n_c)
+        codes = new_codes("taper", S - s0)
+        front()
+        quantize(codes, 0, grouped[:, 0:WIDE * PACK], [(last, s0, WIDE)], [])
+        back()
+        quantize(codes, WIDE, grouped[:, WIDE * PACK:], [(last, s0 + WIDE, n + n_a - WIDE)], [])
+        handed = staging(k, BATCHES[-1] * BLOCK)
+        pool_weights(handed[:], raws[k][:, BATCHES[k]:, :], BATCHES[-1])
+        grouped = staging(k + 1, (n_b + n_c) * PACK)
         vector_gate(grouped[:, 0:n_b * PACK], taper_b, s_b, n_b)
-        quantize(new_codes("last_blocks", BATCHES[-1] * N), 0, handed[:], [], last_blocks)
         vector_gate(grouped[:, n_b * PACK:], taper_c, s_c, n_c)
-        quantize(tiles, s_b - s0, grouped[:, 0:n_b * PACK], [(g, s_b, n_b)], [])
-        quantize(tiles, s_c - s0, grouped[:, n_b * PACK:], [(g, s_c, n_c)], [])
+        quantize(new_codes("last_blocks", BATCHES[-1] * N), 0, handed[:], [], list(range(sum(BATCHES[:-1]), sum(BATCHES))))
+        quantize(codes, s_b - s0, grouped[:, 0:n_b * PACK], [(last, s_b, n_b)], [])
+        quantize(codes, s_c - s0, grouped[:, n_b * PACK:], [(last, s_c, n_c)], [])
         for i in closed:
-            nc.vector.tensor_copy(y[:, GROUPS[i][0]:GROUPS[i][1]], sums[i][:])
+            nc.vector.tensor_copy(y[:, GROUPS[i][0]:GROUPS[i][1]], accs[i][:])
 
-        term = keep.tile([P, T], F32, name="first", tag="window10")
+        first = keep.tile([P, T], F32, name="first", tag="window10")
         middle = keep.tile([P, T], F32, name="middle", tag="window11")
         total = keep.tile([P, T], F32, name="total", tag="window12")
 
         def fetch(r, a, b):
             return y[:].indirect(lists[r][:, a // LIST:b // LIST])
+
+        runs = [(a, b) for a, b in zip(TOKEN_CUTS[:-1], TOKEN_CUTS[1:])]
+        own, shared = runs[0], runs[1:]
 
         def scalar_fetch(tile, r, run):
             a, b = run
@@ -366,18 +359,19 @@ def tile_moe_pre_lin_none_kernel(tc, xT, w, gate, offs, pos1, pos2, pos3, out):
             nc.vector.tensor_tensor(total[:, a:b], total[:, a:b], middle[:, a:b], ADD)
             store(run)
 
-        alone, *shared = list(zip(TOKEN_CUTS[:-1], TOKEN_CUTS[1:]))
-        scalar_fetch(term, 0, shared[0])
-        for run, following in zip(shared, shared[1:] + [None]):
-            if following is not None:
-                scalar_fetch(term, 0, following)
-            scalar_fetch(middle, 1, run)
-        nc.vector.tensor_copy(term[:, alone[0]:alone[1]], fetch(0, alone[0], alone[1]))
-        gather_add(middle, 1, term, alone)
-        gather_add(total, 2, term, shared[0])
-        gather_add(total, 2, middle, alone)
-        store(alone)
-        for run, following in zip(shared, shared[1:] + [None]):
-            if following is not None:
-                gather_add(total, 2, term, following)
-            finish(run)
+        scalar_fetch(first, 0, shared[0])
+        scalar_fetch(first, 0, shared[1])
+        scalar_fetch(middle, 1, shared[0])
+        scalar_fetch(first, 0, shared[2])
+        scalar_fetch(middle, 1, shared[1])
+        scalar_fetch(middle, 1, shared[2])
+        nc.vector.tensor_copy(first[:, own[0]:own[1]], fetch(0, own[0], own[1]))
+        gather_add(middle, 1, first, own)
+        gather_add(total, 2, first, shared[0])
+        gather_add(total, 2, middle, own)
+        store(own)
+        gather_add(total, 2, first, shared[1])
+        finish(shared[0])
+        gather_add(total, 2, first, shared[2])
+        finish(shared[1])
+        finish(shared[2])

from contextlib import ExitStack

import concourse.mybir as mybir
from concourse.masks import make_identity

K, T, E, C, N = 1536, 1024, 12, 256, 128
S = E * C

F32 = mybir.dt.float32
BF16 = mybir.dt.bfloat16
U32 = mybir.dt.uint32
U16 = mybir.dt.uint16
U8 = mybir.dt.uint8
FP8X4 = mybir.dt.float8_e4m3fn_x4
MULT = mybir.AluOpType.mult
ADD = mybir.AluOpType.add
COPY = mybir.ActivationFunctionType.Copy

P = 128
PACK = 4
K_PASS = P * PACK
PASSES = K // K_PASS
LIST = 16

FLOPS = 2 * K * S * N
BYTES = 4 * (K * T + E * K * N + S + N * T) + 2 * (S + 3 * T)

FIRST = 1152
SPARE = 8
RUN = 4
BANK = 512
HALF = C // 2
WIDE = 1024
PIECE = 256
BATCHES = [6, 5, 5, 5, 5, 4, 5, 1]
HEAD_BATCH = BATCHES[0]
HEAD_BLOCKS = 2
BLOCK = PACK * N
RING = 3
PLACES = [0, PACK * FIRST * 4, PACK * (FIRST + WIDE) * 4]
BANK_COUNT = 8
GATE_BANKS = 2
OWN_SLOTS = 1024
GROUPS = [(a, a + BANK) for a in range(0, S - BANK, BANK)] + [(S - BANK, S - C), (S - C, S - HALF), (S - HALF, S)]
REUSED = {6: 1, 7: 2}
UNITS = [(0, 896, FIRST), (0, 2048, WIDE), (1, 1024, WIDE), (1, 2048, WIDE), (2, 256, WIDE), (2, 1280, 896)]
TAPER = [(2176, 512), (2688, 256), (2944, 128)]
BY_VECTOR = (4, 6)
PIECES = [(0, 0), (0, 640), (1, 512), (1, 768), (1, 0), (1, 256), (2, 0)]
KEPT = 384
TOKEN_CUTS = [0, 192, 608, 896, T]


def tile_moe_pre_lin_none_kernel(tc, xT, w, gate, offs, pos1, pos2, pos3, out):
    nc = tc.nc
    with ExitStack() as ctx:
        keep = ctx.enter_context(tc.tile_pool(name="keep", bufs=1))
        picked_pool = ctx.enter_context(tc.tile_pool(name="picked", bufs=1))
        own_pool = ctx.enter_context(tc.tile_pool(name="own", bufs=1))
        psum = ctx.enter_context(tc.psum_pool(name="psum", bufs=1))
        gate_psum = ctx.enter_context(tc.psum_pool(name="gate_psum", bufs=GATE_BANKS))

        offsets = keep.tile([P, S // LIST], U16, name="offsets")
        nc.sync.dma_start(offsets[:], offs)
        identity = keep.tile([P, P], F32, name="identity")
        make_identity(nc, identity[:])
        cold = keep.tile([P, 8], F32, name="cold")
        nc.vector.memset(cold[:], 0.0)
        warm = keep.tile([P, 8], F32, name="warm")
        nc.scalar.activation(warm[:], cold[:], COPY)

        w_blocks = w.rearrange("e (g p j) n -> p (e g) (j n)", p=P, j=PACK)
        sum_banks = BANK_COUNT - GATE_BANKS
        accs = {i: psum.tile([P, b - a], F32, name=f"acc{i}") for i, (a, b) in enumerate(GROUPS[:sum_banks])}
        y = keep.tile([P, S], F32, name="y")
        windows = {}

        def load_window(g, j):
            window = keep.tile([P, (T if g % 2 else FIRST) + SPARE], F32, name=f"window{g}{j}", tag=f"window{g % 2}{j}")
            rows = xT[g * K_PASS:(g + 1) * K_PASS, :].rearrange("(p j) t -> p j t", j=PACK)
            nc.sync.dma_start(window[:, 0:T], rows[:, j, :])
            windows[(g, j)] = window

        def load_blocks(b0, blocks, tag):
            raw = keep.tile([P, blocks, BLOCK], F32, name=f"raw{b0}", tag=tag)
            nc.sync.dma_start(raw[:], w_blocks[:, b0:b0 + blocks, :])
            return raw

        def tokens(g, j, s0, n):
            return windows[(g, j)][:].indirect(offsets[:, s0 // LIST:(s0 + n) // LIST])

        def staging(which, columns):
            return keep.tile([P, columns], BF16, name="staging", tag=f"staging{which % 2}", align_bytes=64)

        def new_codes(name, words):
            codes = keep.tile([P, words], U32, name=f"codes_{name}", align_bytes=64)
            scales = keep.tile([P, words], U8, name=f"scales_{name}", align_bytes=64)
            return codes, scales, name

        x_at = {}
        w_at = {}
        issued = set()
        closed = []

        def passes_done(s0):
            return len([1 for g in range(PASSES) if (g, s0) in issued])

        def ready(g, s0):
            return (g, s0) in x_at and (g, s0) not in issued and s0 // C * PASSES + g in w_at

        def joined(g, s0):
            s1 = s0 + HALF
            if s0 % C or not ready(g, s1) or (passes_done(s0) == 0) != (passes_done(s1) == 0):
                return False
            return x_at[(g, s0)][3] == x_at[(g, s1)][3] and x_at[(g, s0)][2] + HALF == x_at[(g, s1)][2]

        def multiply():
            for g in range(PASSES):
                for i, (a, b) in enumerate(GROUPS):
                    for s0 in range(a, b, HALF):
                        if i in accs and ready(g, s0):
                            one_pass(i, a, b, g, s0, C if s0 + C <= b and joined(g, s0) else HALF)

        def one_pass(i, a, b, g, s0, n):
            before = sum([passes_done(s) for s in range(a, b, HALF)])
            closes = before + n // HALF == PASSES * (b - a) // HALF
            for s in range(s0, s0 + n, HALF):
                issued.add((g, s))
            w_codes, w_scales, wc = w_at[s0 // C * PASSES + g]
            x_codes, x_scales, xc, x_name = x_at[(g, s0)]
            nc.tensor.matmul_mx(
                out=accs[i][:, s0 - a:s0 - a + n],
                lhsT=w_codes[:, wc:wc + N].bitcast(FP8X4),
                lhsT_scale=w_scales[:, wc:wc + N],
                rhs=x_codes[:, xc:xc + n].bitcast(FP8X4),
                rhs_scale=x_scales[:, xc:xc + n],
                start=(before == 0),
                stop=closes,
            )
            if closes:
                if i in BY_VECTOR:
                    closed.append(i)
                else:
                    nc.scalar.copy(y[:, a:b], accs[i][:])
                for late, bank in REUSED.items():
                    if bank == i:
                        c, d = GROUPS[late]
                        accs[late] = psum.tile([P, d - c], F32, name=f"late{late}", tag=f"acc{i}")

        def quantize(pair, first, source, slots, blocks):
            codes, scales, name = pair
            words = sum([n for g, s0, n in slots]) + len(blocks) * N
            nc.vector.quantize_mx(
                out=codes[:, first:first + words].bitcast(FP8X4), scales=scales[:, first:first + words], in_=source
            )
            at = first
            for b in blocks:
                w_at[b] = (codes, scales, at)
                at = at + N
            for g, s0, n in slots:
                for s in range(0, n, HALF):
                    x_at[(g, s0 + s)] = (codes, scales, at + s, name)
                at = at + n
            multiply()

        def vector_gather(planes, g, j, s0, n):
            nc.vector.tensor_copy(planes[:, j, :], tokens(g, j, s0, n))

        def scalar_unit(picked, g, s0, n):
            for j in range(PACK):
                nc.scalar.activation(picked[:, j, :], tokens(g, j, s0, n), COPY)
            return picked

        def vector_gate(grouped, planes, s0, n):
            step = n // 3 if n == FIRST else BANK
            for first in range(0, n, step):
                width = min(step, n - first)
                spread = gate_psum.tile([P, width], F32, name="spread")
                for a in range(0, width, P):
                    c = (s0 + first + a) // P
                    nc.tensor.transpose(spread[:, a:a + P], gate_columns[:, c:c + 1].to_broadcast([P, P]), identity[:])
                gate_runs = spread[:].rearrange("p (c o i) -> p c o i", o=1, i=RUN)
                nc.vector.tensor_tensor(
                    grouped[:, first * PACK:(first + width) * PACK].rearrange("p (c i j) -> p c j i", i=RUN, j=PACK),
                    planes[:, :, first:first + width].rearrange("p j (c i) -> p c j i", i=RUN),
                    gate_runs.broadcast_to([P, width // RUN, PACK, RUN]),
                    MULT,
                )

        def gate_row(s0, n):
            return first_gates[:, s0:s0 + n] if s0 < PIECE else gates[:, s0 - PIECE:s0 - PIECE + n]

        def pool_gate(grouped, planes, s0, n):
            nc.gpsimd.tensor_tensor(
                grouped.rearrange("p (c i j) -> p c j i", i=RUN, j=PACK),
                planes.rearrange("p j (c i) -> p c j i", i=RUN),
                gate_row(s0, n).rearrange("p (c o i) -> p c o i", o=1, i=RUN).broadcast_to([P, n // RUN, PACK, RUN]),
                MULT,
            )

        def pool_weights(grouped, raw, blocks):
            nc.gpsimd.tensor_scalar(
                grouped.rearrange("p (b n j) -> p b n j", b=blocks, j=PACK),
                raw.rearrange("p b (j n) -> p b n j", j=PACK),
                1.0, 0.0, MULT, ADD,
            )

        def new_picked(u, n):
            place = u % RING
            return picked_pool.tile([P, PACK, n], F32, name="picked", tag=f"picked{place}", offset=PLACES[place])

        def new_piece(k):
            offset = 0 if k % 2 else PACK * (KEPT + PIECE) * 4
            return own_pool.tile([P, PACK, PIECE], F32, name=f"piece{k}", tag=f"piece{k % 2}", offset=offset)

        opening = picked_pool.tile([P, PACK, PIECE], F32, name="opening", offset=PLACES[2])
        kept = own_pool.tile([P, PACK, KEPT + PIECE], F32, name="kept", offset=0)
        pieces = {0: opening[:], 1: kept[:, :, KEPT:]}
        handed = staging(1, (HEAD_BATCH * N + PIECE) * PACK)
        picked = new_picked(0, FIRST)
        for j in range(PACK):
            load_window(0, j)
            vector_gather(opening, 0, j, 0, PIECE)
            vector_gather(kept, 0, j, PIECE, KEPT + PIECE)
            nc.scalar.activation(picked[:, j, :], tokens(0, j, UNITS[0][1], FIRST), COPY)
            if j == 1:
                gate_rows = keep.tile([P, P], F32, name="gate_rows")
                nc.sync.dma_start(gate_rows[:], gate.rearrange("k (c p) -> (k c) p", p=P)[0:P, :])
                turned = gate_psum.tile([P, P], F32, name="spread")
                nc.tensor.transpose(turned[:], gate_rows[:], identity[:])
                gate_columns = keep.tile([P, S // P], F32, name="gate_columns")
                nc.vector.tensor_copy(gate_columns[:], turned[:, 0:S // P])
            if j * HEAD_BLOCKS < HEAD_BATCH:
                b0 = j * HEAD_BLOCKS
                raw = picked_pool.tile([P, HEAD_BLOCKS, BLOCK], F32, name=f"early{j}", offset=PLACES[1] + b0 * BLOCK * 4)
                nc.sync.dma_start(raw[:], w_blocks[:, b0:b0 + HEAD_BLOCKS, :])
                pool_weights(handed[:, b0 * BLOCK:(b0 + HEAD_BLOCKS) * BLOCK], raw[:], HEAD_BLOCKS)
        first_gates = keep.tile([P, PIECE], F32, name="first_gates")
        nc.sync.dma_start(first_gates[:], gate[0:P, 0:PIECE])
        load_window(1, 0)
        raws = {1: load_blocks(HEAD_BATCH, BATCHES[1], "raw1")}
        load_window(1, 1)
        gates = keep.tile([P, OWN_SLOTS - PIECE], F32, name="gates")
        nc.sync.dma_start(gates[:], gate[0:P, PIECE:OWN_SLOTS])
        for j in range(2, PACK):
            load_window(1, j)
        raws[2] = load_blocks(sum(BATCHES[:2]), BATCHES[2], "raw0")
        lists = []
        for r, pos in enumerate((pos1, pos2, pos3)):
            tile = keep.tile([P, T // LIST], U16, name=f"pos{r}")
            nc.sync.dma_start(tile[:], pos)
            lists.append(tile)

        def gather_piece(k, planes):
            for j in planes:
                vector_gather(pieces[k], PIECES[k][0], j, PIECES[k][1], PIECE)

        pool_gate(handed[:, HEAD_BATCH * BLOCK:], pieces[0], 0, PIECE)
        grouped = staging(0, KEPT * PACK)
        vector_gate(grouped, kept[:, :, 0:KEPT], PIECE, KEPT)
        pieces[2] = new_piece(2)[:]
        gather_piece(2, [0])
        quantize(new_codes("kept", KEPT), 0, grouped[:], [(0, PIECE, KEPT)], [])
        quantize(new_codes("batch0", HEAD_BATCH * N + PIECE), 0, handed[:], [(0, 0, PIECE)], list(range(HEAD_BATCH)))

        def pool_batch(k):
            blocks = BATCHES[k]
            handed = staging(k + 1, (blocks * N + PIECE) * PACK)
            pool_weights(handed[:, 0:blocks * BLOCK], raws[k][:, 0:blocks, :], blocks)
            if k + 2 <= len(UNITS):
                first = sum(BATCHES[:k + 2])
                count = BATCHES[k + 2] if k + 2 < len(UNITS) else sum(BATCHES[k + 2:])
                raws[k + 2] = load_blocks(first, count, f"raw{k % 2}")
            pool_gate(handed[:, blocks * BLOCK:], pieces[k], PIECES[k][1], PIECE)
            codes = new_codes(f"batch{k}", blocks * N + PIECE)
            b0 = sum(BATCHES[:k])
            cut = blocks - 1
            front = lambda: quantize(codes, 0, handed[:, 0:cut * BLOCK], [], list(range(b0, b0 + cut)))
            back = lambda: quantize(codes, cut * N, handed[:, cut * BLOCK:], [PIECES[k] + (PIECE,)], [b0 + cut])
            return front, back

        def quantize_unit(u, grouped):
            g, s0, n = UNITS[u]
            codes = new_codes(f"unit{u}", n)
            quantize(codes, 0, grouped[:, 0:WIDE * PACK], [(g, s0, WIDE)], [])
            if n > WIDE:
                quantize(codes, WIDE, grouped[:, WIDE * PACK:n * PACK], [(g, s0 + WIDE, n - WIDE)], [])

        for k in range(1, len(UNITS)):
            if k == 2:
                for j in range(PACK):
                    load_window(2, j)
            ahead = scalar_unit(new_picked(k, UNITS[k][2]), *UNITS[k])
            front, back = pool_batch(k)
            if k > 1:
                pieces[k + 1] = new_piece(k + 1)[:]
            gather_piece(k + 1, [1] if k == 1 else [0, 1])
            g, s0, n = UNITS[k - 1]
            grouped = staging(k, n * PACK)
            vector_gate(grouped, picked, s0, n)
            gather_piece(k + 1, [2] if k == len(UNITS) - 1 else [2, 3])
            front()
            quantize_unit(k - 1, grouped)
            back()
            picked = ahead

        last = PASSES - 1
        k = len(UNITS)
        (s_a, n_a), (s_b, n_b), (s_c, n_c) = TAPER
        taper_a = scalar_unit(new_picked(k, n_a), last, s_a, n_a)
        taper_b = scalar_unit(keep.tile([P, PACK, n_b], F32, name="taper_b", tag="window13"), last, s_b, n_b)
        taper_c = scalar_unit(keep.tile([P, PACK, n_c], F32, name="taper_c", tag="raw1"), last, s_c, n_c)
        gather_piece(k, [3])
        front, back = pool_batch(k)
        g, s0, n = UNITS[k - 1]
        grouped = staging(k, (n + n_a) * PACK)
        vector_gate(grouped[:, 0:n * PACK], picked, s0, n)
        vector_gate(grouped[:, n * PACK:], taper_a, s_a, n_a)
        codes = new_codes("taper", S - s0)
        front()
        quantize(codes, 0, grouped[:, 0:WIDE * PACK], [(last, s0, WIDE)], [])
        back()
        quantize(codes, WIDE, grouped[:, WIDE * PACK:], [(last, s0 + WIDE, n + n_a - WIDE)], [])
        handed = staging(k, BATCHES[-1] * BLOCK)
        pool_weights(handed[:], raws[k][:, BATCHES[k]:, :], BATCHES[-1])
        grouped = staging(k + 1, (n_b + n_c) * PACK)
        vector_gate(grouped[:, 0:n_b * PACK], taper_b, s_b, n_b)
        vector_gate(grouped[:, n_b * PACK:], taper_c, s_c, n_c)
        quantize(new_codes("last_blocks", BATCHES[-1] * N), 0, handed[:], [], list(range(sum(BATCHES[:-1]), sum(BATCHES))))
        quantize(codes, s_b - s0, grouped[:, 0:n_b * PACK], [(last, s_b, n_b)], [])
        quantize(codes, s_c - s0, grouped[:, n_b * PACK:], [(last, s_c, n_c)], [])
        for i in closed:
            nc.vector.tensor_copy(y[:, GROUPS[i][0]:GROUPS[i][1]], accs[i][:])

        first = keep.tile([P, T], F32, name="first", tag="window10")
        middle = keep.tile([P, T], F32, name="middle", tag="window11")
        total = keep.tile([P, T], F32, name="total", tag="window12")

        def fetch(r, a, b):
            return y[:].indirect(lists[r][:, a // LIST:b // LIST])

        runs = [(a, b) for a, b in zip(TOKEN_CUTS[:-1], TOKEN_CUTS[1:])]
        own, shared = runs[0], runs[1:]

        def scalar_fetch(tile, r, run):
            a, b = run
            nc.scalar.activation(tile[:, a:b], fetch(r, a, b), COPY)

        def gather_add(tile, r, other, run):
            a, b = run
            nc.vector.tensor_tensor(tile[:, a:b], fetch(r, a, b), other[:, a:b], ADD)

        def store(run):
            a, b = run
            nc.sync.dma_start(out[:, a:b], total[:, a:b])

        def finish(run):
            a, b = run
            nc.vector.tensor_tensor(total[:, a:b], total[:, a:b], middle[:, a:b], ADD)
            store(run)

        scalar_fetch(first, 0, shared[0])
        scalar_fetch(first, 0, shared[1])
        scalar_fetch(middle, 1, shared[0])
        scalar_fetch(first, 0, shared[2])
        scalar_fetch(middle, 1, shared[1])
        scalar_fetch(middle, 1, shared[2])
        nc.vector.tensor_copy(first[:, own[0]:own[1]], fetch(0, own[0], own[1]))
        gather_add(middle, 1, first, own)
        gather_add(total, 2, first, shared[0])
        gather_add(total, 2, middle, own)
        store(own)
        gather_add(total, 2, first, shared[1])
        finish(shared[0])
        gather_add(total, 2, first, shared[2])
        finish(shared[1])
        finish(shared[2])
